import numpy as np
import ml_dtypes


def mxq(x, axis, fmt="e4m3"):
    dtype, down = {"e4m3": (ml_dtypes.float8_e4m3fn, 7), "e5m2": (ml_dtypes.float8_e5m2, 14)}[fmt]
    v = np.moveaxis(np.asarray(x, np.float32).astype(ml_dtypes.bfloat16).astype(np.float64), axis, -1)
    blocks = v.reshape(v.shape[:-1] + (-1, 32))
    amax = np.abs(blocks).max(-1, keepdims=True)
    byte = np.maximum(np.where(amax > 0, np.frexp(amax)[1] - 1 + 127, 0) - down, 1)
    scale = np.exp2(byte - 127.0)
    codes = (blocks / scale).astype(np.float32).astype(dtype).astype(np.float64)
    return np.moveaxis((codes * scale).reshape(v.shape), -1, axis)


WIDE = False


def mx_kscale(k):
    if not WIDE:
        return np.ones(k)
    levels = np.array([10, -10, 5, -5, 0])
    if k % 512:
        return np.exp2(np.random.permutation(np.resize(levels, k // 32))).repeat(32)
    a = np.empty((k // 512, 16))
    for p in range(k // 512):
        a[p, :8] = np.random.permutation(np.resize(levels, 8))
        for g in range(8):
            far = levels[np.abs(levels - a[p, g]) >= 10]
            a[p, g + 8] = far[np.random.randint(len(far))]
    return np.exp2(a.ravel()).repeat(32)


def f64(x):
    return np.asarray(x).astype(np.float64)


def striped(idx):
    return np.tile(idx.reshape(-1, 16).T, (8, 1)).astype(np.uint16)


def unstriped(offs):
    return offs[:16].T.reshape(-1).astype(np.int64)


E2M1 = np.array([0.0, 0.5, 1.0, 1.5, 2.0, 3.0, 4.0, 6.0, -0.0, -0.5, -1.0, -1.5, -2.0, -3.0, -4.0, -6.0])


def pack_weight(w, fmt):
    k, n = w.shape
    w = f64(np.asarray(w, np.float32).astype(ml_dtypes.bfloat16)).reshape(k // 32, 32, n)
    amax = np.abs(w).max(1)
    if fmt == "e4m3":
        byte = np.frexp(amax)[1] - 1 + 127 - 7
    else:
        mant, ex = np.frexp(amax / 6.0)
        byte = np.where(mant > 0.5, ex, ex - 1) + 127
    byte = np.clip(np.where(amax > 0, byte, 1), 1, 254)
    scaled = (w * np.exp2(127.0 - byte)[:, None, :]).reshape(k, n).astype(np.float32)
    by_word = np.ascontiguousarray(scaled.reshape(k // 512, 128, 4, n).transpose(0, 1, 3, 2))
    if fmt == "e4m3":
        words = by_word.astype(ml_dtypes.float8_e4m3fn).view(np.uint8)
    else:
        c = by_word.astype(ml_dtypes.float4_e2m1fn).view(np.uint8) & 0xF
        words = (c[..., 0::2] | (c[..., 1::2] << 4)).reshape(k // 512, 128, 2 * n)
    return np.ascontiguousarray(words), np.ascontiguousarray(byte.astype(np.uint8).reshape(k // 512, 16, n))


def unpack_weight(words, scales, fmt):
    g, _, n = scales.shape
    words = np.ascontiguousarray(words).reshape(g, 128, n, -1)
    if fmt == "e4m3":
        vals = words.view(ml_dtypes.float8_e4m3fn).astype(np.float64)
    else:
        nib = np.empty((g, 128, n, 4), np.uint8)
        nib[..., 0::2] = words & 0xF
        nib[..., 1::2] = words >> 4
        vals = E2M1[nib]
    vals = vals * np.repeat(np.exp2(scales.astype(np.float64) - 127.0), 8, axis=1)[..., None]
    return vals.transpose(0, 1, 3, 2).reshape(g * 512, n)


def d_relu2(v):
    return 2.0 * np.maximum(v, 0.0)


K, T, E, C, H, N = 512, 640, 5, 256, 512, 512


def by_expert(wq, xq):
    return np.concatenate([wq[e].T @ xq[:, e * C:(e + 1) * C] for e in range(E)], axis=1)


def setup_inputs():
    n = np.random.standard_normal
    v = mx_kscale(N)
    u = mx_kscale(H)
    first = np.random.permutation(np.repeat(np.arange(E), T // E))
    second = (first + 1 + np.random.permutation(np.repeat(np.arange(E - 1), -(-T // (E - 1)))[:T])) % E
    while np.bincount(second, minlength=E).max() != T // E:
        load = np.bincount(second, minlength=E); hi, lo = int(load.argmax()), int(load.argmin())
        t = np.flatnonzero((second == hi) & (first != lo))[0]; second[t] = lo
    slot_token = np.empty(E * C, np.int64); pos = np.empty((2, T), np.int64); fill = np.zeros(E, np.int64)
    place = np.stack([np.random.permutation(C) for _ in range(E)])
    for r, deal in enumerate((first, second)):
        for t in np.random.permutation(T):
            e = deal[t]; j = e * C + place[e, fill[e]]; fill[e] += 1; slot_token[j] = t; pos[r, t] = j
    g = np.random.uniform(0.2, 0.8, T)
    w_slot = np.empty(E * C); w_slot[pos[0]] = g; w_slot[pos[1]] = 1.0 - g
    dy = pack_weight(n((N, T)) * v[:, None], "e4m3")
    wt = pack_weight(n((N, K)) / np.sqrt(N) / v[:, None], "e2m1")
    wbt = [pack_weight(m, "e4m3") for m in n((E, N, H)) / np.sqrt(N) / v[None, :, None] * u]
    wat = [pack_weight(m, "e4m3") for m in n((E, H, K)) / np.sqrt(H) / u[None, :, None]]
    return {
        "dy_words": dy[0],
        "dy_scales": dy[1],
        "wt_words": wt[0],
        "wt_scales": wt[1],
        "wbt_words": np.stack([m[0] for m in wbt]),
        "wbt_scales": np.stack([m[1] for m in wbt]),
        "wat_words": np.stack([m[0] for m in wat]),
        "wat_scales": np.stack([m[1] for m in wat]),
        "a": (n((H, E * C))).astype(np.float32),
        "gate": (np.tile(w_slot, (128, 1))).astype(np.float32),
        "offs": striped(slot_token),
        "pos1": striped(pos[0]),
        "pos2": striped(pos[1]),
    }


def reference(dy_words, dy_scales, wt_words, wt_scales, wbt_words, wbt_scales, wat_words, wat_scales, a, gate, offs, pos1, pos2):
    wt = unpack_weight(wt_words, wt_scales, "e2m1")
    wbt = np.stack([unpack_weight(wbt_words[e], wbt_scales[e], "e4m3") for e in range(E)])
    wat = np.stack([unpack_weight(wat_words[e], wat_scales[e], "e4m3") for e in range(E)])
    idx = unstriped(offs)
    dy = unpack_weight(dy_words, dy_scales, "e4m3")
    base = wt.T @ dy
    dh = f64(gate[:1]) * by_expert(wbt, dy[:, idx]) * d_relu2(f64(a))
    dx = by_expert(wat, mxq(dh, 0, "e4m3"))
    c = dx[:, unstriped(pos1)] + dx[:, unstriped(pos2)]
    return base + c

@@ -1,0 +1,228 @@
+from contextlib import ExitStack
+
+import concourse.mybir as mybir
+from concourse.masks import make_identity
+
+K, T, E, C, H, N = 512, 640, 5, 256, 512, 512
+S = E * C
+P = 128
+FLOPS = 2 * K * N * T + 2 * S * N * H + 2 * S * H * K
+
+F32 = mybir.dt.float32
+BF16 = mybir.dt.bfloat16
+I32 = mybir.dt.int32
+U32 = mybir.dt.uint32
+U16 = mybir.dt.uint16
+U8 = mybir.dt.uint8
+FP8X4 = mybir.dt.float8_e4m3fn_x4
+FP4X4 = mybir.dt.float4_e2m1fn_x4
+COPY = mybir.ActivationFunctionType.Copy
+ALU = mybir.AluOpType
+
+
+def tile_moe_adb_relu2_kernel(
+    tc, dy_words, dy_scales, wt_words, wt_scales, wbt_words, wbt_scales, wat_words, wat_scales, a, gate, offs, pos1, pos2, out
+):
+    nc = tc.nc
+    with ExitStack() as ctx:
+        keep = ctx.enter_context(tc.tile_pool(name="keep", bufs=1))
+        ring = ctx.enter_context(tc.tile_pool(name="ring", bufs=4))
+        psum = ctx.enter_context(tc.psum_pool(name="psum", bufs=1))
+
+        offs_sb = keep.tile([P, S // 16], U16)
+        pos1_sb = keep.tile([P, T // 16], U16)
+        pos2_sb = keep.tile([P, T // 16], U16)
+        dyw = keep.tile([P, T], I32, align_bytes=64)
+        dys = keep.tile([P, T], U8, align_bytes=64)
+        wtw = keep.tile([P, 2 * K], U8, align_bytes=64)
+        wts = keep.tile([P, K], U8, align_bytes=64)
+        wbw = keep.tile([P, E, H], I32, align_bytes=64)
+        wbs = keep.tile([P, E, H], U8, align_bytes=64)
+        waw0 = keep.tile([P, E, P], I32, align_bytes=64)
+        waw1 = keep.tile([P, E, K - P], I32, align_bytes=64)
+        was = keep.tile([P, E, K], U8, align_bytes=64)
+        gate_rows = keep.tile([P, P], F32)
+        gate2 = keep.tile([P, S // P], F32)
+        ident = keep.tile([P, P], F32)
+        xw = keep.tile([P, S], U32, align_bytes=64)
+        xs = keep.tile([P, S], U8, align_bytes=64)
+        sg = keep.tile([P, S // P, 4, P], F32)
+        dh = keep.tile([P, S, 4], BF16, align_bytes=64)
+        dhw = keep.tile([P, S], U32, align_bytes=64)
+        dhs = keep.tile([P, S], U8, align_bytes=64)
+        base_t = keep.tile([P, T // P, K - P], F32)
+        base_last = keep.tile([P, T], F32)
+        a_cuts = [(0, 1), (1, 3), (3, 5)]
+        a_sb = [keep.tile([P, 4, (hi - lo) * C], F32, name="a%d" % lo) for lo, hi in a_cuts]
+        dx = [keep.tile([P, S], F32, name="dx%d" % c) for c in range(4)]
+
+        nc.vector.memset(dys[:].bitcast(I32), 0)
+        nc.vector.memset(wbs[:].rearrange("p e n -> p (e n)").bitcast(I32), 0)
+        nc.vector.memset(was[:].rearrange("p e n -> p (e n)").bitcast(I32), 0)
+        nc.vector.memset(wts[:].bitcast(I32), 0)
+        make_identity(nc, ident[:])
+
+        wb_src = wbt_words.rearrange("e o p n d -> p (e o) (n d)").bitcast(I32)
+        wa_src = wat_words.rearrange("e o p n d -> p (e o) (n d)").bitcast(I32)
+        a_src = a.rearrange("(p t) s -> p t s", t=4)
+
+        def load_scales(engine, plane, rows):
+            rest = (slice(None),) * (len(rows.shape) - 1)
+            for q in range(4):
+                engine.dma_start(
+                    out=plane[(slice(32 * q, 32 * q + 4),) + rest].bitcast(I32),
+                    in_=rows[(slice(4 * q, 4 * q + 4),) + rest].bitcast(I32),
+                )
+
+        def load_a(n):
+            lo, hi = a_cuts[n]
+            nc.sync.dma_start(out=a_sb[n][:], in_=a_src[:, :, lo * C : hi * C])
+
+        nc.sync.dma_start(offs_sb[:], offs)
+        nc.sync.dma_start(out=dyw[:], in_=dy_words[0].rearrange("p t d -> p (t d)").bitcast(I32))
+        load_scales(nc.sync, dys, dy_scales[0])
+        nc.sync.dma_start(out=wbw[:], in_=wb_src)
+        nc.sync.dma_start(out=gate_rows[:], in_=gate.rearrange("r (c s) -> (r c) s", s=P)[0:P, :])
+        load_scales(nc.sync, wbs, wbt_scales.rearrange("e o r n -> r (e o) n"))
+        load_a(0)
+        load_a(1)
+        nc.sync.dma_start(out=waw0[:], in_=wa_src[:, :, 0:P])
+        load_scales(nc.sync, was, wat_scales.rearrange("e o r n -> r (e o) n"))
+        load_a(2)
+        load_scales(nc.sync, wts, wt_scales[0])
+        nc.sync.dma_start(out=wtw[:].bitcast(I32), in_=wt_words[0].bitcast(I32))
+        nc.sync.dma_start(out=waw1[:], in_=wa_src[:, :, P:K])
+        nc.sync.dma_start(pos1_sb[:], pos1)
+        nc.sync.dma_start(pos2_sb[:], pos2)
+
+        def bank(tag, bufs):
+            return psum.tile([P, 512], F32, name=tag, tag=tag, bufs=bufs)
+
+        def mm_bank():
+            return bank("mm", 2)
+
+        def tr_bank():
+            return bank("tr", 3)
+
+        def dx_bank():
+            return bank("dxb", 3)
+
+        gb = tr_bank()
+        nc.tensor.transpose(gb[:, 0:P], gate_rows[:], ident[:])
+        nc.scalar.activation(gate2[:], gb[:, 0 : S // P], COPY, scale=2.0)
+
+        for e in range(E):
+            cols = slice(e * C, (e + 1) * C)
+            lst = offs_sb[:, e * C // 16 : (e + 1) * C // 16]
+            nc.vector.tensor_copy(xw[:, cols], dyw[:].bitcast(U32).indirect(lst))
+            nc.vector.tensor_copy(xs[:, cols], dys[:].indirect(lst))
+
+        for b in range(S // P):
+            e = b * P // C
+            cols = slice(b * P, (b + 1) * P)
+            acc = mm_bank()
+            nc.tensor.matmul_mx(
+                out=acc[:], lhsT=xw[:, cols].bitcast(FP8X4), lhsT_scale=xs[:, cols],
+                rhs=wbw[:, e, :].bitcast(FP8X4), rhs_scale=wbs[:, e, :], start=True, stop=True,
+            )
+            nc.scalar.activation(sg[:, b, :, :], acc[:].rearrange("p (m t) -> p t m", t=4), COPY, scale=gate2[:, b : b + 1])
+
+        def quantize(lo, hi):
+            nc.vector.quantize_mx(
+                out=dhw[:, lo:hi].bitcast(FP8X4), scales=dhs[:, lo:hi], in_=dh[:, lo:hi, :].rearrange("p s t -> p (s t)")
+            )
+
+        def second(c, lo, hi):
+            acc = dx_bank()
+            for s0 in range(lo, hi, C):
+                s1 = min(s0 + C, hi)
+                e = s0 // C
+                w = waw0[:, e, :] if c == 0 else waw1[:, e, (c - 1) * P : c * P]
+                nc.tensor.matmul_mx(
+                    out=acc[:, s0 - lo : s1 - lo], lhsT=w.bitcast(FP8X4), lhsT_scale=was[:, e, c * P : (c + 1) * P],
+                    rhs=dhw[:, s0:s1].bitcast(FP8X4), rhs_scale=dhs[:, s0:s1], start=True, stop=True,
+                )
+            nc.scalar.copy(dx[c][:, lo:hi], acc[:, 0 : hi - lo])
+
+        def make_dh(b):
+            turned = tr_bank()
+            for t in range(4):
+                nc.tensor.transpose(turned[:, t * P : (t + 1) * P], sg[:, b, t, :], ident[:])
+            e = b * P // C
+            n = [i for i, (lo, hi) in enumerate(a_cuts) if lo <= e < hi][0]
+            s0 = b * P - a_cuts[n][0] * C
+            nc.vector.scalar_tensor_tensor(
+                out=dh[:, b * P : (b + 1) * P, :],
+                in0=a_sb[n][:, :, s0 : s0 + P].rearrange("p t s -> p s t"),
+                scalar=0.0,
+                in1=turned[:].rearrange("p (t s) -> p s t", t=4),
+                op0=ALU.max,
+                op1=ALU.mult,
+            )
+
+        for e in range(E):
+            make_dh(2 * e)
+            if e > 0:
+                quantize((e - 1) * C, e * C)
+                second(0, (e - 1) * C, e * C)
+            make_dh(2 * e + 1)
+        for lo in (S - C, S - P):
+            quantize(lo, lo + P)
+            second(0, lo, lo + P)
+
+        for b in range(T // P):
+            cols = slice(b * P, (b + 1) * P)
+            acc = mm_bank()
+            for k0, k1 in ((0, 256), (256, 384)):
+                nc.tensor.matmul_mx(
+                    out=acc[:, k0:k1], lhsT=dyw[:, cols].bitcast(FP8X4), lhsT_scale=dys[:, cols],
+                    rhs=wtw[:, 2 * k0 : 2 * k1].bitcast(FP4X4), rhs_scale=wts[:, k0:k1], start=True, stop=True,
+                )
+            nc.scalar.copy(base_t[:, b, :], acc[:, 0 : K - P])
+        for t0, t1 in ((0, 512), (512, T)):
+            acc = mm_bank()
+            nc.tensor.matmul_mx(
+                out=acc[:, 0 : t1 - t0], lhsT=wtw[:, 2 * (K - P) : 2 * K].bitcast(FP4X4), lhsT_scale=wts[:, K - P : K],
+                rhs=dyw[:, t0:t1].bitcast(FP8X4), rhs_scale=dys[:, t0:t1], start=True, stop=True,
+            )
+            nc.scalar.copy(base_last[:, t0:t1], acc[:, 0 : t1 - t0])
+
+        def add_turned(dst, first, other):
+            nc.tensor.matmul(dst, lhsT=first, rhs=ident[:], start=True, stop=False, is_transpose=True)
+            nc.tensor.matmul(dst, lhsT=other, rhs=ident[:], start=False, stop=True, is_transpose=True)
+
+        for c in range(1, 4):
+            for lo, hi in ((0, 512), (512, 1024), (1024, S)):
+                second(c, lo, hi)
+        halves = ((0, 3), (3, 5))
+        for c in range(4):
+            g1 = ring.tile([P, T], F32)
+            g2 = ring.tile([P, T], F32)
+            res = ring.tile([P, T], F32)
+            rows = slice(c * P, (c + 1) * P)
+            nc.vector.tensor_copy(g1[:], dx[c][:].indirect(pos1_sb[:]))
+            if c < 3:
+                nc.vector.tensor_copy(g2[:], dx[c][:].indirect(pos2_sb[:]))
+                sum_t = ring.tile([P, T], F32)
+                for b0, b1 in halves:
+                    acc = mm_bank()
+                    for b in range(b0, b1):
+                        cols = slice(b * P, (b + 1) * P)
+                        add_turned(acc[:, (b - b0) * P : (b - b0 + 1) * P], g1[:, cols], g2[:, cols])
+                    nc.scalar.copy(sum_t[:, b0 * P : b1 * P], acc[:, 0 : (b1 - b0) * P])
+                for b0, b1 in halves:
+                    acc = tr_bank()
+                    for b in range(b0, b1):
+                        add_turned(acc[:, (b - b0) * P : (b - b0 + 1) * P], sum_t[:, b * P : (b + 1) * P], base_t[:, b, rows])
+                    nc.scalar.copy(res[:, b0 * P : b1 * P], acc[:, 0 : (b1 - b0) * P])
+                nc.sync.dma_start(out=out[rows, :], in_=res[:])
+            else:
+                part = keep.tile([P, T], F32)
+                half = T // 2
+                nc.vector.tensor_copy(g2[:, 0:half], dx[c][:].indirect(pos2_sb[:, 0 : half // 16]))
+                nc.vector.tensor_tensor(part[:], g1[:], base_last[:], ALU.add)
+                nc.vector.tensor_tensor(res[:, 0:half], part[:, 0:half], g2[:, 0:half], ALU.add)
+                nc.sync.dma_start(out=out[rows, 0:half], in_=res[:, 0:half])
+                nc.vector.tensor_copy(g2[:, half:T], dx[c][:].indirect(pos2_sb[:, half // 16 : T // 16]))
+                nc.vector.tensor_tensor(res[:, half:T], part[:, half:T], g2[:, half:T], ALU.add)
+                nc.sync.dma_start(out=out[rows, half:T], in_=res[:, half:T])

@@ -6,6 +6,7 @@ from concourse.masks import make_identity
 K, T, E, C, H, N = 512, 640, 5, 256, 512, 512
 S = E * C
 P = 128
+WIN = 768
 FLOPS = 2 * K * N * T + 2 * S * N * H + 2 * S * H * K
 
 F32 = mybir.dt.float32
@@ -32,9 +33,8 @@ def tile_moe_adb_relu2_kernel(
         offs_sb = keep.tile([P, S // 16], U16)
         pos1_sb = keep.tile([P, T // 16], U16)
         pos2_sb = keep.tile([P, T // 16], U16)
-        dyw = keep.tile([P, T], I32, align_bytes=64)
-        dys = keep.tile([P, T], U8, align_bytes=64)
-        wtw = keep.tile([P, 2 * K], U8, align_bytes=64)
+        dyw = keep.tile([P, WIN], I32, align_bytes=64)
+        dys = keep.tile([P, WIN], U8, align_bytes=64)
         wts = keep.tile([P, K], U8, align_bytes=64)
         wbw = keep.tile([P, E, H], I32, align_bytes=64)
         wbs = keep.tile([P, E, H], U8, align_bytes=64)
@@ -50,13 +50,12 @@ def tile_moe_adb_relu2_kernel(
         dh = keep.tile([P, S, 4], BF16, align_bytes=64)
         dhw = keep.tile([P, S], U32, align_bytes=64)
         dhs = keep.tile([P, S], U8, align_bytes=64)
-        base_t = keep.tile([P, T // P, K - P], F32)
-        base_last = keep.tile([P, T], F32)
         a_cuts = [(0, 1), (1, 3), (3, 5)]
-        a_sb = [keep.tile([P, 4, (hi - lo) * C], F32, name="a%d" % lo) for lo, hi in a_cuts]
+        a_sb = [keep.tile([P, 4, (hi - lo) * C], F32, name="a%d" % lo, tag="a%d" % lo, align_bytes=64) for lo, hi in a_cuts]
         dx = [keep.tile([P, S], F32, name="dx%d" % c) for c in range(4)]
 
         nc.vector.memset(dys[:].bitcast(I32), 0)
+        nc.vector.memset(dyw[:, T:WIN], 0)
         nc.vector.memset(wbs[:].rearrange("p e n -> p (e n)").bitcast(I32), 0)
         nc.vector.memset(was[:].rearrange("p e n -> p (e n)").bitcast(I32), 0)
         nc.vector.memset(wts[:].bitcast(I32), 0)
@@ -78,22 +77,22 @@ def tile_moe_adb_relu2_kernel(
             lo, hi = a_cuts[n]
             nc.sync.dma_start(out=a_sb[n][:], in_=a_src[:, :, lo * C : hi * C])
 
+        nc.sync.dma_start(out=dyw[:, 0:T], in_=dy_words[0].rearrange("p t d -> p (t d)").bitcast(I32))
         nc.sync.dma_start(offs_sb[:], offs)
-        nc.sync.dma_start(out=dyw[:], in_=dy_words[0].rearrange("p t d -> p (t d)").bitcast(I32))
-        load_scales(nc.sync, dys, dy_scales[0])
-        nc.sync.dma_start(out=wbw[:], in_=wb_src)
+        load_scales(nc.sync, dys[:, 0:T], dy_scales[0])
+        nc.sync.dma_start(out=wbw[:, 0:2, :], in_=wb_src[:, 0:2, :])
         nc.sync.dma_start(out=gate_rows[:], in_=gate.rearrange("r (c s) -> (r c) s", s=P)[0:P, :])
         load_scales(nc.sync, wbs, wbt_scales.rearrange("e o r n -> r (e o) n"))
+        nc.sync.dma_start(out=wbw[:, 2:5, :], in_=wb_src[:, 2:5, :])
         load_a(0)
         load_a(1)
         nc.sync.dma_start(out=waw0[:], in_=wa_src[:, :, 0:P])
-        load_scales(nc.sync, was, wat_scales.rearrange("e o r n -> r (e o) n"))
         load_a(2)
-        load_scales(nc.sync, wts, wt_scales[0])
-        nc.sync.dma_start(out=wtw[:].bitcast(I32), in_=wt_words[0].bitcast(I32))
+        load_scales(nc.sync, was, wat_scales.rearrange("e o r n -> r (e o) n"))
         nc.sync.dma_start(out=waw1[:], in_=wa_src[:, :, P:K])
         nc.sync.dma_start(pos1_sb[:], pos1)
         nc.sync.dma_start(pos2_sb[:], pos2)
+        load_scales(nc.sync, wts, wt_scales[0])
 
         def bank(tag, bufs):
             return psum.tile([P, 512], F32, name=tag, tag=tag, bufs=bufs)
@@ -111,9 +110,9 @@ def tile_moe_adb_relu2_kernel(
         nc.tensor.transpose(gb[:, 0:P], gate_rows[:], ident[:])
         nc.scalar.activation(gate2[:], gb[:, 0 : S // P], COPY, scale=2.0)
 
-        for e in range(E):
-            cols = slice(e * C, (e + 1) * C)
-            lst = offs_sb[:, e * C // 16 : (e + 1) * C // 16]
+        for lo, hi in a_cuts:
+            cols = slice(lo * C, hi * C)
+            lst = offs_sb[:, lo * C // 16 : hi * C // 16]
             nc.vector.tensor_copy(xw[:, cols], dyw[:].bitcast(U32).indirect(lst))
             nc.vector.tensor_copy(xs[:, cols], dys[:].indirect(lst))
 
@@ -170,59 +169,70 @@ def tile_moe_adb_relu2_kernel(
             quantize(lo, lo + P)
             second(0, lo, lo + P)
 
-        for b in range(T // P):
-            cols = slice(b * P, (b + 1) * P)
-            acc = mm_bank()
-            for k0, k1 in ((0, 256), (256, 384)):
-                nc.tensor.matmul_mx(
-                    out=acc[:, k0:k1], lhsT=dyw[:, cols].bitcast(FP8X4), lhsT_scale=dys[:, cols],
-                    rhs=wtw[:, 2 * k0 : 2 * k1].bitcast(FP4X4), rhs_scale=wts[:, k0:k1], start=True, stop=True,
-                )
-            nc.scalar.copy(base_t[:, b, :], acc[:, 0 : K - P])
-        for t0, t1 in ((0, 512), (512, T)):
-            acc = mm_bank()
-            nc.tensor.matmul_mx(
-                out=acc[:, 0 : t1 - t0], lhsT=wtw[:, 2 * (K - P) : 2 * K].bitcast(FP4X4), lhsT_scale=wts[:, K - P : K],
-                rhs=dyw[:, t0:t1].bitcast(FP8X4), rhs_scale=dys[:, t0:t1], start=True, stop=True,
-            )
-            nc.scalar.copy(base_last[:, t0:t1], acc[:, 0 : t1 - t0])
+        wtw = keep.tile([P, 2 * K], U8, tag="a3", align_bytes=64)
+        nc.sync.dma_start(out=wtw[:].bitcast(I32), in_=wt_words[0].bitcast(I32))
 
         def add_turned(dst, first, other):
             nc.tensor.matmul(dst, lhsT=first, rhs=ident[:], start=True, stop=False, is_transpose=True)
             nc.tensor.matmul(dst, lhsT=other, rhs=ident[:], start=False, stop=True, is_transpose=True)
 
-        for c in range(1, 4):
+        def second_all(c):
             for lo, hi in ((0, 512), (512, 1024), (1024, S)):
                 second(c, lo, hi)
+
         halves = ((0, 3), (3, 5))
+        second_all(1)
+        second_all(2)
         for c in range(4):
             g1 = ring.tile([P, T], F32)
             g2 = ring.tile([P, T], F32)
             res = ring.tile([P, T], F32)
             rows = slice(c * P, (c + 1) * P)
+            w_c = wtw[:, 2 * c * P : 2 * (c + 1) * P].bitcast(FP4X4)
             nc.vector.tensor_copy(g1[:], dx[c][:].indirect(pos1_sb[:]))
             if c < 3:
                 nc.vector.tensor_copy(g2[:], dx[c][:].indirect(pos2_sb[:]))
-                sum_t = ring.tile([P, T], F32)
+                base_t = ring.tile([P, T], F32)
                 for b0, b1 in halves:
                     acc = mm_bank()
                     for b in range(b0, b1):
                         cols = slice(b * P, (b + 1) * P)
+                        nc.tensor.matmul_mx(
+                            out=acc[:, (b - b0) * P : (b - b0 + 1) * P], lhsT=dyw[:, cols].bitcast(FP8X4), lhsT_scale=dys[:, cols],
+                            rhs=w_c, rhs_scale=wts[:, rows], start=True, stop=True,
+                        )
+                    nc.scalar.copy(base_t[:, b0 * P : b1 * P], acc[:, 0 : (b1 - b0) * P])
+                sum_t = ring.tile([P, T], F32)
+                for b0, b1 in halves:
+                    acc = dx_bank()
+                    for b in range(b0, b1):
+                        cols = slice(b * P, (b + 1) * P)
                         add_turned(acc[:, (b - b0) * P : (b - b0 + 1) * P], g1[:, cols], g2[:, cols])
                     nc.scalar.copy(sum_t[:, b0 * P : b1 * P], acc[:, 0 : (b1 - b0) * P])
+                if c == 0:
+                    second_all(3)
                 for b0, b1 in halves:
                     acc = tr_bank()
                     for b in range(b0, b1):
-                        add_turned(acc[:, (b - b0) * P : (b - b0 + 1) * P], sum_t[:, b * P : (b + 1) * P], base_t[:, b, rows])
+                        cols = slice(b * P, (b + 1) * P)
+                        add_turned(acc[:, (b - b0) * P : (b - b0 + 1) * P], sum_t[:, cols], base_t[:, cols])
                     nc.scalar.copy(res[:, b0 * P : b1 * P], acc[:, 0 : (b1 - b0) * P])
                 nc.sync.dma_start(out=out[rows, :], in_=res[:])
             else:
                 part = keep.tile([P, T], F32)
-                half = T // 2
-                nc.vector.tensor_copy(g2[:, 0:half], dx[c][:].indirect(pos2_sb[:, 0 : half // 16]))
-                nc.vector.tensor_tensor(part[:], g1[:], base_last[:], ALU.add)
-                nc.vector.tensor_tensor(res[:, 0:half], part[:, 0:half], g2[:, 0:half], ALU.add)
-                nc.sync.dma_start(out=out[rows, 0:half], in_=res[:, 0:half])
-                nc.vector.tensor_copy(g2[:, half:T], dx[c][:].indirect(pos2_sb[:, half // 16 : T // 16]))
-                nc.vector.tensor_tensor(res[:, half:T], part[:, half:T], g2[:, half:T], ALU.add)
-                nc.sync.dma_start(out=out[rows, half:T], in_=res[:, half:T])
+                cut = 384
+                nc.vector.tensor_copy(g2[:, 0:cut], dx[c][:].indirect(pos2_sb[:, 0 : cut // 16]))
+                for t0, t1 in ((0, cut), (cut, T)):
+                    acc = mm_bank()
+                    for u0 in range(t0, t1, 256):
+                        u1 = min(u0 + 256, t1)
+                        nc.tensor.matmul_mx(
+                            out=acc[:, u0 - t0 : u1 - t0], lhsT=w_c, lhsT_scale=wts[:, rows],
+                            rhs=dyw[:, u0:u1].bitcast(FP8X4), rhs_scale=dys[:, u0:u1], start=True, stop=True,
+                        )
+                    nc.vector.tensor_tensor(part[:, t0:t1], g1[:, t0:t1], acc[:, 0 : t1 - t0], ALU.add)
+                nc.vector.tensor_tensor(res[:, 0:cut], part[:, 0:cut], g2[:, 0:cut], ALU.add)
+                nc.sync.dma_start(out=out[rows, 0:cut], in_=res[:, 0:cut])
+                nc.vector.tensor_copy(g2[:, cut:T], dx[c][:].indirect(pos2_sb[:, cut // 16 : T // 16]))
+                nc.vector.tensor_tensor(res[:, cut:T], part[:, cut:T], g2[:, cut:T], ALU.add)
+                nc.sync.dma_start(out=out[rows, cut:T], in_=res[:, cut:T])

@@ -38,8 +38,7 @@ def tile_moe_adb_relu2_kernel(
         wts = keep.tile([P, K], U8, align_bytes=64)
         wbw = keep.tile([P, E, H], I32, align_bytes=64)
         wbs = keep.tile([P, E, H], U8, align_bytes=64)
-        waw0 = keep.tile([P, E, P], I32, align_bytes=64)
-        waw1 = keep.tile([P, E, K - P], I32, align_bytes=64)
+        waw = keep.tile([P, E, K], I32, align_bytes=64)
         was = keep.tile([P, E, K], U8, align_bytes=64)
         gate_rows = keep.tile([P, P], F32)
         gate2 = keep.tile([P, S // P], F32)
@@ -50,8 +49,8 @@ def tile_moe_adb_relu2_kernel(
         dh = keep.tile([P, S, 4], BF16, align_bytes=64)
         dhw = keep.tile([P, S], U32, align_bytes=64)
         dhs = keep.tile([P, S], U8, align_bytes=64)
-        a_cuts = [(0, 1), (1, 3), (3, 5)]
-        a_sb = [keep.tile([P, 4, (hi - lo) * C], F32, name="a%d" % lo, tag="a%d" % lo, align_bytes=64) for lo, hi in a_cuts]
+        a_cuts = [(0, 2), (2, 4), (4, 5)]
+        a_sb = [keep.tile([P, 4, (hi - lo) * C + 9], F32, name="a%d" % lo, tag="a%d" % lo, align_bytes=64) for lo, hi in a_cuts]
         dx = [keep.tile([P, S], F32, name="dx%d" % c) for c in range(4)]
 
         nc.vector.memset(dys[:].bitcast(I32), 0)
@@ -75,10 +74,10 @@ def tile_moe_adb_relu2_kernel(
 
         def load_a(n):
             lo, hi = a_cuts[n]
-            nc.sync.dma_start(out=a_sb[n][:], in_=a_src[:, :, lo * C : hi * C])
+            nc.sync.dma_start(out=a_sb[n][:, :, 0 : (hi - lo) * C], in_=a_src[:, :, lo * C : hi * C])
 
-        nc.sync.dma_start(out=dyw[:, 0:T], in_=dy_words[0].rearrange("p t d -> p (t d)").bitcast(I32))
         nc.sync.dma_start(offs_sb[:], offs)
+        nc.sync.dma_start(out=dyw[:, 0:T], in_=dy_words[0].rearrange("p t d -> p (t d)").bitcast(I32))
         load_scales(nc.sync, dys[:, 0:T], dy_scales[0])
         nc.sync.dma_start(out=wbw[:, 0:2, :], in_=wb_src[:, 0:2, :])
         nc.sync.dma_start(out=gate_rows[:], in_=gate.rearrange("r (c s) -> (r c) s", s=P)[0:P, :])
@@ -86,10 +85,10 @@ def tile_moe_adb_relu2_kernel(
         nc.sync.dma_start(out=wbw[:, 2:5, :], in_=wb_src[:, 2:5, :])
         load_a(0)
         load_a(1)
-        nc.sync.dma_start(out=waw0[:], in_=wa_src[:, :, 0:P])
-        load_a(2)
         load_scales(nc.sync, was, wat_scales.rearrange("e o r n -> r (e o) n"))
-        nc.sync.dma_start(out=waw1[:], in_=wa_src[:, :, P:K])
+        nc.sync.dma_start(out=waw[:, 0:3, :], in_=wa_src[:, 0:3, :])
+        load_a(2)
+        nc.sync.dma_start(out=waw[:, 3:5, :], in_=wa_src[:, 3:5, :])
         nc.sync.dma_start(pos1_sb[:], pos1)
         nc.sync.dma_start(pos2_sb[:], pos2)
         load_scales(nc.sync, wts, wt_scales[0])
@@ -106,11 +105,17 @@ def tile_moe_adb_relu2_kernel(
         def dx_bank():
             return bank("dxb", 3)
 
+        warm = mm_bank()
+        for n in range(3):
+            nc.tensor.matmul_mx(
+                out=warm[:], lhsT=dyw[:, 0:P].bitcast(FP8X4), lhsT_scale=dys[:, 0:P],
+                rhs=dyw[:, 0:512].bitcast(FP8X4), rhs_scale=dys[:, 0:512], start=True, stop=True,
+            )
         gb = tr_bank()
         nc.tensor.transpose(gb[:, 0:P], gate_rows[:], ident[:])
         nc.scalar.activation(gate2[:], gb[:, 0 : S // P], COPY, scale=2.0)
 
-        for lo, hi in a_cuts:
+        for lo, hi in ((0, 1), (1, 3), (3, 5)):
             cols = slice(lo * C, hi * C)
             lst = offs_sb[:, lo * C // 16 : hi * C // 16]
             nc.vector.tensor_copy(xw[:, cols], dyw[:].bitcast(U32).indirect(lst))
@@ -131,17 +136,20 @@ def tile_moe_adb_relu2_kernel(
                 out=dhw[:, lo:hi].bitcast(FP8X4), scales=dhs[:, lo:hi], in_=dh[:, lo:hi, :].rearrange("p s t -> p (s t)")
             )
 
-        def second(c, lo, hi):
-            acc = dx_bank()
+        def second(c, lo, hi, last=False):
+            acc = mm_bank() if last else dx_bank()
             for s0 in range(lo, hi, C):
                 s1 = min(s0 + C, hi)
                 e = s0 // C
-                w = waw0[:, e, :] if c == 0 else waw1[:, e, (c - 1) * P : c * P]
+                w = waw[:, e, c * P : (c + 1) * P]
                 nc.tensor.matmul_mx(
                     out=acc[:, s0 - lo : s1 - lo], lhsT=w.bitcast(FP8X4), lhsT_scale=was[:, e, c * P : (c + 1) * P],
                     rhs=dhw[:, s0:s1].bitcast(FP8X4), rhs_scale=dhs[:, s0:s1], start=True, stop=True,
                 )
-            nc.scalar.copy(dx[c][:, lo:hi], acc[:, 0 : hi - lo])
+            if last:
+                nc.vector.tensor_copy(dx[c][:, lo:hi], acc[:, 0 : hi - lo])
+            else:
+                nc.scalar.copy(dx[c][:, lo:hi], acc[:, 0 : hi - lo])
 
         def make_dh(b):
             turned = tr_bank()
@@ -167,9 +175,9 @@ def tile_moe_adb_relu2_kernel(
             make_dh(2 * e + 1)
         for lo in (S - C, S - P):
             quantize(lo, lo + P)
-            second(0, lo, lo + P)
+            second(0, lo, lo + P, last=(lo == S - P))
 
-        wtw = keep.tile([P, 2 * K], U8, tag="a3", align_bytes=64)
+        wtw = keep.tile([P, 2 * K], U8, tag="a4", align_bytes=64)
         nc.sync.dma_start(out=wtw[:].bitcast(I32), in_=wt_words[0].bitcast(I32))
 
         def add_turned(dst, first, other):

@@ -6,8 +6,20 @@ from concourse.masks import make_identity
 K, T, E, C, H, N = 512, 640, 5, 256, 512, 512
 S = E * C
 P = 128
-WIN = 768
+PACK = 4
+BANK = 512
+PER_COL = 16
+CHUNKS = K // P
+WINDOW = 768
 FLOPS = 2 * K * N * T + 2 * S * N * H + 2 * S * H * K
+
+GATHER_CUTS = ((0, 1), (1, 3), (3, 5))
+A_CUTS = ((0, 1), (1, 3), (3, 4), (4, 5))
+WB_FIRST = 3
+TOKEN_GROUPS = ((0, 3), (3, 5))
+CUT = TOKEN_GROUPS[1][0] * P
+BASE_PASS = 256
+WARM_PASSES = 3
 
 F32 = mybir.dt.float32
 BF16 = mybir.dt.bfloat16
@@ -27,34 +39,36 @@ def tile_moe_adb_relu2_kernel(
     nc = tc.nc
     with ExitStack() as ctx:
         keep = ctx.enter_context(tc.tile_pool(name="keep", bufs=1))
-        ring = ctx.enter_context(tc.tile_pool(name="ring", bufs=4))
+        ring = ctx.enter_context(tc.tile_pool(name="ring", bufs=CHUNKS))
         psum = ctx.enter_context(tc.psum_pool(name="psum", bufs=1))
 
-        offs_sb = keep.tile([P, S // 16], U16)
-        pos1_sb = keep.tile([P, T // 16], U16)
-        pos2_sb = keep.tile([P, T // 16], U16)
-        dyw = keep.tile([P, WIN], I32, align_bytes=64)
-        dys = keep.tile([P, WIN], U8, align_bytes=64)
+        offs_sb = keep.tile([P, S // PER_COL], U16)
+        pos1_sb = keep.tile([P, T // PER_COL], U16)
+        pos2_sb = keep.tile([P, T // PER_COL], U16)
+        dyw = keep.tile([P, WINDOW], I32, align_bytes=64)
+        dys = keep.tile([P, WINDOW], U8, align_bytes=64)
         wts = keep.tile([P, K], U8, align_bytes=64)
         wbw = keep.tile([P, E, H], I32, align_bytes=64)
         wbs = keep.tile([P, E, H], U8, align_bytes=64)
-        waw = keep.tile([P, E, K], I32, align_bytes=64)
+        waw_first = keep.tile([P, E, P], I32, align_bytes=64)
+        waw_rest = keep.tile([P, E, K - P], I32, align_bytes=64)
         was = keep.tile([P, E, K], U8, align_bytes=64)
         gate_rows = keep.tile([P, P], F32)
         gate2 = keep.tile([P, S // P], F32)
         ident = keep.tile([P, P], F32)
         xw = keep.tile([P, S], U32, align_bytes=64)
         xs = keep.tile([P, S], U8, align_bytes=64)
-        sg = keep.tile([P, S // P, 4, P], F32)
-        dh = keep.tile([P, S, 4], BF16, align_bytes=64)
+        gated = keep.tile([P, S // P, PACK, P], F32)
+        dh = keep.tile([P, S, PACK], BF16, align_bytes=64)
         dhw = keep.tile([P, S], U32, align_bytes=64)
         dhs = keep.tile([P, S], U8, align_bytes=64)
-        a_cuts = [(0, 2), (2, 4), (4, 5)]
-        a_sb = [keep.tile([P, 4, (hi - lo) * C + 9], F32, name="a%d" % lo, tag="a%d" % lo, align_bytes=64) for lo, hi in a_cuts]
-        dx = [keep.tile([P, S], F32, name="dx%d" % c) for c in range(4)]
+        a_sb = [
+            keep.tile([P, PACK, (hi - lo) * C], F32, name="a%d" % lo, tag="a%d" % lo, align_bytes=64) for lo, hi in A_CUTS
+        ]
+        dx = [keep.tile([P, S], F32, name="dx%d" % c) for c in range(CHUNKS)]
 
         nc.vector.memset(dys[:].bitcast(I32), 0)
-        nc.vector.memset(dyw[:, T:WIN], 0)
+        nc.vector.memset(dyw[:, T:WINDOW], 0)
         nc.vector.memset(wbs[:].rearrange("p e n -> p (e n)").bitcast(I32), 0)
         nc.vector.memset(was[:].rearrange("p e n -> p (e n)").bitcast(I32), 0)
         nc.vector.memset(wts[:].bitcast(I32), 0)
@@ -62,185 +76,197 @@ def tile_moe_adb_relu2_kernel(
 
         wb_src = wbt_words.rearrange("e o p n d -> p (e o) (n d)").bitcast(I32)
         wa_src = wat_words.rearrange("e o p n d -> p (e o) (n d)").bitcast(I32)
-        a_src = a.rearrange("(p t) s -> p t s", t=4)
+        a_src = a.rearrange("(p t) s -> p t s", t=PACK)
 
-        def load_scales(engine, plane, rows):
+        def load_scales(tile, rows):
             rest = (slice(None),) * (len(rows.shape) - 1)
             for q in range(4):
-                engine.dma_start(
-                    out=plane[(slice(32 * q, 32 * q + 4),) + rest].bitcast(I32),
+                nc.sync.dma_start(
+                    out=tile[(slice(32 * q, 32 * q + 4),) + rest].bitcast(I32),
                     in_=rows[(slice(4 * q, 4 * q + 4),) + rest].bitcast(I32),
                 )
 
         def load_a(n):
-            lo, hi = a_cuts[n]
-            nc.sync.dma_start(out=a_sb[n][:, :, 0 : (hi - lo) * C], in_=a_src[:, :, lo * C : hi * C])
+            lo, hi = A_CUTS[n]
+            nc.sync.dma_start(out=a_sb[n][:], in_=a_src[:, :, lo * C : hi * C])
 
         nc.sync.dma_start(offs_sb[:], offs)
         nc.sync.dma_start(out=dyw[:, 0:T], in_=dy_words[0].rearrange("p t d -> p (t d)").bitcast(I32))
-        load_scales(nc.sync, dys[:, 0:T], dy_scales[0])
-        nc.sync.dma_start(out=wbw[:, 0:2, :], in_=wb_src[:, 0:2, :])
+        load_scales(dys[:, 0:T], dy_scales[0])
+        nc.sync.dma_start(out=wbw[:, 0:WB_FIRST, :], in_=wb_src[:, 0:WB_FIRST, :])
         nc.sync.dma_start(out=gate_rows[:], in_=gate.rearrange("r (c s) -> (r c) s", s=P)[0:P, :])
-        load_scales(nc.sync, wbs, wbt_scales.rearrange("e o r n -> r (e o) n"))
-        nc.sync.dma_start(out=wbw[:, 2:5, :], in_=wb_src[:, 2:5, :])
+        load_scales(wbs, wbt_scales.rearrange("e o r n -> r (e o) n"))
         load_a(0)
+        nc.sync.dma_start(out=wbw[:, WB_FIRST:E, :], in_=wb_src[:, WB_FIRST:E, :])
         load_a(1)
-        load_scales(nc.sync, was, wat_scales.rearrange("e o r n -> r (e o) n"))
-        nc.sync.dma_start(out=waw[:, 0:3, :], in_=wa_src[:, 0:3, :])
         load_a(2)
-        nc.sync.dma_start(out=waw[:, 3:5, :], in_=wa_src[:, 3:5, :])
+        nc.sync.dma_start(out=waw_first[:], in_=wa_src[:, :, 0:P])
+        load_scales(was, wat_scales.rearrange("e o r n -> r (e o) n"))
+        load_a(3)
+        nc.sync.dma_start(out=waw_rest[:], in_=wa_src[:, :, P:K])
         nc.sync.dma_start(pos1_sb[:], pos1)
         nc.sync.dma_start(pos2_sb[:], pos2)
-        load_scales(nc.sync, wts, wt_scales[0])
-
-        def bank(tag, bufs):
-            return psum.tile([P, 512], F32, name=tag, tag=tag, bufs=bufs)
+        load_scales(wts, wt_scales[0])
 
         def mm_bank():
-            return bank("mm", 2)
+            return psum.tile([P, BANK], F32, name="mm", tag="mm", bufs=2)
 
         def tr_bank():
-            return bank("tr", 3)
+            return psum.tile([P, BANK], F32, name="tr", tag="tr", bufs=3)
 
         def dx_bank():
-            return bank("dxb", 3)
+            return psum.tile([P, BANK], F32, name="dxb", tag="dxb", bufs=3)
 
         warm = mm_bank()
-        for n in range(3):
+        for n in range(WARM_PASSES):
             nc.tensor.matmul_mx(
                 out=warm[:], lhsT=dyw[:, 0:P].bitcast(FP8X4), lhsT_scale=dys[:, 0:P],
-                rhs=dyw[:, 0:512].bitcast(FP8X4), rhs_scale=dys[:, 0:512], start=True, stop=True,
+                rhs=dyw[:, 0:BANK].bitcast(FP8X4), rhs_scale=dys[:, 0:BANK], start=True, stop=True,
             )
-        gb = tr_bank()
-        nc.tensor.transpose(gb[:, 0:P], gate_rows[:], ident[:])
-        nc.scalar.activation(gate2[:], gb[:, 0 : S // P], COPY, scale=2.0)
 
-        for lo, hi in ((0, 1), (1, 3), (3, 5)):
-            cols = slice(lo * C, hi * C)
-            lst = offs_sb[:, lo * C // 16 : hi * C // 16]
-            nc.vector.tensor_copy(xw[:, cols], dyw[:].bitcast(U32).indirect(lst))
-            nc.vector.tensor_copy(xs[:, cols], dys[:].indirect(lst))
+        gate_turned = tr_bank()
+        nc.tensor.transpose(gate_turned[:, 0:P], gate_rows[:], ident[:])
+        nc.scalar.activation(gate2[:], gate_turned[:, 0 : S // P], COPY, scale=2.0)
+
+        for lo, hi in GATHER_CUTS:
+            slots = slice(lo * C, hi * C)
+            entries = offs_sb[:, lo * C // PER_COL : hi * C // PER_COL]
+            nc.vector.tensor_copy(xw[:, slots], dyw[:].bitcast(U32).indirect(entries))
+            nc.vector.tensor_copy(xs[:, slots], dys[:].indirect(entries))
 
         for b in range(S // P):
             e = b * P // C
-            cols = slice(b * P, (b + 1) * P)
+            slots = slice(b * P, (b + 1) * P)
             acc = mm_bank()
             nc.tensor.matmul_mx(
-                out=acc[:], lhsT=xw[:, cols].bitcast(FP8X4), lhsT_scale=xs[:, cols],
+                out=acc[:], lhsT=xw[:, slots].bitcast(FP8X4), lhsT_scale=xs[:, slots],
                 rhs=wbw[:, e, :].bitcast(FP8X4), rhs_scale=wbs[:, e, :], start=True, stop=True,
             )
-            nc.scalar.activation(sg[:, b, :, :], acc[:].rearrange("p (m t) -> p t m", t=4), COPY, scale=gate2[:, b : b + 1])
+            nc.scalar.activation(
+                gated[:, b, :, :], acc[:].rearrange("p (m t) -> p t m", t=PACK), COPY, scale=gate2[:, b : b + 1]
+            )
+
+        def make_dh(b):
+            turned = tr_bank()
+            for t in range(PACK):
+                nc.tensor.transpose(turned[:, t * P : (t + 1) * P], gated[:, b, t, :], ident[:])
+            e = b * P // C
+            n = [i for i, (lo, hi) in enumerate(A_CUTS) if lo <= e < hi][0]
+            s0 = b * P - A_CUTS[n][0] * C
+            nc.vector.scalar_tensor_tensor(
+                out=dh[:, b * P : (b + 1) * P, :],
+                in0=a_sb[n][:, :, s0 : s0 + P].rearrange("p t s -> p s t"),
+                scalar=0.0,
+                in1=turned[:].rearrange("p (t s) -> p s t", t=PACK),
+                op0=ALU.max,
+                op1=ALU.mult,
+            )
 
         def quantize(lo, hi):
             nc.vector.quantize_mx(
                 out=dhw[:, lo:hi].bitcast(FP8X4), scales=dhs[:, lo:hi], in_=dh[:, lo:hi, :].rearrange("p s t -> p (s t)")
             )
 
-        def second(c, lo, hi, last=False):
-            acc = mm_bank() if last else dx_bank()
+        def second(c, lo, hi, acc, copy):
             for s0 in range(lo, hi, C):
                 s1 = min(s0 + C, hi)
                 e = s0 // C
-                w = waw[:, e, c * P : (c + 1) * P]
+                words = waw_first[:, e, :] if c == 0 else waw_rest[:, e, (c - 1) * P : c * P]
                 nc.tensor.matmul_mx(
-                    out=acc[:, s0 - lo : s1 - lo], lhsT=w.bitcast(FP8X4), lhsT_scale=was[:, e, c * P : (c + 1) * P],
+                    out=acc[:, s0 - lo : s1 - lo], lhsT=words.bitcast(FP8X4), lhsT_scale=was[:, e, c * P : (c + 1) * P],
                     rhs=dhw[:, s0:s1].bitcast(FP8X4), rhs_scale=dhs[:, s0:s1], start=True, stop=True,
                 )
-            if last:
-                nc.vector.tensor_copy(dx[c][:, lo:hi], acc[:, 0 : hi - lo])
-            else:
-                nc.scalar.copy(dx[c][:, lo:hi], acc[:, 0 : hi - lo])
+            copy(dx[c][:, lo:hi], acc[:, 0 : hi - lo])
 
-        def make_dh(b):
-            turned = tr_bank()
-            for t in range(4):
-                nc.tensor.transpose(turned[:, t * P : (t + 1) * P], sg[:, b, t, :], ident[:])
-            e = b * P // C
-            n = [i for i, (lo, hi) in enumerate(a_cuts) if lo <= e < hi][0]
-            s0 = b * P - a_cuts[n][0] * C
-            nc.vector.scalar_tensor_tensor(
-                out=dh[:, b * P : (b + 1) * P, :],
-                in0=a_sb[n][:, :, s0 : s0 + P].rearrange("p t s -> p s t"),
-                scalar=0.0,
-                in1=turned[:].rearrange("p (t s) -> p s t", t=4),
-                op0=ALU.max,
-                op1=ALU.mult,
-            )
+        def second_all(c):
+            for lo in range(0, S, BANK):
+                second(c, lo, min(lo + BANK, S), dx_bank(), nc.scalar.copy)
 
         for e in range(E):
             make_dh(2 * e)
             if e > 0:
                 quantize((e - 1) * C, e * C)
-                second(0, (e - 1) * C, e * C)
+                second(0, (e - 1) * C, e * C, dx_bank(), nc.scalar.copy)
             make_dh(2 * e + 1)
-        for lo in (S - C, S - P):
-            quantize(lo, lo + P)
-            second(0, lo, lo + P, last=(lo == S - P))
+        quantize(S - C, S - P)
+        second(0, S - C, S - P, dx_bank(), nc.scalar.copy)
+        quantize(S - P, S)
+        second(0, S - P, S, mm_bank(), nc.vector.tensor_copy)
 
-        wtw = keep.tile([P, 2 * K], U8, tag="a4", align_bytes=64)
+        wtw = keep.tile([P, 2 * K], U8, tag="a%d" % A_CUTS[-1][0], align_bytes=64)
         nc.sync.dma_start(out=wtw[:].bitcast(I32), in_=wt_words[0].bitcast(I32))
+
+        def wt_chunk(c):
+            return wtw[:, 2 * c * P : 2 * (c + 1) * P].bitcast(FP4X4)
 
         def add_turned(dst, first, other):
             nc.tensor.matmul(dst, lhsT=first, rhs=ident[:], start=True, stop=False, is_transpose=True)
             nc.tensor.matmul(dst, lhsT=other, rhs=ident[:], start=False, stop=True, is_transpose=True)
 
-        def second_all(c):
-            for lo, hi in ((0, 512), (512, 1024), (1024, S)):
-                second(c, lo, hi)
+        def add_turned_groups(groups, new_bank, dst, first, other):
+            for b0, b1 in groups:
+                acc = new_bank()
+                for b in range(b0, b1):
+                    block = slice(b * P, (b + 1) * P)
+                    add_turned(acc[:, (b - b0) * P : (b - b0 + 1) * P], first[:, block], other[:, block])
+                nc.scalar.copy(dst[:, b0 * P : b1 * P], acc[:, 0 : (b1 - b0) * P])
 
-        halves = ((0, 3), (3, 5))
+        def sum_on_tensor(c, res, g1, g2, groups):
+            rows = slice(c * P, (c + 1) * P)
+            base_t = ring.tile([P, T], F32)
+            for b0, b1 in groups:
+                acc = mm_bank()
+                for b in range(b0, b1):
+                    block = slice(b * P, (b + 1) * P)
+                    nc.tensor.matmul_mx(
+                        out=acc[:, (b - b0) * P : (b - b0 + 1) * P], lhsT=dyw[:, block].bitcast(FP8X4), lhsT_scale=dys[:, block],
+                        rhs=wt_chunk(c), rhs_scale=wts[:, rows], start=True, stop=True,
+                    )
+                nc.scalar.copy(base_t[:, b0 * P : b1 * P], acc[:, 0 : (b1 - b0) * P])
+            sum_t = ring.tile([P, T], F32)
+            add_turned_groups(groups, dx_bank, sum_t, g1, g2)
+            if c == 0:
+                second_all(CHUNKS - 1)
+            add_turned_groups(groups, tr_bank, res, sum_t, base_t)
+
+        def base_plus(c, part, g1, t0, t1, acc):
+            rows = slice(c * P, (c + 1) * P)
+            for u0 in range(t0, t1, BASE_PASS):
+                u1 = min(u0 + BASE_PASS, t1)
+                nc.tensor.matmul_mx(
+                    out=acc[:, u0 - t0 : u1 - t0], lhsT=wt_chunk(c), lhsT_scale=wts[:, rows],
+                    rhs=dyw[:, u0:u1].bitcast(FP8X4), rhs_scale=dys[:, u0:u1], start=True, stop=True,
+                )
+            nc.vector.tensor_tensor(part[:, t0:t1], g1[:, t0:t1], acc[:, 0 : t1 - t0], ALU.add)
+
+        def finish_on_vector(rows, res, part, g2, t0, t1):
+            nc.vector.tensor_tensor(res[:, t0:t1], part[:, t0:t1], g2[:, t0:t1], ALU.add)
+            nc.sync.dma_start(out=out[rows, t0:t1], in_=res[:, t0:t1])
+
         second_all(1)
         second_all(2)
-        for c in range(4):
+        for c in range(CHUNKS):
             g1 = ring.tile([P, T], F32)
             g2 = ring.tile([P, T], F32)
             res = ring.tile([P, T], F32)
             rows = slice(c * P, (c + 1) * P)
-            w_c = wtw[:, 2 * c * P : 2 * (c + 1) * P].bitcast(FP4X4)
             nc.vector.tensor_copy(g1[:], dx[c][:].indirect(pos1_sb[:]))
-            if c < 3:
+            if c < CHUNKS - 2:
                 nc.vector.tensor_copy(g2[:], dx[c][:].indirect(pos2_sb[:]))
-                base_t = ring.tile([P, T], F32)
-                for b0, b1 in halves:
-                    acc = mm_bank()
-                    for b in range(b0, b1):
-                        cols = slice(b * P, (b + 1) * P)
-                        nc.tensor.matmul_mx(
-                            out=acc[:, (b - b0) * P : (b - b0 + 1) * P], lhsT=dyw[:, cols].bitcast(FP8X4), lhsT_scale=dys[:, cols],
-                            rhs=w_c, rhs_scale=wts[:, rows], start=True, stop=True,
-                        )
-                    nc.scalar.copy(base_t[:, b0 * P : b1 * P], acc[:, 0 : (b1 - b0) * P])
-                sum_t = ring.tile([P, T], F32)
-                for b0, b1 in halves:
-                    acc = dx_bank()
-                    for b in range(b0, b1):
-                        cols = slice(b * P, (b + 1) * P)
-                        add_turned(acc[:, (b - b0) * P : (b - b0 + 1) * P], g1[:, cols], g2[:, cols])
-                    nc.scalar.copy(sum_t[:, b0 * P : b1 * P], acc[:, 0 : (b1 - b0) * P])
-                if c == 0:
-                    second_all(3)
-                for b0, b1 in halves:
-                    acc = tr_bank()
-                    for b in range(b0, b1):
-                        cols = slice(b * P, (b + 1) * P)
-                        add_turned(acc[:, (b - b0) * P : (b - b0 + 1) * P], sum_t[:, cols], base_t[:, cols])
-                    nc.scalar.copy(res[:, b0 * P : b1 * P], acc[:, 0 : (b1 - b0) * P])
+                sum_on_tensor(c, res, g1, g2, TOKEN_GROUPS)
                 nc.sync.dma_start(out=out[rows, :], in_=res[:])
+            elif c == CHUNKS - 2:
+                nc.vector.tensor_copy(g2[:], dx[c][:].indirect(pos2_sb[:]))
+                sum_on_tensor(c, res, g1, g2, TOKEN_GROUPS[0:1])
+                part = ring.tile([P, T], F32)
+                base_plus(c, part, g1, CUT, T, mm_bank())
+                finish_on_vector(rows, res, part, g2, CUT, T)
+                nc.scalar.dma_start(out=out[rows, 0:CUT], in_=res[:, 0:CUT])
             else:
-                part = keep.tile([P, T], F32)
-                cut = 384
-                nc.vector.tensor_copy(g2[:, 0:cut], dx[c][:].indirect(pos2_sb[:, 0 : cut // 16]))
-                for t0, t1 in ((0, cut), (cut, T)):
-                    acc = mm_bank()
-                    for u0 in range(t0, t1, 256):
-                        u1 = min(u0 + 256, t1)
-                        nc.tensor.matmul_mx(
-                            out=acc[:, u0 - t0 : u1 - t0], lhsT=w_c, lhsT_scale=wts[:, rows],
-                            rhs=dyw[:, u0:u1].bitcast(FP8X4), rhs_scale=dys[:, u0:u1], start=True, stop=True,
-                        )
-                    nc.vector.tensor_tensor(part[:, t0:t1], g1[:, t0:t1], acc[:, 0 : t1 - t0], ALU.add)
-                nc.vector.tensor_tensor(res[:, 0:cut], part[:, 0:cut], g2[:, 0:cut], ALU.add)
-                nc.sync.dma_start(out=out[rows, 0:cut], in_=res[:, 0:cut])
-                nc.vector.tensor_copy(g2[:, cut:T], dx[c][:].indirect(pos2_sb[:, cut // 16 : T // 16]))
-                nc.vector.tensor_tensor(res[:, cut:T], part[:, cut:T], g2[:, cut:T], ALU.add)
-                nc.sync.dma_start(out=out[rows, cut:T], in_=res[:, cut:T])
+                part = ring.tile([P, T], F32)
+                nc.vector.tensor_copy(g2[:, 0:CUT], dx[c][:].indirect(pos2_sb[:, 0 : CUT // PER_COL]))
+                base_plus(c, part, g1, 0, CUT, mm_bank())
+                base_plus(c, part, g1, CUT, T, tr_bank())
+                finish_on_vector(rows, res, part, g2, 0, CUT)
+                nc.vector.tensor_copy(g2[:, CUT:T], dx[c][:].indirect(pos2_sb[:, CUT // PER_COL : T // PER_COL]))
+                finish_on_vector(rows, res, part, g2, CUT, T)

@@ -48,6 +48,8 @@ def tile_moe_adb_relu2_kernel(
         dyw = keep.tile([P, WINDOW], I32, align_bytes=64)
         dys = keep.tile([P, WINDOW], U8, align_bytes=64)
         wts = keep.tile([P, K], U8, align_bytes=64)
+        wtw = keep.tile([P, 2 * K], U8, align_bytes=64)
+        base = [keep.tile([P, T], F32, name="base%d" % c) for c in range(CHUNKS)]
         wbw = keep.tile([P, E, H], I32, align_bytes=64)
         wbs = keep.tile([P, E, H], U8, align_bytes=64)
         waw_first = keep.tile([P, E, P], I32, align_bytes=64)
@@ -107,6 +109,7 @@ def tile_moe_adb_relu2_kernel(
         nc.sync.dma_start(pos1_sb[:], pos1)
         nc.sync.dma_start(pos2_sb[:], pos2)
         load_scales(wts, wt_scales[0])
+        nc.sync.dma_start(out=wtw[:].bitcast(I32), in_=wt_words[0].bitcast(I32))
 
         def mm_bank():
             return psum.tile([P, BANK], F32, name="mm", tag="mm", bufs=2)
@@ -188,85 +191,35 @@ def tile_moe_adb_relu2_kernel(
                 quantize((e - 1) * C, e * C)
                 second(0, (e - 1) * C, e * C, dx_bank(), nc.scalar.copy)
             make_dh(2 * e + 1)
+        for c in range(CHUNKS):
+            for t0, t1 in ((0, BANK), (BANK, T)):
+                acc = mm_bank()
+                nc.tensor.matmul_mx(
+                    out=acc[:, 0 : t1 - t0], lhsT=wtw[:, 2 * c * P : 2 * (c + 1) * P].bitcast(FP4X4), lhsT_scale=wts[:, c * P : (c + 1) * P],
+                    rhs=dyw[:, t0:t1].bitcast(FP8X4), rhs_scale=dys[:, t0:t1], start=True, stop=True,
+                )
+                nc.scalar.copy(base[c][:, t0:t1], acc[:, 0 : t1 - t0])
         quantize(S - C, S - P)
         second(0, S - C, S - P, dx_bank(), nc.scalar.copy)
         quantize(S - P, S)
-        second(0, S - P, S, mm_bank(), nc.vector.tensor_copy)
+        second(0, S - P, S, tr_bank(), nc.vector.tensor_copy)
 
-        wtw = keep.tile([P, 2 * K], U8, tag="a%d" % A_CUTS[-1][0], align_bytes=64)
-        nc.sync.dma_start(out=wtw[:].bitcast(I32), in_=wt_words[0].bitcast(I32))
+        for c in range(1, CHUNKS):
+            second_all(c)
+        part = [keep.tile([P, T], F32, name="part%d" % c) for c in range(CHUNKS)]
+        res = [keep.tile([P, T], F32, name="res%d" % c) for c in range(CHUNKS)]
 
-        def wt_chunk(c):
-            return wtw[:, 2 * c * P : 2 * (c + 1) * P].bitcast(FP4X4)
+        def first_sum(c):
+            nc.vector.tensor_tensor(part[c][:], dx[c][:].indirect(pos1_sb[:]), base[c][:], ALU.add)
 
-        def add_turned(dst, first, other):
-            nc.tensor.matmul(dst, lhsT=first, rhs=ident[:], start=True, stop=False, is_transpose=True)
-            nc.tensor.matmul(dst, lhsT=other, rhs=ident[:], start=False, stop=True, is_transpose=True)
+        def last_sum(c, t0, t1):
+            entries = pos2_sb[:, t0 // PER_COL : t1 // PER_COL]
+            nc.vector.tensor_tensor(res[c][:, t0:t1], dx[c][:].indirect(entries), part[c][:, t0:t1], ALU.add)
+            nc.sync.dma_start(out=out[c * P : (c + 1) * P, t0:t1], in_=res[c][:, t0:t1])
 
-        def add_turned_groups(groups, new_bank, dst, first, other):
-            for b0, b1 in groups:
-                acc = new_bank()
-                for b in range(b0, b1):
-                    block = slice(b * P, (b + 1) * P)
-                    add_turned(acc[:, (b - b0) * P : (b - b0 + 1) * P], first[:, block], other[:, block])
-                nc.scalar.copy(dst[:, b0 * P : b1 * P], acc[:, 0 : (b1 - b0) * P])
-
-        def sum_on_tensor(c, res, g1, g2, groups):
-            rows = slice(c * P, (c + 1) * P)
-            base_t = ring.tile([P, T], F32)
-            for b0, b1 in groups:
-                acc = mm_bank()
-                for b in range(b0, b1):
-                    block = slice(b * P, (b + 1) * P)
-                    nc.tensor.matmul_mx(
-                        out=acc[:, (b - b0) * P : (b - b0 + 1) * P], lhsT=dyw[:, block].bitcast(FP8X4), lhsT_scale=dys[:, block],
-                        rhs=wt_chunk(c), rhs_scale=wts[:, rows], start=True, stop=True,
-                    )
-                nc.scalar.copy(base_t[:, b0 * P : b1 * P], acc[:, 0 : (b1 - b0) * P])
-            sum_t = ring.tile([P, T], F32)
-            add_turned_groups(groups, dx_bank, sum_t, g1, g2)
-            if c == 0:
-                second_all(CHUNKS - 1)
-            add_turned_groups(groups, tr_bank, res, sum_t, base_t)
-
-        def base_plus(c, part, g1, t0, t1, acc):
-            rows = slice(c * P, (c + 1) * P)
-            for u0 in range(t0, t1, BASE_PASS):
-                u1 = min(u0 + BASE_PASS, t1)
-                nc.tensor.matmul_mx(
-                    out=acc[:, u0 - t0 : u1 - t0], lhsT=wt_chunk(c), lhsT_scale=wts[:, rows],
-                    rhs=dyw[:, u0:u1].bitcast(FP8X4), rhs_scale=dys[:, u0:u1], start=True, stop=True,
-                )
-            nc.vector.tensor_tensor(part[:, t0:t1], g1[:, t0:t1], acc[:, 0 : t1 - t0], ALU.add)
-
-        def finish_on_vector(rows, res, part, g2, t0, t1):
-            nc.vector.tensor_tensor(res[:, t0:t1], part[:, t0:t1], g2[:, t0:t1], ALU.add)
-            nc.sync.dma_start(out=out[rows, t0:t1], in_=res[:, t0:t1])
-
-        second_all(1)
-        second_all(2)
-        for c in range(CHUNKS):
-            g1 = ring.tile([P, T], F32)
-            g2 = ring.tile([P, T], F32)
-            res = ring.tile([P, T], F32)
-            rows = slice(c * P, (c + 1) * P)
-            nc.vector.tensor_copy(g1[:], dx[c][:].indirect(pos1_sb[:]))
-            if c < CHUNKS - 2:
-                nc.vector.tensor_copy(g2[:], dx[c][:].indirect(pos2_sb[:]))
-                sum_on_tensor(c, res, g1, g2, TOKEN_GROUPS)
-                nc.sync.dma_start(out=out[rows, :], in_=res[:])
-            elif c == CHUNKS - 2:
-                nc.vector.tensor_copy(g2[:], dx[c][:].indirect(pos2_sb[:]))
-                sum_on_tensor(c, res, g1, g2, TOKEN_GROUPS[0:1])
-                part = ring.tile([P, T], F32)
-                base_plus(c, part, g1, CUT, T, mm_bank())
-                finish_on_vector(rows, res, part, g2, CUT, T)
-                nc.scalar.dma_start(out=out[rows, 0:CUT], in_=res[:, 0:CUT])
-            else:
-                part = ring.tile([P, T], F32)
-                nc.vector.tensor_copy(g2[:, 0:CUT], dx[c][:].indirect(pos2_sb[:, 0 : CUT // PER_COL]))
-                base_plus(c, part, g1, 0, CUT, mm_bank())
-                base_plus(c, part, g1, CUT, T, tr_bank())
-                finish_on_vector(rows, res, part, g2, 0, CUT)
-                nc.vector.tensor_copy(g2[:, CUT:T], dx[c][:].indirect(pos2_sb[:, CUT // PER_COL : T // PER_COL]))
-                finish_on_vector(rows, res, part, g2, CUT, T)
+        first_sum(0)
+        for c in range(1, CHUNKS):
+            first_sum(c)
+            last_sum(c - 1, 0, T)
+        last_sum(CHUNKS - 1, 0, CUT)
+        last_sum(CHUNKS - 1, CUT, T)

@@ -20,6 +20,7 @@ TOKEN_GROUPS = ((0, 3), (3, 5))
 CUT = TOKEN_GROUPS[1][0] * P
 BASE_PASS = 256
 WARM_PASSES = 3
+NB = 3
 
 F32 = mybir.dt.float32
 BF16 = mybir.dt.bfloat16
@@ -49,11 +50,10 @@ def tile_moe_adb_relu2_kernel(
         dys = keep.tile([P, WINDOW], U8, align_bytes=64)
         wts = keep.tile([P, K], U8, align_bytes=64)
         wtw = keep.tile([P, 2 * K], U8, align_bytes=64)
-        base = [keep.tile([P, T], F32, name="base%d" % c) for c in range(CHUNKS)]
+        base = keep.tile([P, CHUNKS, T], F32)
         wbw = keep.tile([P, E, H], I32, align_bytes=64)
         wbs = keep.tile([P, E, H], U8, align_bytes=64)
-        waw_first = keep.tile([P, E, P], I32, align_bytes=64)
-        waw_rest = keep.tile([P, E, K - P], I32, align_bytes=64)
+        waw = keep.tile([P, E, K], I32, align_bytes=64)
         was = keep.tile([P, E, K], U8, align_bytes=64)
         gate_rows = keep.tile([P, P], F32)
         gate2 = keep.tile([P, S // P], F32)
@@ -69,7 +69,7 @@ def tile_moe_adb_relu2_kernel(
         ]
         dx = [keep.tile([P, S], F32, name="dx%d" % c) for c in range(CHUNKS)]
 
-        nc.vector.memset(dys[:].bitcast(I32), 0)
+        nc.gpsimd.memset(dys[:].bitcast(I32), 0)
         nc.vector.memset(dyw[:, T:WINDOW], 0)
         nc.vector.memset(wbs[:].rearrange("p e n -> p (e n)").bitcast(I32), 0)
         nc.vector.memset(was[:].rearrange("p e n -> p (e n)").bitcast(I32), 0)
@@ -92,9 +92,9 @@ def tile_moe_adb_relu2_kernel(
             lo, hi = A_CUTS[n]
             nc.sync.dma_start(out=a_sb[n][:], in_=a_src[:, :, lo * C : hi * C])
 
-        nc.sync.dma_start(offs_sb[:], offs)
         nc.sync.dma_start(out=dyw[:, 0:T], in_=dy_words[0].rearrange("p t d -> p (t d)").bitcast(I32))
         load_scales(dys[:, 0:T], dy_scales[0])
+        nc.sync.dma_start(offs_sb[:], offs)
         nc.sync.dma_start(out=wbw[:, 0:WB_FIRST, :], in_=wb_src[:, 0:WB_FIRST, :])
         nc.sync.dma_start(out=gate_rows[:], in_=gate.rearrange("r (c s) -> (r c) s", s=P)[0:P, :])
         load_scales(wbs, wbt_scales.rearrange("e o r n -> r (e o) n"))
@@ -102,32 +102,25 @@ def tile_moe_adb_relu2_kernel(
         nc.sync.dma_start(out=wbw[:, WB_FIRST:E, :], in_=wb_src[:, WB_FIRST:E, :])
         load_a(1)
         load_a(2)
-        nc.sync.dma_start(out=waw_first[:], in_=wa_src[:, :, 0:P])
-        load_scales(was, wat_scales.rearrange("e o r n -> r (e o) n"))
         load_a(3)
-        nc.sync.dma_start(out=waw_rest[:], in_=wa_src[:, :, P:K])
+        nc.sync.dma_start(out=wtw[:].bitcast(I32), in_=wt_words[0].bitcast(I32))
+        load_scales(wts, wt_scales[0])
+        nc.sync.dma_start(out=waw[:], in_=wa_src)
+        load_scales(was, wat_scales.rearrange("e o r n -> r (e o) n"))
         nc.sync.dma_start(pos1_sb[:], pos1)
         nc.sync.dma_start(pos2_sb[:], pos2)
-        load_scales(wts, wt_scales[0])
-        nc.sync.dma_start(out=wtw[:].bitcast(I32), in_=wt_words[0].bitcast(I32))
 
-        def mm_bank():
-            return psum.tile([P, BANK], F32, name="mm", tag="mm", bufs=2)
+        banks = [psum.tile([P, BANK], F32, name="bank%d" % n) for n in range(8)]
+        mm_banks, tr_banks, dx_banks = banks[0:5], banks[5:8], banks[2:5]
 
-        def tr_bank():
-            return psum.tile([P, BANK], F32, name="tr", tag="tr", bufs=3)
-
-        def dx_bank():
-            return psum.tile([P, BANK], F32, name="dxb", tag="dxb", bufs=3)
-
-        warm = mm_bank()
+        warm = mm_banks[4]
         for n in range(WARM_PASSES):
             nc.tensor.matmul_mx(
                 out=warm[:], lhsT=dyw[:, 0:P].bitcast(FP8X4), lhsT_scale=dys[:, 0:P],
                 rhs=dyw[:, 0:BANK].bitcast(FP8X4), rhs_scale=dys[:, 0:BANK], start=True, stop=True,
             )
 
-        gate_turned = tr_bank()
+        gate_turned = tr_banks[2]
         nc.tensor.transpose(gate_turned[:, 0:P], gate_rows[:], ident[:])
         nc.scalar.activation(gate2[:], gate_turned[:, 0 : S // P], COPY, scale=2.0)
 
@@ -137,10 +130,10 @@ def tile_moe_adb_relu2_kernel(
             nc.vector.tensor_copy(xw[:, slots], dyw[:].bitcast(U32).indirect(entries))
             nc.vector.tensor_copy(xs[:, slots], dys[:].indirect(entries))
 
-        for b in range(S // P):
+        def first(b):
             e = b * P // C
             slots = slice(b * P, (b + 1) * P)
-            acc = mm_bank()
+            acc = mm_banks[b % NB]
             nc.tensor.matmul_mx(
                 out=acc[:], lhsT=xw[:, slots].bitcast(FP8X4), lhsT_scale=xs[:, slots],
                 rhs=wbw[:, e, :].bitcast(FP8X4), rhs_scale=wbs[:, e, :], start=True, stop=True,
@@ -150,7 +143,7 @@ def tile_moe_adb_relu2_kernel(
             )
 
         def make_dh(b):
-            turned = tr_bank()
+            turned = tr_banks[b % 3]
             for t in range(PACK):
                 nc.tensor.transpose(turned[:, t * P : (t + 1) * P], gated[:, b, t, :], ident[:])
             e = b * P // C
@@ -174,52 +167,65 @@ def tile_moe_adb_relu2_kernel(
             for s0 in range(lo, hi, C):
                 s1 = min(s0 + C, hi)
                 e = s0 // C
-                words = waw_first[:, e, :] if c == 0 else waw_rest[:, e, (c - 1) * P : c * P]
+                words = waw[:, e, c * P : (c + 1) * P]
                 nc.tensor.matmul_mx(
                     out=acc[:, s0 - lo : s1 - lo], lhsT=words.bitcast(FP8X4), lhsT_scale=was[:, e, c * P : (c + 1) * P],
                     rhs=dhw[:, s0:s1].bitcast(FP8X4), rhs_scale=dhs[:, s0:s1], start=True, stop=True,
                 )
             copy(dx[c][:, lo:hi], acc[:, 0 : hi - lo])
 
-        def second_all(c):
-            for lo in range(0, S, BANK):
-                second(c, lo, min(lo + BANK, S), dx_bank(), nc.scalar.copy)
+        def base_pass(c, t0, t1, dst):
+            nc.tensor.matmul_mx(
+                out=dst, lhsT=wtw[:, 2 * c * P : 2 * (c + 1) * P].bitcast(FP4X4), lhsT_scale=wts[:, c * P : (c + 1) * P],
+                rhs=dyw[:, t0:t1].bitcast(FP8X4), rhs_scale=dys[:, t0:t1], start=True, stop=True,
+            )
 
-        for e in range(E):
-            make_dh(2 * e)
-            if e > 0:
-                quantize((e - 1) * C, e * C)
-                second(0, (e - 1) * C, e * C, dx_bank(), nc.scalar.copy)
-            make_dh(2 * e + 1)
-        for c in range(CHUNKS):
-            for t0, t1 in ((0, BANK), (BANK, T)):
-                acc = mm_bank()
-                nc.tensor.matmul_mx(
-                    out=acc[:, 0 : t1 - t0], lhsT=wtw[:, 2 * c * P : 2 * (c + 1) * P].bitcast(FP4X4), lhsT_scale=wts[:, c * P : (c + 1) * P],
-                    rhs=dyw[:, t0:t1].bitcast(FP8X4), rhs_scale=dys[:, t0:t1], start=True, stop=True,
-                )
-                nc.scalar.copy(base[c][:, t0:t1], acc[:, 0 : t1 - t0])
+        def base_main(c, acc):
+            base_pass(c, 0, BANK, acc[:])
+            nc.scalar.copy(base[:, c, 0:BANK], acc[:])
+
+        def base_tails(acc):
+            for c in range(CHUNKS):
+                base_pass(c, BANK, T, acc[:, c * P : (c + 1) * P])
+            nc.scalar.copy(base[:, :, BANK:T], acc[:].rearrange("p (c t) -> p c t", c=CHUNKS))
+
+        first(0)
+        for b in range(S // P):
+            if b + 1 < S // P:
+                first(b + 1)
+            make_dh(b)
+            if b % 2 == 0 and b > 0:
+                quantize((b - 2) * P, b * P)
+        base_main(0, tr_banks[1])
+        base_tails(tr_banks[2])
+        for e in range(E - 1):
+            second(0, e * C, (e + 1) * C, mm_banks[(e + 3) % 5], nc.scalar.copy)
         quantize(S - C, S - P)
-        second(0, S - C, S - P, dx_bank(), nc.scalar.copy)
+        second(0, S - C, S - P, mm_banks[2], nc.scalar.copy)
         quantize(S - P, S)
-        second(0, S - P, S, tr_bank(), nc.vector.tensor_copy)
+        second(0, S - P, S, mm_banks[3], nc.vector.tensor_copy)
 
+        later = [mm_banks[2], mm_banks[3], tr_banks[0]]
         for c in range(1, CHUNKS):
-            second_all(c)
+            for n, lo in enumerate(range(0, S, BANK)):
+                second(c, lo, min(lo + BANK, S), later[n], nc.scalar.copy)
+            base_main(c, mm_banks[1])
+
         part = [keep.tile([P, T], F32, name="part%d" % c) for c in range(CHUNKS)]
         res = [keep.tile([P, T], F32, name="res%d" % c) for c in range(CHUNKS)]
 
-        def first_sum(c):
-            nc.vector.tensor_tensor(part[c][:], dx[c][:].indirect(pos1_sb[:]), base[c][:], ALU.add)
+        def gather_add(dst, c, pos_sb, other, t0, t1):
+            entries = pos_sb[:, t0 // PER_COL : t1 // PER_COL]
+            nc.vector.tensor_tensor(dst[:, t0:t1], dx[c][:].indirect(entries), other[:, t0:t1], ALU.add)
 
-        def last_sum(c, t0, t1):
-            entries = pos2_sb[:, t0 // PER_COL : t1 // PER_COL]
-            nc.vector.tensor_tensor(res[c][:, t0:t1], dx[c][:].indirect(entries), part[c][:, t0:t1], ALU.add)
-            nc.sync.dma_start(out=out[c * P : (c + 1) * P, t0:t1], in_=res[c][:, t0:t1])
-
-        first_sum(0)
-        for c in range(1, CHUNKS):
-            first_sum(c)
-            last_sum(c - 1, 0, T)
-        last_sum(CHUNKS - 1, 0, CUT)
-        last_sum(CHUNKS - 1, CUT, T)
+        for c in range(CHUNKS):
+            rows = slice(c * P, (c + 1) * P)
+            pieces = ((0, CUT), (CUT, T))
+            for t0, t1 in pieces:
+                gather_add(part[c], c, pos1_sb, base[:, c, :], t0, t1)
+            for t0, t1 in pieces:
+                gather_add(res[c], c, pos2_sb, part[c], t0, t1)
+                if c == CHUNKS - 1:
+                    nc.sync.dma_start(out=out[rows, t0:t1], in_=res[c][:, t0:t1])
+            if c < CHUNKS - 1:
+                nc.sync.dma_start(out=out[rows, :], in_=res[c][:])

@@ -14,7 +14,7 @@ WINDOW = 768
 FLOPS = 2 * K * N * T + 2 * S * N * H + 2 * S * H * K
 
 GATHER_CUTS = ((0, 1), (1, 3), (3, 5))
-A_CUTS = ((0, 1), (1, 3), (3, 4), (4, 5))
+A_CUTS = ((0, 2), (2, 4), (4, 5))
 WB_FIRST = 3
 TOKEN_GROUPS = ((0, 3), (3, 5))
 CUT = TOKEN_GROUPS[1][0] * P
@@ -53,7 +53,7 @@ def tile_moe_adb_relu2_kernel(
         base = keep.tile([P, CHUNKS, T], F32)
         wbw = keep.tile([P, E, H], I32, align_bytes=64)
         wbs = keep.tile([P, E, H], U8, align_bytes=64)
-        waw = keep.tile([P, E, K], I32, align_bytes=64)
+        waw = [keep.tile([P, E, K // 2], I32, name="waw%d" % h, align_bytes=64) for h in range(2)]
         was = keep.tile([P, E, K], U8, align_bytes=64)
         gate_rows = keep.tile([P, P], F32)
         gate2 = keep.tile([P, S // P], F32)
@@ -100,15 +100,15 @@ def tile_moe_adb_relu2_kernel(
         load_scales(wbs, wbt_scales.rearrange("e o r n -> r (e o) n"))
         load_a(0)
         nc.sync.dma_start(out=wbw[:, WB_FIRST:E, :], in_=wb_src[:, WB_FIRST:E, :])
-        load_a(1)
-        load_a(2)
-        load_a(3)
         nc.sync.dma_start(out=wtw[:].bitcast(I32), in_=wt_words[0].bitcast(I32))
         load_scales(wts, wt_scales[0])
-        nc.sync.dma_start(out=waw[:], in_=wa_src)
+        load_a(1)
+        load_a(2)
+        nc.sync.dma_start(out=waw[0][:], in_=wa_src[:, :, 0 : K // 2])
         load_scales(was, wat_scales.rearrange("e o r n -> r (e o) n"))
         nc.sync.dma_start(pos1_sb[:], pos1)
         nc.sync.dma_start(pos2_sb[:], pos2)
+        nc.sync.dma_start(out=waw[1][:], in_=wa_src[:, :, K // 2 : K])
 
         banks = [psum.tile([P, BANK], F32, name="bank%d" % n) for n in range(8)]
         mm_banks, tr_banks, dx_banks = banks[0:5], banks[5:8], banks[2:5]
@@ -167,7 +167,7 @@ def tile_moe_adb_relu2_kernel(
             for s0 in range(lo, hi, C):
                 s1 = min(s0 + C, hi)
                 e = s0 // C
-                words = waw[:, e, c * P : (c + 1) * P]
+                words = waw[c // 2][:, e, c % 2 * P : (c % 2 + 1) * P]
                 nc.tensor.matmul_mx(
                     out=acc[:, s0 - lo : s1 - lo], lhsT=words.bitcast(FP8X4), lhsT_scale=was[:, e, c * P : (c + 1) * P],
                     rhs=dhw[:, s0:s1].bitcast(FP8X4), rhs_scale=dhs[:, s0:s1], start=True, stop=True,

@@ -19,7 +19,6 @@ WB_FIRST = 3
 TOKEN_GROUPS = ((0, 3), (3, 5))
 CUT = TOKEN_GROUPS[1][0] * P
 BASE_PASS = 256
-WARM_PASSES = 3
 NB = 3
 
 F32 = mybir.dt.float32
@@ -80,10 +79,10 @@ def tile_moe_adb_relu2_kernel(
         wa_src = wat_words.rearrange("e o p n d -> p (e o) (n d)").bitcast(I32)
         a_src = a.rearrange("(p t) s -> p t s", t=PACK)
 
-        def load_scales(tile, rows):
+        def load_scales(tile, rows, queues=(nc.sync,) * 4):
             rest = (slice(None),) * (len(rows.shape) - 1)
             for q in range(4):
-                nc.sync.dma_start(
+                queues[q].dma_start(
                     out=tile[(slice(32 * q, 32 * q + 4),) + rest].bitcast(I32),
                     in_=rows[(slice(4 * q, 4 * q + 4),) + rest].bitcast(I32),
                 )
@@ -93,17 +92,17 @@ def tile_moe_adb_relu2_kernel(
             nc.sync.dma_start(out=a_sb[n][:], in_=a_src[:, :, lo * C : hi * C])
 
         nc.sync.dma_start(out=dyw[:, 0:T], in_=dy_words[0].rearrange("p t d -> p (t d)").bitcast(I32))
-        load_scales(dys[:, 0:T], dy_scales[0])
+        load_scales(dys[:, 0:T], dy_scales[0], (nc.scalar, nc.scalar, nc.sync, nc.sync))
         nc.sync.dma_start(offs_sb[:], offs)
         nc.sync.dma_start(out=wbw[:, 0:WB_FIRST, :], in_=wb_src[:, 0:WB_FIRST, :])
         nc.sync.dma_start(out=gate_rows[:], in_=gate.rearrange("r (c s) -> (r c) s", s=P)[0:P, :])
         load_scales(wbs, wbt_scales.rearrange("e o r n -> r (e o) n"))
         load_a(0)
         nc.sync.dma_start(out=wbw[:, WB_FIRST:E, :], in_=wb_src[:, WB_FIRST:E, :])
-        nc.sync.dma_start(out=wtw[:].bitcast(I32), in_=wt_words[0].bitcast(I32))
-        load_scales(wts, wt_scales[0])
         load_a(1)
         load_a(2)
+        nc.sync.dma_start(out=wtw[:].bitcast(I32), in_=wt_words[0].bitcast(I32))
+        load_scales(wts, wt_scales[0])
         nc.sync.dma_start(out=waw[0][:], in_=wa_src[:, :, 0 : K // 2])
         load_scales(was, wat_scales.rearrange("e o r n -> r (e o) n"))
         nc.sync.dma_start(pos1_sb[:], pos1)
@@ -112,13 +111,6 @@ def tile_moe_adb_relu2_kernel(
 
         banks = [psum.tile([P, BANK], F32, name="bank%d" % n) for n in range(8)]
         mm_banks, tr_banks, dx_banks = banks[0:5], banks[5:8], banks[2:5]
-
-        warm = mm_banks[4]
-        for n in range(WARM_PASSES):
-            nc.tensor.matmul_mx(
-                out=warm[:], lhsT=dyw[:, 0:P].bitcast(FP8X4), lhsT_scale=dys[:, 0:P],
-                rhs=dyw[:, 0:BANK].bitcast(FP8X4), rhs_scale=dys[:, 0:BANK], start=True, stop=True,
-            )
 
         gate_turned = tr_banks[2]
         nc.tensor.transpose(gate_turned[:, 0:P], gate_rows[:], ident[:])
@@ -193,23 +185,28 @@ def tile_moe_adb_relu2_kernel(
         for b in range(S // P):
             if b + 1 < S // P:
                 first(b + 1)
+            if b == 9:
+                base_main(0, mm_banks[3])
+                base_tails(mm_banks[4])
+                for c in range(1, 1):
+                    base_main(c, mm_banks[3 + (c + 1) % 2])
             make_dh(b)
             if b % 2 == 0 and b > 0:
                 quantize((b - 2) * P, b * P)
-        base_main(0, tr_banks[1])
-        base_tails(tr_banks[2])
-        for e in range(E - 1):
-            second(0, e * C, (e + 1) * C, mm_banks[(e + 3) % 5], nc.scalar.copy)
+        second(0, 0, 2 * C, mm_banks[0], nc.scalar.copy)
+        second(0, 2 * C, 3 * C, mm_banks[1], nc.scalar.copy)
+        second(0, 3 * C, 4 * C, mm_banks[2], nc.scalar.copy)
         quantize(S - C, S - P)
-        second(0, S - C, S - P, mm_banks[2], nc.scalar.copy)
+        second(0, S - C, S - P, mm_banks[4], nc.scalar.copy)
         quantize(S - P, S)
         second(0, S - P, S, mm_banks[3], nc.vector.tensor_copy)
 
-        later = [mm_banks[2], mm_banks[3], tr_banks[0]]
+        later = [mm_banks[4], mm_banks[3], tr_banks[0]]
         for c in range(1, CHUNKS):
             for n, lo in enumerate(range(0, S, BANK)):
                 second(c, lo, min(lo + BANK, S), later[n], nc.scalar.copy)
-            base_main(c, mm_banks[1])
+            if c >= 1:
+                base_main(c, mm_banks[1])
 
         part = [keep.tile([P, T], F32, name="part%d" % c) for c in range(CHUNKS)]
         res = [keep.tile([P, T], F32, name="res%d" % c) for c in range(CHUNKS)]

@@ -10,16 +10,15 @@ PACK = 4
 BANK = 512
 PER_COL = 16
 CHUNKS = K // P
+BLOCKS = S // P
 WINDOW = 768
 FLOPS = 2 * K * N * T + 2 * S * N * H + 2 * S * H * K
 
 GATHER_CUTS = ((0, 1), (1, 3), (3, 5))
 A_CUTS = ((0, 2), (2, 4), (4, 5))
 WB_FIRST = 3
-TOKEN_GROUPS = ((0, 3), (3, 5))
-CUT = TOKEN_GROUPS[1][0] * P
-BASE_PASS = 256
-NB = 3
+QUANT_BLOCKS = 4
+TOKEN_PIECES = ((0, 384), (384, T))
 
 F32 = mybir.dt.float32
 BF16 = mybir.dt.bfloat16
@@ -39,7 +38,6 @@ def tile_moe_adb_relu2_kernel(
     nc = tc.nc
     with ExitStack() as ctx:
         keep = ctx.enter_context(tc.tile_pool(name="keep", bufs=1))
-        ring = ctx.enter_context(tc.tile_pool(name="ring", bufs=CHUNKS))
         psum = ctx.enter_context(tc.psum_pool(name="psum", bufs=1))
 
         offs_sb = keep.tile([P, S // PER_COL], U16)
@@ -55,21 +53,24 @@ def tile_moe_adb_relu2_kernel(
         waw = [keep.tile([P, E, K // 2], I32, name="waw%d" % h, align_bytes=64) for h in range(2)]
         was = keep.tile([P, E, K], U8, align_bytes=64)
         gate_rows = keep.tile([P, P], F32)
-        gate2 = keep.tile([P, S // P], F32)
+        gate2 = keep.tile([P, BLOCKS], F32)
         ident = keep.tile([P, P], F32)
         xw = keep.tile([P, S], U32, align_bytes=64)
         xs = keep.tile([P, S], U8, align_bytes=64)
-        gated = keep.tile([P, S // P, PACK, P], F32)
+        gated = keep.tile([P, BLOCKS, PACK, P], F32)
         dh = keep.tile([P, S, PACK], BF16, align_bytes=64)
         dhw = keep.tile([P, S], U32, align_bytes=64)
         dhs = keep.tile([P, S], U8, align_bytes=64)
         a_sb = [
-            keep.tile([P, PACK, (hi - lo) * C], F32, name="a%d" % lo, tag="a%d" % lo, align_bytes=64) for lo, hi in A_CUTS
+            keep.tile([P, PACK, (hi - lo) * C], F32, name="a%d" % lo, align_bytes=64) for lo, hi in A_CUTS
         ]
         dx = [keep.tile([P, S], F32, name="dx%d" % c) for c in range(CHUNKS)]
+        part = [keep.tile([P, T], F32, name="part%d" % c) for c in range(CHUNKS)]
+        res = [keep.tile([P, T], F32, name="res%d" % c) for c in range(CHUNKS)]
 
         nc.gpsimd.memset(dys[:].bitcast(I32), 0)
         nc.vector.memset(dyw[:, T:WINDOW], 0)
+        nc.vector.memset(gate_rows[:], 0.0)
         nc.vector.memset(wbs[:].rearrange("p e n -> p (e n)").bitcast(I32), 0)
         nc.vector.memset(was[:].rearrange("p e n -> p (e n)").bitcast(I32), 0)
         nc.vector.memset(wts[:].bitcast(I32), 0)
@@ -95,7 +96,7 @@ def tile_moe_adb_relu2_kernel(
         load_scales(dys[:, 0:T], dy_scales[0], (nc.scalar, nc.scalar, nc.sync, nc.sync))
         nc.sync.dma_start(offs_sb[:], offs)
         nc.sync.dma_start(out=wbw[:, 0:WB_FIRST, :], in_=wb_src[:, 0:WB_FIRST, :])
-        nc.sync.dma_start(out=gate_rows[:], in_=gate.rearrange("r (c s) -> (r c) s", s=P)[0:P, :])
+        nc.sync.dma_start(out=gate_rows[0:BLOCKS, :], in_=gate[0].rearrange("(b p) -> b p", p=P))
         load_scales(wbs, wbt_scales.rearrange("e o r n -> r (e o) n"))
         load_a(0)
         nc.sync.dma_start(out=wbw[:, WB_FIRST:E, :], in_=wb_src[:, WB_FIRST:E, :])
@@ -110,11 +111,11 @@ def tile_moe_adb_relu2_kernel(
         nc.sync.dma_start(out=waw[1][:], in_=wa_src[:, :, K // 2 : K])
 
         banks = [psum.tile([P, BANK], F32, name="bank%d" % n) for n in range(8)]
-        mm_banks, tr_banks, dx_banks = banks[0:5], banks[5:8], banks[2:5]
+        first_banks, base_banks, turn_banks = banks[0:3], banks[3:5], banks[5:8]
 
-        gate_turned = tr_banks[2]
+        gate_turned = turn_banks[-1]
         nc.tensor.transpose(gate_turned[:, 0:P], gate_rows[:], ident[:])
-        nc.scalar.activation(gate2[:], gate_turned[:, 0 : S // P], COPY, scale=2.0)
+        nc.scalar.activation(gate2[:], gate_turned[:, 0:BLOCKS], COPY, scale=2.0)
 
         for lo, hi in GATHER_CUTS:
             slots = slice(lo * C, hi * C)
@@ -125,7 +126,7 @@ def tile_moe_adb_relu2_kernel(
         def first(b):
             e = b * P // C
             slots = slice(b * P, (b + 1) * P)
-            acc = mm_banks[b % NB]
+            acc = first_banks[b % len(first_banks)]
             nc.tensor.matmul_mx(
                 out=acc[:], lhsT=xw[:, slots].bitcast(FP8X4), lhsT_scale=xs[:, slots],
                 rhs=wbw[:, e, :].bitcast(FP8X4), rhs_scale=wbs[:, e, :], start=True, stop=True,
@@ -135,7 +136,7 @@ def tile_moe_adb_relu2_kernel(
             )
 
         def make_dh(b):
-            turned = tr_banks[b % 3]
+            turned = turn_banks[b % len(turn_banks)]
             for t in range(PACK):
                 nc.tensor.transpose(turned[:, t * P : (t + 1) * P], gated[:, b, t, :], ident[:])
             e = b * P // C
@@ -182,34 +183,28 @@ def tile_moe_adb_relu2_kernel(
             nc.scalar.copy(base[:, :, BANK:T], acc[:].rearrange("p (c t) -> p c t", c=CHUNKS))
 
         first(0)
-        for b in range(S // P):
-            if b + 1 < S // P:
+        for b in range(BLOCKS):
+            if b + 1 < BLOCKS:
                 first(b + 1)
-            if b == 9:
-                base_main(0, mm_banks[3])
-                base_tails(mm_banks[4])
-                for c in range(1, 1):
-                    base_main(c, mm_banks[3 + (c + 1) % 2])
+            else:
+                base_main(0, base_banks[0])
+                base_tails(base_banks[1])
             make_dh(b)
-            if b % 2 == 0 and b > 0:
-                quantize((b - 2) * P, b * P)
-        second(0, 0, 2 * C, mm_banks[0], nc.scalar.copy)
-        second(0, 2 * C, 3 * C, mm_banks[1], nc.scalar.copy)
-        second(0, 3 * C, 4 * C, mm_banks[2], nc.scalar.copy)
+            if b > 0 and b % QUANT_BLOCKS == 0:
+                quantize((b - QUANT_BLOCKS) * P, b * P)
+
+        second(0, 0, BANK, first_banks[0], nc.scalar.copy)
+        second(0, BANK, 2 * BANK, first_banks[1], nc.scalar.copy)
         quantize(S - C, S - P)
-        second(0, S - C, S - P, mm_banks[4], nc.scalar.copy)
+        second(0, S - C, S - P, base_banks[1], nc.scalar.copy)
         quantize(S - P, S)
-        second(0, S - P, S, mm_banks[3], nc.vector.tensor_copy)
+        second(0, S - P, S, base_banks[0], nc.vector.tensor_copy)
 
-        later = [mm_banks[4], mm_banks[3], tr_banks[0]]
+        later_banks = [base_banks[1], base_banks[0], turn_banks[0]]
         for c in range(1, CHUNKS):
-            for n, lo in enumerate(range(0, S, BANK)):
-                second(c, lo, min(lo + BANK, S), later[n], nc.scalar.copy)
-            if c >= 1:
-                base_main(c, mm_banks[1])
-
-        part = [keep.tile([P, T], F32, name="part%d" % c) for c in range(CHUNKS)]
-        res = [keep.tile([P, T], F32, name="res%d" % c) for c in range(CHUNKS)]
+            for acc, lo in zip(later_banks, range(0, S, BANK)):
+                second(c, lo, min(lo + BANK, S), acc, nc.scalar.copy)
+            base_main(c, first_banks[1])
 
         def gather_add(dst, c, pos_sb, other, t0, t1):
             entries = pos_sb[:, t0 // PER_COL : t1 // PER_COL]
@@ -217,12 +212,12 @@ def tile_moe_adb_relu2_kernel(
 
         for c in range(CHUNKS):
             rows = slice(c * P, (c + 1) * P)
-            pieces = ((0, CUT), (CUT, T))
-            for t0, t1 in pieces:
+            last = c == CHUNKS - 1
+            for t0, t1 in TOKEN_PIECES:
                 gather_add(part[c], c, pos1_sb, base[:, c, :], t0, t1)
-            for t0, t1 in pieces:
+            for t0, t1 in TOKEN_PIECES:
                 gather_add(res[c], c, pos2_sb, part[c], t0, t1)
-                if c == CHUNKS - 1:
+                if last:
                     nc.sync.dma_start(out=out[rows, t0:t1], in_=res[c][:, t0:t1])
-            if c < CHUNKS - 1:
+            if not last:
                 nc.sync.dma_start(out=out[rows, :], in_=res[c][:])

@@ -14,10 +14,19 @@ BLOCKS = S // P
 WINDOW = 768
 FLOPS = 2 * K * N * T + 2 * S * N * H + 2 * S * H * K
 
-GATHER_CUTS = ((0, 1), (1, 3), (3, 5))
-A_CUTS = ((0, 2), (2, 4), (4, 5))
+GATHER_CUTS = ((0, 3), (3, 7), (7, 10))
+A_CUTS = ((0, 1), (1, 3), (3, 4), (4, 5))
 WB_FIRST = 3
 QUANT_BLOCKS = 4
+LEAD = 2
+POOL_BLOCKS = ()
+LOADS = ("dy", "wb0", "gate", "wbs", "wb1", "a0", "a1", "a2", "a3", "wt", "wa0", "was", "wae", "pos",)
+WB_CUTS = ((0, 3), (3, 5))
+ORDER = ("f00", "f11", "f22", "t03", "f30", "t14", "f41", "t25", "f52", "t36", "f60", "t47", "q0", "f71", "t53", "f82", "t64", "f90", "t75", "t86", "q1", "b01", "c12", "t97", "s00", "s13",)
+GATE_POOL = 0
+WHOLE = 1
+LATER = ((6, 7, 2, 0, 3), (1, 4, 5, 6), (7, 2, 0, 3))
+TAIL_BANKS = (4, 5)
 TOKEN_PIECES = ((0, 384), (384, T))
 
 F32 = mybir.dt.float32
@@ -29,6 +38,7 @@ U8 = mybir.dt.uint8
 FP8X4 = mybir.dt.float8_e4m3fn_x4
 FP4X4 = mybir.dt.float4_e2m1fn_x4
 COPY = mybir.ActivationFunctionType.Copy
+RELU = mybir.ActivationFunctionType.Relu
 ALU = mybir.AluOpType
 
 
@@ -48,7 +58,7 @@ def tile_moe_adb_relu2_kernel(
         wts = keep.tile([P, K], U8, align_bytes=64)
         wtw = keep.tile([P, 2 * K], U8, align_bytes=64)
         base = keep.tile([P, CHUNKS, T], F32)
-        wbw = keep.tile([P, E, H], I32, align_bytes=64)
+        wbw = [keep.tile([P, hi - lo, H], I32, name="wbw%d" % lo, align_bytes=64) for lo, hi in WB_CUTS]
         wbs = keep.tile([P, E, H], U8, align_bytes=64)
         waw = [keep.tile([P, E, K // 2], I32, name="waw%d" % h, align_bytes=64) for h in range(2)]
         was = keep.tile([P, E, K], U8, align_bytes=64)
@@ -57,8 +67,10 @@ def tile_moe_adb_relu2_kernel(
         ident = keep.tile([P, P], F32)
         xw = keep.tile([P, S], U32, align_bytes=64)
         xs = keep.tile([P, S], U8, align_bytes=64)
-        gated = keep.tile([P, BLOCKS, PACK, P], F32)
-        dh = keep.tile([P, S, PACK], BF16, align_bytes=64)
+        gated = [keep.tile([P, H], F32, name="gated%d" % b) for b in range(BLOCKS)]
+        dh = keep.tile([P, S * PACK], BF16, align_bytes=64)
+        relu_rows = {b: keep.tile([P, H], F32, name="relu%d" % b) for b in POOL_BLOCKS}
+        dh_rows = {b: keep.tile([P, H], BF16, name="rows%d" % b, align_bytes=64) for b in POOL_BLOCKS}
         dhw = keep.tile([P, S], U32, align_bytes=64)
         dhs = keep.tile([P, S], U8, align_bytes=64)
         a_sb = [
@@ -66,7 +78,7 @@ def tile_moe_adb_relu2_kernel(
         ]
         dx = [keep.tile([P, S], F32, name="dx%d" % c) for c in range(CHUNKS)]
         part = [keep.tile([P, T], F32, name="part%d" % c) for c in range(CHUNKS)]
-        res = [keep.tile([P, T], F32, name="res%d" % c) for c in range(CHUNKS)]
+        res = {c: keep.tile([P, T], F32, name="res%d" % c) for c in range(CHUNKS)}
 
         nc.gpsimd.memset(dys[:].bitcast(I32), 0)
         nc.vector.memset(dyw[:, T:WINDOW], 0)
@@ -92,59 +104,96 @@ def tile_moe_adb_relu2_kernel(
             lo, hi = A_CUTS[n]
             nc.sync.dma_start(out=a_sb[n][:], in_=a_src[:, :, lo * C : hi * C])
 
-        nc.sync.dma_start(out=dyw[:, 0:T], in_=dy_words[0].rearrange("p t d -> p (t d)").bitcast(I32))
-        load_scales(dys[:, 0:T], dy_scales[0], (nc.scalar, nc.scalar, nc.sync, nc.sync))
-        nc.sync.dma_start(offs_sb[:], offs)
-        nc.sync.dma_start(out=wbw[:, 0:WB_FIRST, :], in_=wb_src[:, 0:WB_FIRST, :])
-        nc.sync.dma_start(out=gate_rows[0:BLOCKS, :], in_=gate[0].rearrange("(b p) -> b p", p=P))
-        load_scales(wbs, wbt_scales.rearrange("e o r n -> r (e o) n"))
-        load_a(0)
-        nc.sync.dma_start(out=wbw[:, WB_FIRST:E, :], in_=wb_src[:, WB_FIRST:E, :])
-        load_a(1)
-        load_a(2)
-        nc.sync.dma_start(out=wtw[:].bitcast(I32), in_=wt_words[0].bitcast(I32))
-        load_scales(wts, wt_scales[0])
-        nc.sync.dma_start(out=waw[0][:], in_=wa_src[:, :, 0 : K // 2])
-        load_scales(was, wat_scales.rearrange("e o r n -> r (e o) n"))
-        nc.sync.dma_start(pos1_sb[:], pos1)
-        nc.sync.dma_start(pos2_sb[:], pos2)
-        nc.sync.dma_start(out=waw[1][:], in_=wa_src[:, :, K // 2 : K])
+        for what in LOADS:
+            if what == "dy":
+                nc.sync.dma_start(out=dyw[:, 0:T], in_=dy_words[0].rearrange("p t d -> p (t d)").bitcast(I32))
+                load_scales(dys[:, 0:T], dy_scales[0], (nc.scalar, nc.scalar, nc.sync, nc.sync))
+                nc.sync.dma_start(offs_sb[:], offs)
+            elif what == "gate":
+                (nc.gpsimd if GATE_POOL else nc.sync).dma_start(out=gate_rows[0:BLOCKS, :], in_=gate[0].rearrange("(b p) -> b p", p=P))
+            elif what == "wbs":
+                load_scales(wbs, wbt_scales.rearrange("e o r n -> r (e o) n"))
+            elif what == "was":
+                load_scales(was, wat_scales.rearrange("e o r n -> r (e o) n"))
+            elif what == "wt":
+                nc.sync.dma_start(out=wtw[:].bitcast(I32), in_=wt_words[0].bitcast(I32))
+                load_scales(wts, wt_scales[0])
+            elif what == "pos":
+                nc.sync.dma_start(pos2_sb[:], pos2)
+                nc.sync.dma_start(pos1_sb[:], pos1)
+            elif what == "wae":
+                for e in range(E):
+                    nc.sync.dma_start(out=waw[1][:, e, :], in_=wa_src[:, e, K // 2 : K])
+            elif what.startswith("wb"):
+                lo, hi = WB_CUTS[int(what[2:])]
+                nc.sync.dma_start(out=wbw[int(what[2:])][:], in_=wb_src[:, lo:hi, :])
+            elif what.startswith("wa"):
+                h = int(what[2:])
+                nc.sync.dma_start(out=waw[h][:], in_=wa_src[:, :, h * K // 2 : (h + 1) * K // 2])
+            else:
+                load_a(int(what[1:]))
 
         banks = [psum.tile([P, BANK], F32, name="bank%d" % n) for n in range(8)]
-        first_banks, base_banks, turn_banks = banks[0:3], banks[3:5], banks[5:8]
 
-        gate_turned = turn_banks[-1]
+
+        gate_turned = banks[7]
         nc.tensor.transpose(gate_turned[:, 0:P], gate_rows[:], ident[:])
         nc.scalar.activation(gate2[:], gate_turned[:, 0:BLOCKS], COPY, scale=2.0)
 
         for lo, hi in GATHER_CUTS:
-            slots = slice(lo * C, hi * C)
-            entries = offs_sb[:, lo * C // PER_COL : hi * C // PER_COL]
+            slots = slice(lo * P, hi * P)
+            entries = offs_sb[:, lo * P // PER_COL : hi * P // PER_COL]
             nc.vector.tensor_copy(xw[:, slots], dyw[:].bitcast(U32).indirect(entries))
             nc.vector.tensor_copy(xs[:, slots], dys[:].indirect(entries))
 
-        def first(b):
+        def first(b, acc):
             e = b * P // C
             slots = slice(b * P, (b + 1) * P)
-            acc = first_banks[b % len(first_banks)]
+            n = [i for i, (lo, hi) in enumerate(WB_CUTS) if lo <= e < hi][0]
             nc.tensor.matmul_mx(
                 out=acc[:], lhsT=xw[:, slots].bitcast(FP8X4), lhsT_scale=xs[:, slots],
-                rhs=wbw[:, e, :].bitcast(FP8X4), rhs_scale=wbs[:, e, :], start=True, stop=True,
+                rhs=wbw[n][:, e - WB_CUTS[n][0], :].bitcast(FP8X4), rhs_scale=wbs[:, e, :], start=True, stop=True,
             )
-            nc.scalar.activation(
-                gated[:, b, :, :], acc[:].rearrange("p (m t) -> p t m", t=PACK), COPY, scale=gate2[:, b : b + 1]
-            )
+            if b in POOL_BLOCKS:
+                dst = gated[b][:].rearrange("s (u m d) -> s u m d", u=2, d=2)
+                src = acc[:].rearrange("s (m u d) -> s u m d", u=2, d=2)
+            else:
+                dst = gated[b][:].rearrange("s (t m) -> s t m", t=PACK)
+                src = acc[:].rearrange("s (m t) -> s t m", t=PACK)
+            nc.scalar.activation(dst, src, COPY, scale=gate2[:, b : b + 1])
 
-        def make_dh(b):
-            turned = turn_banks[b % len(turn_banks)]
-            for t in range(PACK):
-                nc.tensor.transpose(turned[:, t * P : (t + 1) * P], gated[:, b, t, :], ident[:])
+        def a_block(b):
             e = b * P // C
             n = [i for i, (lo, hi) in enumerate(A_CUTS) if lo <= e < hi][0]
             s0 = b * P - A_CUTS[n][0] * C
+            return a_sb[n][:, :, s0 : s0 + P]
+
+        def relu_turned(b, turned):
+            for t in range(PACK):
+                nc.tensor.transpose(turned[:, t * P : (t + 1) * P], a_block(b)[:, t, :], ident[:])
+            nc.scalar.activation(
+                relu_rows[b][:].rearrange("s (u m d) -> s u m d", u=2, d=2),
+                turned[:].rearrange("s (u d m) -> s u m d", u=2, d=2), RELU,
+            )
+
+        def pool_product(b):
+            nc.gpsimd.tensor_tensor(dh_rows[b][:], gated[b][:], relu_rows[b][:], ALU.mult)
+
+        def words_back(b, turned):
+            words = dh_rows[b][:].bitcast(F32)
+            for u in range(2):
+                nc.tensor.transpose(turned[:, u * P : (u + 1) * P], words[:, u * P : (u + 1) * P], ident[:])
+            nc.scalar.copy(
+                dh[:, b * H : (b + 1) * H].bitcast(F32).rearrange("p (s u) -> p s u", u=2),
+                turned[:, 0 : 2 * P].rearrange("p (u s) -> p s u", u=2),
+            )
+
+        def make_dh(b, turned):
+            for t in range(PACK):
+                nc.tensor.transpose(turned[:, t * P : (t + 1) * P], gated[b][:, t * P : (t + 1) * P], ident[:])
             nc.vector.scalar_tensor_tensor(
-                out=dh[:, b * P : (b + 1) * P, :],
-                in0=a_sb[n][:, :, s0 : s0 + P].rearrange("p t s -> p s t"),
+                out=dh[:, b * H : (b + 1) * H].rearrange("p (s t) -> p s t", t=PACK),
+                in0=a_block(b).rearrange("p t s -> p s t"),
                 scalar=0.0,
                 in1=turned[:].rearrange("p (t s) -> p s t", t=PACK),
                 op0=ALU.max,
@@ -153,7 +202,7 @@ def tile_moe_adb_relu2_kernel(
 
         def quantize(lo, hi):
             nc.vector.quantize_mx(
-                out=dhw[:, lo:hi].bitcast(FP8X4), scales=dhs[:, lo:hi], in_=dh[:, lo:hi, :].rearrange("p s t -> p (s t)")
+                out=dhw[:, lo:hi].bitcast(FP8X4), scales=dhs[:, lo:hi], in_=dh[:, lo * PACK : hi * PACK]
             )
 
         def second(c, lo, hi, acc, copy):
@@ -177,47 +226,75 @@ def tile_moe_adb_relu2_kernel(
             base_pass(c, 0, BANK, acc[:])
             nc.scalar.copy(base[:, c, 0:BANK], acc[:])
 
-        def base_tails(acc):
-            for c in range(CHUNKS):
-                base_pass(c, BANK, T, acc[:, c * P : (c + 1) * P])
-            nc.scalar.copy(base[:, :, BANK:T], acc[:].rearrange("p (c t) -> p c t", c=CHUNKS))
+        def base_tails(lo, hi, acc):
+            for c in range(lo, hi):
+                base_pass(c, BANK, T, acc[:, (c - lo) * P : (c - lo + 1) * P])
+            nc.scalar.copy(base[:, lo:hi, BANK:T], acc[:, 0 : (hi - lo) * P].rearrange("p (c t) -> p c t", t=P))
 
-        first(0)
-        for b in range(BLOCKS):
-            if b + 1 < BLOCKS:
-                first(b + 1)
+        for step in ORDER:
+            kind, n, bank = step[0], int(step[1]), banks[int(step[2:] or 0)]
+            if kind == "r":
+                relu_turned(n, bank)
+            elif kind == "f":
+                first(n, bank)
+            elif kind == "m":
+                pool_product(n)
+            elif kind == "t":
+                make_dh(n, bank)
+            elif kind == "w":
+                words_back(n, bank)
+            elif kind == "q":
+                quantize(n * BANK, (n + 1) * BANK)
+            elif kind == "s":
+                second(0, n * BANK, (n + 1) * BANK, bank, nc.scalar.copy)
+            elif kind == "b":
+                base_main(n, bank)
             else:
-                base_main(0, base_banks[0])
-                base_tails(base_banks[1])
-            make_dh(b)
-            if b > 0 and b % QUANT_BLOCKS == 0:
-                quantize((b - QUANT_BLOCKS) * P, b * P)
-
-        second(0, 0, BANK, first_banks[0], nc.scalar.copy)
-        second(0, BANK, 2 * BANK, first_banks[1], nc.scalar.copy)
+                base_tails(0, n, bank)
+                tails_done = n
+        tail_banks = [banks[n] for n in TAIL_BANKS]
         quantize(S - C, S - P)
-        second(0, S - C, S - P, base_banks[1], nc.scalar.copy)
+        second(0, S - C, S - P, tail_banks[0], nc.scalar.copy)
         quantize(S - P, S)
-        second(0, S - P, S, base_banks[0], nc.vector.tensor_copy)
+        second(0, S - P, S, tail_banks[1], nc.vector.tensor_copy)
 
-        later_banks = [base_banks[1], base_banks[0], turn_banks[0]]
         for c in range(1, CHUNKS):
+            later_banks = [banks[n] for n in LATER[c - 1]]
             for acc, lo in zip(later_banks, range(0, S, BANK)):
                 second(c, lo, min(lo + BANK, S), acc, nc.scalar.copy)
-            base_main(c, first_banks[1])
+            base_main(c, later_banks[3])
+            if c == 1 and tails_done < CHUNKS:
+                base_tails(tails_done, CHUNKS, later_banks[4])
 
         def gather_add(dst, c, pos_sb, other, t0, t1):
             entries = pos_sb[:, t0 // PER_COL : t1 // PER_COL]
             nc.vector.tensor_tensor(dst[:, t0:t1], dx[c][:].indirect(entries), other[:, t0:t1], ALU.add)
 
-        for c in range(CHUNKS):
-            rows = slice(c * P, (c + 1) * P)
-            last = c == CHUNKS - 1
+        def store(c, t0, t1):
+            nc.sync.dma_start(out=out[c * P : (c + 1) * P, t0:t1], in_=res[c][:, t0:t1])
+
+        last = CHUNKS - 1
+        if WHOLE:
             for t0, t1 in TOKEN_PIECES:
-                gather_add(part[c], c, pos1_sb, base[:, c, :], t0, t1)
+                gather_add(part[0], 0, pos1_sb, base[:, 0, :], t0, t1)
             for t0, t1 in TOKEN_PIECES:
-                gather_add(res[c], c, pos2_sb, part[c], t0, t1)
-                if last:
-                    nc.sync.dma_start(out=out[rows, t0:t1], in_=res[c][:, t0:t1])
-            if not last:
-                nc.sync.dma_start(out=out[rows, :], in_=res[c][:])
+                gather_add(res[0], 0, pos2_sb, part[0], t0, t1)
+            store(0, 0, T)
+            gather_add(part[1], 1, pos1_sb, base[:, 1, :], 0, T)
+            for c in range(1, last):
+                gather_add(part[c + 1], c + 1, pos1_sb, base[:, c + 1, :], 0, T)
+                gather_add(res[c], c, pos2_sb, part[c], 0, T)
+                store(c, 0, T)
+            for t0, t1 in TOKEN_PIECES:
+                gather_add(res[last], last, pos2_sb, part[last], t0, t1)
+                store(last, t0, t1)
+        else:
+            for c in range(CHUNKS):
+                for t0, t1 in TOKEN_PIECES:
+                    gather_add(part[c], c, pos1_sb, base[:, c, :], t0, t1)
+                for t0, t1 in TOKEN_PIECES:
+                    gather_add(res[c], c, pos2_sb, part[c], t0, t1)
+                    if c == last:
+                        store(c, t0, t1)
+                if c != last:
+                    store(c, 0, T)

@@ -15,16 +15,20 @@ WINDOW = 768
 FLOPS = 2 * K * N * T + 2 * S * N * H + 2 * S * H * K
 
 GATHER_CUTS = ((0, 3), (3, 7), (7, 10))
-A_CUTS = ((0, 1), (1, 3), (3, 4), (4, 5))
+A_CUTS = ((0, 1), (1, 3), (3, 5))
 WB_FIRST = 3
 QUANT_BLOCKS = 4
 LEAD = 2
 POOL_BLOCKS = ()
-LOADS = ("dy", "wb0", "gate", "wbs", "wb1", "a0", "a1", "a2", "a3", "wt", "wa0", "was", "wae", "pos",)
+LOADS = ("dy", "wb0", "gate", "wbs", "wb1", "a0", "a1", "a2", "wt", "wa0", "was", "wae", "pos",)
 WB_CUTS = ((0, 3), (3, 5))
 ORDER = ("f00", "f11", "f22", "t03", "f30", "t14", "f41", "t25", "f52", "t36", "f60", "t47", "q0", "f71", "t53", "f82", "t64", "f90", "t75", "t86", "q1", "b01", "c12", "t97", "s00", "s13",)
 GATE_POOL = 0
 WHOLE = 1
+RFORM = 1
+PACKED = 0
+WBS_ACT = 0
+MEMSETS = ("gate", "wbs", "was", "wts")
 LATER = ((6, 7, 2, 0, 3), (1, 4, 5, 6), (7, 2, 0, 3))
 TAIL_BANKS = (4, 5)
 TOKEN_PIECES = ((0, 384), (384, T))
@@ -59,9 +63,9 @@ def tile_moe_adb_relu2_kernel(
         wtw = keep.tile([P, 2 * K], U8, align_bytes=64)
         base = keep.tile([P, CHUNKS, T], F32)
         wbw = [keep.tile([P, hi - lo, H], I32, name="wbw%d" % lo, align_bytes=64) for lo, hi in WB_CUTS]
-        wbs = keep.tile([P, E, H], U8, align_bytes=64)
+        wbs = keep.tile([P, 2 if PACKED else E, H], U8, align_bytes=64)
         waw = [keep.tile([P, E, K // 2], I32, name="waw%d" % h, align_bytes=64) for h in range(2)]
-        was = keep.tile([P, E, K], U8, align_bytes=64)
+        was = keep.tile([P, 2 if PACKED else E, K], U8, align_bytes=64)
         gate_rows = keep.tile([P, P], F32)
         gate2 = keep.tile([P, BLOCKS], F32)
         ident = keep.tile([P, P], F32)
@@ -82,10 +86,14 @@ def tile_moe_adb_relu2_kernel(
 
         nc.gpsimd.memset(dys[:].bitcast(I32), 0)
         nc.vector.memset(dyw[:, T:WINDOW], 0)
-        nc.vector.memset(gate_rows[:], 0.0)
-        nc.vector.memset(wbs[:].rearrange("p e n -> p (e n)").bitcast(I32), 0)
-        nc.vector.memset(was[:].rearrange("p e n -> p (e n)").bitcast(I32), 0)
-        nc.vector.memset(wts[:].bitcast(I32), 0)
+        zeroed = {
+            "gate": gate_rows[:].bitcast(I32),
+            "wbs": wbs[:].rearrange("p e n -> p (e n)").bitcast(I32),
+            "was": was[:].rearrange("p e n -> p (e n)").bitcast(I32),
+            "wts": wts[:].bitcast(I32),
+        }
+        for what in MEMSETS:
+            nc.vector.memset(zeroed[what], 0)
         make_identity(nc, ident[:])
 
         wb_src = wbt_words.rearrange("e o p n d -> p (e o) (n d)").bitcast(I32)
@@ -95,15 +103,34 @@ def tile_moe_adb_relu2_kernel(
         def load_scales(tile, rows, queues=(nc.sync,) * 4):
             rest = (slice(None),) * (len(rows.shape) - 1)
             for q in range(4):
-                queues[q].dma_start(
-                    out=tile[(slice(32 * q, 32 * q + 4),) + rest].bitcast(I32),
-                    in_=rows[(slice(4 * q, 4 * q + 4),) + rest].bitcast(I32),
+                if RFORM:
+                    queues[q].dma_start(
+                        out=tile[(slice(q, P, 32),) + rest].bitcast(I32),
+                        in_=rows[(slice(q, 16, 4),) + rest].bitcast(I32),
+                    )
+                else:
+                    queues[q].dma_start(
+                        out=tile[(slice(32 * q, 32 * q + 4),) + rest].bitcast(I32),
+                        in_=rows[(slice(4 * q, 4 * q + 4),) + rest].bitcast(I32),
+                    )
+
+        def load_packed(tile, scales, queue):
+            for q in range(4):
+                queue.dma_start(
+                    out=tile[32 * q : 32 * q + 16, 0, :].bitcast(I32),
+                    in_=scales[0:PACK, 0, 4 * q : 4 * q + 4, :].bitcast(I32),
                 )
+
+        def plane(tile, e, cols):
+            if PACKED:
+                return tile[4 * (e % PACK) : P, e // PACK, cols]
+            return tile[:, e, cols]
 
         def load_a(n):
             lo, hi = A_CUTS[n]
             nc.sync.dma_start(out=a_sb[n][:], in_=a_src[:, :, lo * C : hi * C])
 
+        wbs_queue = nc.scalar if WBS_ACT else nc.sync
         for what in LOADS:
             if what == "dy":
                 nc.sync.dma_start(out=dyw[:, 0:T], in_=dy_words[0].rearrange("p t d -> p (t d)").bitcast(I32))
@@ -112,9 +139,17 @@ def tile_moe_adb_relu2_kernel(
             elif what == "gate":
                 (nc.gpsimd if GATE_POOL else nc.sync).dma_start(out=gate_rows[0:BLOCKS, :], in_=gate[0].rearrange("(b p) -> b p", p=P))
             elif what == "wbs":
-                load_scales(wbs, wbt_scales.rearrange("e o r n -> r (e o) n"))
+                load_scales(wbs, wbt_scales.rearrange("e o r n -> r (e o) n"), (wbs_queue,) * 4)
             elif what == "was":
                 load_scales(was, wat_scales.rearrange("e o r n -> r (e o) n"))
+            elif what == "wbp":
+                load_packed(wbs, wbt_scales, wbs_queue)
+            elif what == "wap":
+                load_packed(was, wat_scales, nc.sync)
+            elif what == "wbl":
+                load_scales(wbs[:, 1, :], wbt_scales[PACK, 0])
+            elif what == "wal":
+                load_scales(was[:, 1, :], wat_scales[PACK, 0])
             elif what == "wt":
                 nc.sync.dma_start(out=wtw[:].bitcast(I32), in_=wt_words[0].bitcast(I32))
                 load_scales(wts, wt_scales[0])
@@ -152,7 +187,7 @@ def tile_moe_adb_relu2_kernel(
             n = [i for i, (lo, hi) in enumerate(WB_CUTS) if lo <= e < hi][0]
             nc.tensor.matmul_mx(
                 out=acc[:], lhsT=xw[:, slots].bitcast(FP8X4), lhsT_scale=xs[:, slots],
-                rhs=wbw[n][:, e - WB_CUTS[n][0], :].bitcast(FP8X4), rhs_scale=wbs[:, e, :], start=True, stop=True,
+                rhs=wbw[n][:, e - WB_CUTS[n][0], :].bitcast(FP8X4), rhs_scale=plane(wbs, e, slice(0, H)), start=True, stop=True,
             )
             if b in POOL_BLOCKS:
                 dst = gated[b][:].rearrange("s (u m d) -> s u m d", u=2, d=2)
@@ -211,7 +246,7 @@ def tile_moe_adb_relu2_kernel(
                 e = s0 // C
                 words = waw[c // 2][:, e, c % 2 * P : (c % 2 + 1) * P]
                 nc.tensor.matmul_mx(
-                    out=acc[:, s0 - lo : s1 - lo], lhsT=words.bitcast(FP8X4), lhsT_scale=was[:, e, c * P : (c + 1) * P],
+                    out=acc[:, s0 - lo : s1 - lo], lhsT=words.bitcast(FP8X4), lhsT_scale=plane(was, e, slice(c * P, (c + 1) * P)),
                     rhs=dhw[:, s0:s1].bitcast(FP8X4), rhs_scale=dhs[:, s0:s1], start=True, stop=True,
                 )
             copy(dx[c][:, lo:hi], acc[:, 0 : hi - lo])
@@ -281,10 +316,12 @@ def tile_moe_adb_relu2_kernel(
                 gather_add(res[0], 0, pos2_sb, part[0], t0, t1)
             store(0, 0, T)
             gather_add(part[1], 1, pos1_sb, base[:, 1, :], 0, T)
+            gather_add(part[2], 2, pos1_sb, base[:, 2, :], 0, T)
             for c in range(1, last):
-                gather_add(part[c + 1], c + 1, pos1_sb, base[:, c + 1, :], 0, T)
                 gather_add(res[c], c, pos2_sb, part[c], 0, T)
                 store(c, 0, T)
+            for t0, t1 in TOKEN_PIECES:
+                gather_add(part[last], last, pos1_sb, base[:, last, :], t0, t1)
             for t0, t1 in TOKEN_PIECES:
                 gather_add(res[last], last, pos2_sb, part[last], t0, t1)
                 store(last, t0, t1)

@@ -14,22 +14,24 @@ BLOCKS = S // P
 WINDOW = 768
 FLOPS = 2 * K * N * T + 2 * S * N * H + 2 * S * H * K
 
-GATHER_CUTS = ((0, 3), (3, 7), (7, 10))
-A_CUTS = ((0, 1), (1, 3), (3, 5))
+GATHER_CUTS = ((0, 4), (4, 7), (7, 10))
+A_CUTS = ((0, 3), (3, 6), (6, 10))
 WB_FIRST = 3
 QUANT_BLOCKS = 4
 LEAD = 2
 POOL_BLOCKS = ()
-LOADS = ("dy", "wb0", "gate", "wbs", "wb1", "a0", "a1", "a2", "wt", "wa0", "was", "wae", "pos",)
-WB_CUTS = ((0, 3), (3, 5))
+LOADS = ("dy", "wb0", "gate", "wbs", "wb1", "a0", "a1", "a2", "wt", "wa0", "was", "pos", "wa1",)
+WB_CUTS = ((0, 2), (2, 5))
 ORDER = ("f00", "f11", "f22", "t03", "f30", "t14", "f41", "t25", "f52", "t36", "f60", "t47", "q0", "f71", "t53", "f82", "t64", "f90", "t75", "t86", "q1", "b01", "c12", "t97", "s00", "s13",)
 GATE_POOL = 0
-WHOLE = 1
+WHOLE = 0
+WARM = 4
+WA_CUTS = ((0, 1), (1, 4))
 RFORM = 1
 PACKED = 0
 WBS_ACT = 0
 MEMSETS = ("gate", "wbs", "was", "wts")
-LATER = ((6, 7, 2, 0, 3), (1, 4, 5, 6), (7, 2, 0, 3))
+LATER = ((1, 2, 6, 0, 3), (7, 4, 5, 1), (2, 6, 0, 7))
 TAIL_BANKS = (4, 5)
 TOKEN_PIECES = ((0, 384), (384, T))
 
@@ -64,7 +66,7 @@ def tile_moe_adb_relu2_kernel(
         base = keep.tile([P, CHUNKS, T], F32)
         wbw = [keep.tile([P, hi - lo, H], I32, name="wbw%d" % lo, align_bytes=64) for lo, hi in WB_CUTS]
         wbs = keep.tile([P, 2 if PACKED else E, H], U8, align_bytes=64)
-        waw = [keep.tile([P, E, K // 2], I32, name="waw%d" % h, align_bytes=64) for h in range(2)]
+        waw = [keep.tile([P, E, (hi - lo) * P], I32, name="waw%d" % lo, align_bytes=64) for lo, hi in WA_CUTS]
         was = keep.tile([P, 2 if PACKED else E, K], U8, align_bytes=64)
         gate_rows = keep.tile([P, P], F32)
         gate2 = keep.tile([P, BLOCKS], F32)
@@ -78,7 +80,7 @@ def tile_moe_adb_relu2_kernel(
         dhw = keep.tile([P, S], U32, align_bytes=64)
         dhs = keep.tile([P, S], U8, align_bytes=64)
         a_sb = [
-            keep.tile([P, PACK, (hi - lo) * C], F32, name="a%d" % lo, align_bytes=64) for lo, hi in A_CUTS
+            keep.tile([P, PACK, (hi - lo) * P], F32, name="a%d" % lo, align_bytes=64) for lo, hi in A_CUTS
         ]
         dx = [keep.tile([P, S], F32, name="dx%d" % c) for c in range(CHUNKS)]
         part = [keep.tile([P, T], F32, name="part%d" % c) for c in range(CHUNKS)]
@@ -128,7 +130,7 @@ def tile_moe_adb_relu2_kernel(
 
         def load_a(n):
             lo, hi = A_CUTS[n]
-            nc.sync.dma_start(out=a_sb[n][:], in_=a_src[:, :, lo * C : hi * C])
+            nc.sync.dma_start(out=a_sb[n][:], in_=a_src[:, :, lo * P : hi * P])
 
         wbs_queue = nc.scalar if WBS_ACT else nc.sync
         for what in LOADS:
@@ -158,13 +160,13 @@ def tile_moe_adb_relu2_kernel(
                 nc.sync.dma_start(pos1_sb[:], pos1)
             elif what == "wae":
                 for e in range(E):
-                    nc.sync.dma_start(out=waw[1][:, e, :], in_=wa_src[:, e, K // 2 : K])
+                    nc.sync.dma_start(out=waw[1][:, e, :], in_=wa_src[:, e, WA_CUTS[1][0] * P : K])
             elif what.startswith("wb"):
                 lo, hi = WB_CUTS[int(what[2:])]
                 nc.sync.dma_start(out=wbw[int(what[2:])][:], in_=wb_src[:, lo:hi, :])
             elif what.startswith("wa"):
                 h = int(what[2:])
-                nc.sync.dma_start(out=waw[h][:], in_=wa_src[:, :, h * K // 2 : (h + 1) * K // 2])
+                nc.sync.dma_start(out=waw[h][:], in_=wa_src[:, :, WA_CUTS[h][0] * P : WA_CUTS[h][1] * P])
             else:
                 load_a(int(what[1:]))
 
@@ -174,6 +176,12 @@ def tile_moe_adb_relu2_kernel(
         gate_turned = banks[7]
         nc.tensor.transpose(gate_turned[:, 0:P], gate_rows[:], ident[:])
         nc.scalar.activation(gate2[:], gate_turned[:, 0:BLOCKS], COPY, scale=2.0)
+
+        for n in range(WARM):
+            nc.tensor.matmul_mx(
+                out=banks[3][:], lhsT=dyw[:, 0:P].bitcast(FP8X4), lhsT_scale=dys[:, 0:P],
+                rhs=dyw[:, 0:BANK].bitcast(FP8X4), rhs_scale=dys[:, 0:BANK], start=True, stop=True,
+            )
 
         for lo, hi in GATHER_CUTS:
             slots = slice(lo * P, hi * P)
@@ -198,9 +206,8 @@ def tile_moe_adb_relu2_kernel(
             nc.scalar.activation(dst, src, COPY, scale=gate2[:, b : b + 1])
 
         def a_block(b):
-            e = b * P // C
-            n = [i for i, (lo, hi) in enumerate(A_CUTS) if lo <= e < hi][0]
-            s0 = b * P - A_CUTS[n][0] * C
+            n = [i for i, (lo, hi) in enumerate(A_CUTS) if lo <= b < hi][0]
+            s0 = (b - A_CUTS[n][0]) * P
             return a_sb[n][:, :, s0 : s0 + P]
 
         def relu_turned(b, turned):
@@ -244,7 +251,8 @@ def tile_moe_adb_relu2_kernel(
             for s0 in range(lo, hi, C):
                 s1 = min(s0 + C, hi)
                 e = s0 // C
-                words = waw[c // 2][:, e, c % 2 * P : (c % 2 + 1) * P]
+                n = [i for i, (c0, c1) in enumerate(WA_CUTS) if c0 <= c < c1][0]
+                words = waw[n][:, e, (c - WA_CUTS[n][0]) * P : (c - WA_CUTS[n][0] + 1) * P]
                 nc.tensor.matmul_mx(
                     out=acc[:, s0 - lo : s1 - lo], lhsT=words.bitcast(FP8X4), lhsT_scale=plane(was, e, slice(c * P, (c + 1) * P)),
                     rhs=dhw[:, s0:s1].bitcast(FP8X4), rhs_scale=dhs[:, s0:s1], start=True, stop=True,

@@ -15,14 +15,14 @@ WINDOW = 768
 FLOPS = 2 * K * N * T + 2 * S * N * H + 2 * S * H * K
 
 GATHER_CUTS = ((0, 4), (4, 7), (7, 10))
-A_CUTS = ((0, 3), (3, 6), (6, 10))
+A_CUTS = ((0, 2), (2, 5), (5, 7), (7, 10))
 WB_FIRST = 3
 QUANT_BLOCKS = 4
 LEAD = 2
-POOL_BLOCKS = ()
-LOADS = ("dy", "wb0", "gate", "wbs", "wb1", "a0", "a1", "a2", "wt", "wa0", "was", "pos", "wa1",)
+POOL_BLOCKS = (0,)
+LOADS = ("dy", "wb0", "gate", "wbs", "a0", "wb1", "a1", "a2", "a3", "wt", "wa0", "was", "pos", "wa1",)
 WB_CUTS = ((0, 2), (2, 5))
-ORDER = ("f00", "f11", "f22", "t03", "f30", "t14", "f41", "t25", "f52", "t36", "f60", "t47", "q0", "f71", "t53", "f82", "t64", "f90", "t75", "t86", "q1", "b01", "c12", "t97", "s00", "s13",)
+ORDER = ("f00", "f11", "f22", "f30", "t13", "r07", "m0", "f41", "t24", "f52", "t35", "f60", "t46", "w07", "f71", "t53", "q0", "f82", "t64", "f90", "t75", "t86", "q1", "b01", "c12", "t97", "s00", "s13",)
 GATE_POOL = 0
 WHOLE = 0
 WARM = 4

@@ -14,24 +14,26 @@ BLOCKS = S // P
 WINDOW = 768
 FLOPS = 2 * K * N * T + 2 * S * N * H + 2 * S * H * K
 
-GATHER_CUTS = ((0, 4), (4, 7), (7, 10))
+GATHER_CUTS = ((0, 3), (3, 6), (6, 10))
 A_CUTS = ((0, 2), (2, 5), (5, 7), (7, 10))
 WB_FIRST = 3
 QUANT_BLOCKS = 4
 LEAD = 2
 POOL_BLOCKS = (0,)
 LOADS = ("dy", "wb0", "gate", "wbs", "a0", "wb1", "a1", "a2", "a3", "wt", "wa0", "was", "pos", "wa1",)
-WB_CUTS = ((0, 2), (2, 5))
+WB_CUTS = ((0, 3), (3, 5))
 ORDER = ("f00", "f11", "f22", "f30", "t13", "r07", "m0", "f41", "t24", "f52", "t35", "f60", "t46", "w07", "f71", "t53", "q0", "f82", "t64", "f90", "t75", "t86", "q1", "b01", "c12", "t97", "s00", "s13",)
 GATE_POOL = 0
 WHOLE = 0
+PAIR = 1
+RELU_BLOCKS = ()
 WARM = 4
 WA_CUTS = ((0, 1), (1, 4))
 RFORM = 1
 PACKED = 0
 WBS_ACT = 0
 MEMSETS = ("gate", "wbs", "was", "wts")
-LATER = ((1, 2, 6, 0, 3), (7, 4, 5, 1), (2, 6, 0, 7))
+LATER = ((1, 2, 6, 0, 3), (7, 5, 6, 1), (4, 0, 3, 2))
 TAIL_BANKS = (4, 5)
 TOKEN_PIECES = ((0, 384), (384, T))
 
@@ -76,6 +78,7 @@ def tile_moe_adb_relu2_kernel(
         gated = [keep.tile([P, H], F32, name="gated%d" % b) for b in range(BLOCKS)]
         dh = keep.tile([P, S * PACK], BF16, align_bytes=64)
         relu_rows = {b: keep.tile([P, H], F32, name="relu%d" % b) for b in POOL_BLOCKS}
+        relu_woven = {b: keep.tile([P, H], F32, name="woven%d" % b) for b in RELU_BLOCKS}
         dh_rows = {b: keep.tile([P, H], BF16, name="rows%d" % b, align_bytes=64) for b in POOL_BLOCKS}
         dhw = keep.tile([P, S], U32, align_bytes=64)
         dhs = keep.tile([P, S], U8, align_bytes=64)
@@ -233,6 +236,14 @@ def tile_moe_adb_relu2_kernel(
         def make_dh(b, turned):
             for t in range(PACK):
                 nc.tensor.transpose(turned[:, t * P : (t + 1) * P], gated[b][:, t * P : (t + 1) * P], ident[:])
+            if b in RELU_BLOCKS:
+                woven = relu_woven[b][:].rearrange("p (s t) -> p s t", t=PACK)
+                nc.scalar.activation(woven, a_block(b).rearrange("p t s -> p s t"), RELU)
+                nc.vector.tensor_tensor(
+                    dh[:, b * H : (b + 1) * H].rearrange("p (s t) -> p s t", t=PACK), woven,
+                    turned[:].rearrange("p (t s) -> p s t", t=PACK), ALU.mult,
+                )
+                return
             nc.vector.scalar_tensor_tensor(
                 out=dh[:, b * H : (b + 1) * H].rearrange("p (s t) -> p s t", t=PACK),
                 in0=a_block(b).rearrange("p t s -> p s t"),
@@ -274,6 +285,7 @@ def tile_moe_adb_relu2_kernel(
                 base_pass(c, BANK, T, acc[:, (c - lo) * P : (c - lo + 1) * P])
             nc.scalar.copy(base[:, lo:hi, BANK:T], acc[:, 0 : (hi - lo) * P].rearrange("p (c t) -> p c t", t=P))
 
+        mains_done = []
         for step in ORDER:
             kind, n, bank = step[0], int(step[1]), banks[int(step[2:] or 0)]
             if kind == "r":
@@ -292,6 +304,7 @@ def tile_moe_adb_relu2_kernel(
                 second(0, n * BANK, (n + 1) * BANK, bank, nc.scalar.copy)
             elif kind == "b":
                 base_main(n, bank)
+                mains_done.append(n)
             else:
                 base_tails(0, n, bank)
                 tails_done = n
@@ -301,13 +314,21 @@ def tile_moe_adb_relu2_kernel(
         quantize(S - P, S)
         second(0, S - P, S, tail_banks[1], nc.vector.tensor_copy)
 
-        for c in range(1, CHUNKS):
+        for c in range(1, 2 if PAIR else CHUNKS):
             later_banks = [banks[n] for n in LATER[c - 1]]
             for acc, lo in zip(later_banks, range(0, S, BANK)):
                 second(c, lo, min(lo + BANK, S), acc, nc.scalar.copy)
-            base_main(c, later_banks[3])
+            if c not in mains_done:
+                base_main(c, later_banks[3])
             if c == 1 and tails_done < CHUNKS:
                 base_tails(tails_done, CHUNKS, later_banks[4])
+
+        if PAIR:
+            for c in (2, 3):
+                base_main(c, banks[LATER[c - 1][3]])
+            for n, lo in enumerate(range(0, S, BANK)):
+                for c in (2, 3):
+                    second(c, lo, min(lo + BANK, S), banks[LATER[c - 1][n]], nc.scalar.copy)
 
         def gather_add(dst, c, pos_sb, other, t0, t1):
             entries = pos_sb[:, t0 // PER_COL : t1 // PER_COL]
@@ -317,7 +338,21 @@ def tile_moe_adb_relu2_kernel(
             nc.sync.dma_start(out=out[c * P : (c + 1) * P, t0:t1], in_=res[c][:, t0:t1])
 
         last = CHUNKS - 1
-        if WHOLE:
+        if PAIR:
+            for c in (0, 1):
+                for t0, t1 in TOKEN_PIECES:
+                    gather_add(part[c], c, pos1_sb, base[:, c, :], t0, t1)
+                for t0, t1 in TOKEN_PIECES:
+                    gather_add(res[c], c, pos2_sb, part[c], t0, t1)
+                store(c, 0, T)
+            for c in (2, 3):
+                gather_add(part[c], c, pos1_sb, base[:, c, :], 0, T)
+            gather_add(res[2], 2, pos2_sb, part[2], 0, T)
+            store(2, 0, T)
+            for t0, t1 in TOKEN_PIECES:
+                gather_add(res[3], 3, pos2_sb, part[3], t0, t1)
+                store(3, t0, t1)
+        elif WHOLE:
             for t0, t1 in TOKEN_PIECES:
                 gather_add(part[0], 0, pos1_sb, base[:, 0, :], t0, t1)
             for t0, t1 in TOKEN_PIECES:

@@ -22,11 +22,15 @@ LEAD = 2
 POOL_BLOCKS = (0,)
 LOADS = ("dy", "wb0", "gate", "wbs", "a0", "wb1", "a1", "a2", "a3", "wt", "wa0", "was", "pos", "wa1",)
 WB_CUTS = ((0, 3), (3, 5))
-ORDER = ("f00", "f11", "f22", "f30", "t13", "r07", "m0", "f41", "t24", "f52", "t35", "f60", "t46", "w07", "f71", "t53", "q0", "f82", "t64", "f90", "t75", "t86", "q1", "b01", "c12", "t97", "s00", "s13",)
+ORDER = ("f00", "f11", "f22", "f30", "t13", "r07", "m0", "f41", "t24", "f52", "t35", "f60", "t46", "w07", "f71", "t53", "q0", "v8", "f82", "t64", "f90", "t75", "u9", "t86", "h22", "q1", "b01", "c12", "t97", "s00", "s13",)
 GATE_POOL = 0
 WHOLE = 0
+WEAVE_BLOCKS = (8,)
+WEAVE_OVER = (8,)
+LAST_PIECES = ((0, 448), (448, T))
+LAST_ACT = 1
 PAIR = 1
-RELU_BLOCKS = ()
+RELU_BLOCKS = (9,)
 WARM = 4
 WA_CUTS = ((0, 1), (1, 4))
 RFORM = 1
@@ -78,7 +82,9 @@ def tile_moe_adb_relu2_kernel(
         gated = [keep.tile([P, H], F32, name="gated%d" % b) for b in range(BLOCKS)]
         dh = keep.tile([P, S * PACK], BF16, align_bytes=64)
         relu_rows = {b: keep.tile([P, H], F32, name="relu%d" % b) for b in POOL_BLOCKS}
-        relu_woven = {b: keep.tile([P, H], F32, name="woven%d" % b) for b in RELU_BLOCKS}
+        relu_woven = {b: keep.tile([P, H], F32, name="woven%d" % b)[:] for b in RELU_BLOCKS + WEAVE_BLOCKS if b not in WEAVE_OVER}
+        for b in WEAVE_OVER:
+            relu_woven[b] = dh[:, 0 : 2 * H].bitcast(F32)
         dh_rows = {b: keep.tile([P, H], BF16, name="rows%d" % b, align_bytes=64) for b in POOL_BLOCKS}
         dhw = keep.tile([P, S], U32, align_bytes=64)
         dhs = keep.tile([P, S], U8, align_bytes=64)
@@ -180,11 +186,14 @@ def tile_moe_adb_relu2_kernel(
         nc.tensor.transpose(gate_turned[:, 0:P], gate_rows[:], ident[:])
         nc.scalar.activation(gate2[:], gate_turned[:, 0:BLOCKS], COPY, scale=2.0)
 
-        for n in range(WARM):
+        def warm(acc):
             nc.tensor.matmul_mx(
-                out=banks[3][:], lhsT=dyw[:, 0:P].bitcast(FP8X4), lhsT_scale=dys[:, 0:P],
+                out=acc[:], lhsT=dyw[:, 0:P].bitcast(FP8X4), lhsT_scale=dys[:, 0:P],
                 rhs=dyw[:, 0:BANK].bitcast(FP8X4), rhs_scale=dys[:, 0:BANK], start=True, stop=True,
             )
+
+        for n in range(WARM):
+            warm(banks[3])
 
         for lo, hi in GATHER_CUTS:
             slots = slice(lo * P, hi * P)
@@ -221,6 +230,14 @@ def tile_moe_adb_relu2_kernel(
                 turned[:].rearrange("s (u d m) -> s u m d", u=2, d=2), RELU,
             )
 
+        def weave(b):
+            woven = relu_woven[b].rearrange("p (s t) -> p s t", t=PACK)
+            nc.scalar.activation(woven, a_block(b).rearrange("p t s -> p s t"), RELU)
+
+        def pool_weave(b):
+            woven = relu_woven[b].rearrange("p (s t) -> p s t", t=PACK)
+            nc.gpsimd.tensor_scalar(woven, a_block(b).rearrange("p t s -> p s t"), 1.0, 0.0, ALU.mult, ALU.add)
+
         def pool_product(b):
             nc.gpsimd.tensor_tensor(dh_rows[b][:], gated[b][:], relu_rows[b][:], ALU.mult)
 
@@ -237,8 +254,7 @@ def tile_moe_adb_relu2_kernel(
             for t in range(PACK):
                 nc.tensor.transpose(turned[:, t * P : (t + 1) * P], gated[b][:, t * P : (t + 1) * P], ident[:])
             if b in RELU_BLOCKS:
-                woven = relu_woven[b][:].rearrange("p (s t) -> p s t", t=PACK)
-                nc.scalar.activation(woven, a_block(b).rearrange("p t s -> p s t"), RELU)
+                woven = relu_woven[b].rearrange("p (s t) -> p s t", t=PACK)
                 nc.vector.tensor_tensor(
                     dh[:, b * H : (b + 1) * H].rearrange("p (s t) -> p s t", t=PACK), woven,
                     turned[:].rearrange("p (t s) -> p s t", t=PACK), ALU.mult,
@@ -246,7 +262,7 @@ def tile_moe_adb_relu2_kernel(
                 return
             nc.vector.scalar_tensor_tensor(
                 out=dh[:, b * H : (b + 1) * H].rearrange("p (s t) -> p s t", t=PACK),
-                in0=a_block(b).rearrange("p t s -> p s t"),
+                in0=relu_woven[b].rearrange("p (s t) -> p s t", t=PACK) if b in WEAVE_BLOCKS else a_block(b).rearrange("p t s -> p s t"),
                 scalar=0.0,
                 in1=turned[:].rearrange("p (t s) -> p s t", t=PACK),
                 op0=ALU.max,
@@ -292,6 +308,13 @@ def tile_moe_adb_relu2_kernel(
                 relu_turned(n, bank)
             elif kind == "f":
                 first(n, bank)
+            elif kind == "u":
+                weave(n)
+            elif kind == "h":
+                for i in range(n):
+                    warm(bank)
+            elif kind == "v":
+                pool_weave(n)
             elif kind == "m":
                 pool_product(n)
             elif kind == "t":
@@ -312,7 +335,7 @@ def tile_moe_adb_relu2_kernel(
         quantize(S - C, S - P)
         second(0, S - C, S - P, tail_banks[0], nc.scalar.copy)
         quantize(S - P, S)
-        second(0, S - P, S, tail_banks[1], nc.vector.tensor_copy)
+        second(0, S - P, S, tail_banks[1], nc.scalar.copy if LAST_ACT else nc.vector.tensor_copy)
 
         for c in range(1, 2 if PAIR else CHUNKS):
             later_banks = [banks[n] for n in LATER[c - 1]]
@@ -349,7 +372,7 @@ def tile_moe_adb_relu2_kernel(
                 gather_add(part[c], c, pos1_sb, base[:, c, :], 0, T)
             gather_add(res[2], 2, pos2_sb, part[2], 0, T)
             store(2, 0, T)
-            for t0, t1 in TOKEN_PIECES:
+            for t0, t1 in LAST_PIECES:
                 gather_add(res[3], 3, pos2_sb, part[3], t0, t1)
                 store(3, t0, t1)
         elif WHOLE:

@@ -22,11 +22,11 @@ LEAD = 2
 POOL_BLOCKS = (0,)
 LOADS = ("dy", "wb0", "gate", "wbs", "a0", "wb1", "a1", "a2", "a3", "wt", "wa0", "was", "pos", "wa1",)
 WB_CUTS = ((0, 3), (3, 5))
-ORDER = ("f00", "f11", "f22", "f30", "t13", "r07", "m0", "f41", "t24", "f52", "t35", "f60", "t46", "w07", "f71", "t53", "q0", "v8", "f82", "t64", "f90", "t75", "u9", "t86", "h22", "q1", "b01", "c12", "t97", "s00", "s13",)
+ORDER = ("f00", "f11", "f22", "f30", "t13", "r07", "m0", "f41", "t24", "f52", "t35", "f60", "t46", "w07", "f71", "t53", "q0", "f82", "t64", "f90", "t75", "u9", "t86", "h22", "q1", "b01", "c12", "t97", "s00", "s13",)
 GATE_POOL = 0
 WHOLE = 0
-WEAVE_BLOCKS = (8,)
-WEAVE_OVER = (8,)
+WEAVE_BLOCKS = ()
+WEAVE_OVER = ()
 LAST_PIECES = ((0, 448), (448, T))
 LAST_ACT = 1
 PAIR = 1

@@ -20,9 +20,9 @@ WB_FIRST = 3
 QUANT_BLOCKS = 4
 LEAD = 2
 POOL_BLOCKS = (0,)
-LOADS = ("dy", "wb0", "gate", "wbs", "a0", "wb1", "a1", "a2", "a3", "wt", "wa0", "was", "pos", "wa1",)
-WB_CUTS = ((0, 3), (3, 5))
-ORDER = ("f00", "f11", "f22", "f30", "t13", "r07", "m0", "f41", "t24", "f52", "t35", "f60", "t46", "w07", "f71", "t53", "q0", "f82", "t64", "f90", "t75", "u9", "t86", "h22", "q1", "b01", "c12", "t97", "s00", "s13",)
+LOADS = ("dy", "wb0", "gate", "wbs0", "a0", "wb1", "wb2", "a1", "wb3", "a2", "wts", "a3", "wt0", "was0", "wa0", "wa1", "pos1", "wa2", "pos2", "wa3",)
+WB_CUTS = ((0, 2), (2, 3), (3, 4), (4, 5))
+ORDER = "f0.0 f1.1 f2.2 f3.0 t1.3 r0.7 m0 f4.1 t2.4 f5.2 t3.5 f6.0 t4.6 w0.7 f7.1 t5.3 q0.4 f8.2 t6.4 f9.0 t7.5 u9 t8.6 h2.2 q4.8 b0.1 c0.1.2 t9.7 s0.0.4.0 q8.9 q9.10 s0.4.8.3.v s0.8.9.4 s0.9.10.5 s1.0.4.1 s1.4.8.2 s1.8.10.6 b1.0 c1.4.3 b2.1 b3.2 s2.0.4.7 s3.0.4.4 s2.4.8.5 s3.4.8.0 s2.8.10.6 s3.8.10.3"
 GATE_POOL = 0
 WHOLE = 0
 WEAVE_BLOCKS = ()
@@ -32,11 +32,25 @@ LAST_ACT = 1
 PAIR = 1
 RELU_BLOCKS = (9,)
 WARM = 4
-WA_CUTS = ((0, 1), (1, 4))
+SPLIT_X = 0
+SPLIT_Q = 0
+Q_CUTS = ((0, 4), (4, 8), (8, 9), (9, 10))
+CUT = 0
+GATE_BANK = 7
+CLOCK = ()
+PROBE = 1280
+DYS_VEC = 1
+POOL_MEMSETS = ()
+WA_CUTS = ((0, 1, 0, 2), (0, 1, 2, 5), (1, 2, 0, 5), (2, 4, 0, 5))
 RFORM = 1
 PACKED = 0
 WBS_ACT = 0
-MEMSETS = ("gate", "wbs", "was", "wts")
+MEMSETS = ("gate", "wbs0", "was0", "wts")
+WBS_CUTS = ((0, 5),)
+ACT_LOADS = ()
+POOL_LOADS = ()
+WAS_CUTS = ((0, 4),)
+WT_CUTS = ((0, 4),)
 LATER = ((1, 2, 6, 0, 3), (7, 5, 6, 1), (4, 0, 3, 2))
 TAIL_BANKS = (4, 5)
 TOKEN_PIECES = ((0, 384), (384, T))
@@ -68,17 +82,19 @@ def tile_moe_adb_relu2_kernel(
         dyw = keep.tile([P, WINDOW], I32, align_bytes=64)
         dys = keep.tile([P, WINDOW], U8, align_bytes=64)
         wts = keep.tile([P, K], U8, align_bytes=64)
-        wtw = keep.tile([P, 2 * K], U8, align_bytes=64)
+        wtw = [keep.tile([P, 2 * (hi - lo) * P], U8, name="wtw%d" % lo, align_bytes=64) for lo, hi in WT_CUTS]
         base = keep.tile([P, CHUNKS, T], F32)
         wbw = [keep.tile([P, hi - lo, H], I32, name="wbw%d" % lo, align_bytes=64) for lo, hi in WB_CUTS]
-        wbs = keep.tile([P, 2 if PACKED else E, H], U8, align_bytes=64)
-        waw = [keep.tile([P, E, (hi - lo) * P], I32, name="waw%d" % lo, align_bytes=64) for lo, hi in WA_CUTS]
-        was = keep.tile([P, 2 if PACKED else E, K], U8, align_bytes=64)
+        wbs = [keep.tile([P, hi - lo, H], U8, name="wbs%d" % lo, align_bytes=64) for lo, hi in WBS_CUTS]
+        waw = [keep.tile([P, e1 - e0, (hi - lo) * P], I32, name="waw%d_%d" % (lo, e0), align_bytes=64) for lo, hi, e0, e1 in WA_CUTS]
+        was = [keep.tile([P, E, (hi - lo) * P], U8, name="was%d" % lo, align_bytes=64) for lo, hi in WAS_CUTS]
         gate_rows = keep.tile([P, P], F32)
         gate2 = keep.tile([P, BLOCKS], F32)
         ident = keep.tile([P, P], F32)
-        xw = keep.tile([P, S], U32, align_bytes=64)
-        xs = keep.tile([P, S], U8, align_bytes=64)
+        x_cuts = GATHER_CUTS if SPLIT_X else ((0, BLOCKS),)
+        q_cuts = Q_CUTS if SPLIT_Q else ((0, BLOCKS),)
+        xw = [keep.tile([P, (hi - lo) * P], U32, name="xw%d" % lo, align_bytes=64) for lo, hi in x_cuts]
+        xs = [keep.tile([P, (hi - lo) * P], U8, name="xs%d" % lo, align_bytes=64) for lo, hi in x_cuts]
         gated = [keep.tile([P, H], F32, name="gated%d" % b) for b in range(BLOCKS)]
         dh = keep.tile([P, S * PACK], BF16, align_bytes=64)
         relu_rows = {b: keep.tile([P, H], F32, name="relu%d" % b) for b in POOL_BLOCKS}
@@ -86,8 +102,13 @@ def tile_moe_adb_relu2_kernel(
         for b in WEAVE_OVER:
             relu_woven[b] = dh[:, 0 : 2 * H].bitcast(F32)
         dh_rows = {b: keep.tile([P, H], BF16, name="rows%d" % b, align_bytes=64) for b in POOL_BLOCKS}
-        dhw = keep.tile([P, S], U32, align_bytes=64)
-        dhs = keep.tile([P, S], U8, align_bytes=64)
+        dhw = [keep.tile([P, (hi - lo) * P], U32, name="dhw%d" % lo, align_bytes=64) for lo, hi in q_cuts]
+        dhs = [keep.tile([P, (hi - lo) * P], U8, name="dhs%d" % lo, align_bytes=64) for lo, hi in q_cuts]
+
+        def piece(tiles, cuts, lo, hi):
+            n = [i for i, (b0, b1) in enumerate(cuts) if b0 * P <= lo and hi <= b1 * P][0]
+            return tiles[n][:, lo - cuts[n][0] * P : hi - cuts[n][0] * P]
+
         a_sb = [
             keep.tile([P, PACK, (hi - lo) * P], F32, name="a%d" % lo, align_bytes=64) for lo, hi in A_CUTS
         ]
@@ -95,16 +116,18 @@ def tile_moe_adb_relu2_kernel(
         part = [keep.tile([P, T], F32, name="part%d" % c) for c in range(CHUNKS)]
         res = {c: keep.tile([P, T], F32, name="res%d" % c) for c in range(CHUNKS)}
 
-        nc.gpsimd.memset(dys[:].bitcast(I32), 0)
+        (nc.vector if DYS_VEC else nc.gpsimd).memset(dys[:].bitcast(I32), 0)
         nc.vector.memset(dyw[:, T:WINDOW], 0)
         zeroed = {
             "gate": gate_rows[:].bitcast(I32),
-            "wbs": wbs[:].rearrange("p e n -> p (e n)").bitcast(I32),
-            "was": was[:].rearrange("p e n -> p (e n)").bitcast(I32),
             "wts": wts[:].bitcast(I32),
         }
+        for n in range(len(WBS_CUTS)):
+            zeroed["wbs%d" % n] = wbs[n][:].rearrange("p e n -> p (e n)").bitcast(I32)
+        for n in range(len(WAS_CUTS)):
+            zeroed["was%d" % n] = was[n][:].rearrange("p e n -> p (e n)").bitcast(I32)
         for what in MEMSETS:
-            nc.vector.memset(zeroed[what], 0)
+            (nc.gpsimd if what in POOL_MEMSETS else nc.vector).memset(zeroed[what], 0)
         make_identity(nc, ident[:])
 
         wb_src = wbt_words.rearrange("e o p n d -> p (e o) (n d)").bitcast(I32)
@@ -141,50 +164,52 @@ def tile_moe_adb_relu2_kernel(
             lo, hi = A_CUTS[n]
             nc.sync.dma_start(out=a_sb[n][:], in_=a_src[:, :, lo * P : hi * P])
 
-        wbs_queue = nc.scalar if WBS_ACT else nc.sync
+        def queue_of(what):
+            return nc.gpsimd if what in POOL_LOADS else nc.scalar if what in ACT_LOADS else nc.sync
+
         for what in LOADS:
             if what == "dy":
                 nc.sync.dma_start(out=dyw[:, 0:T], in_=dy_words[0].rearrange("p t d -> p (t d)").bitcast(I32))
                 load_scales(dys[:, 0:T], dy_scales[0], (nc.scalar, nc.scalar, nc.sync, nc.sync))
                 nc.sync.dma_start(offs_sb[:], offs)
             elif what == "gate":
-                (nc.gpsimd if GATE_POOL else nc.sync).dma_start(out=gate_rows[0:BLOCKS, :], in_=gate[0].rearrange("(b p) -> b p", p=P))
-            elif what == "wbs":
-                load_scales(wbs, wbt_scales.rearrange("e o r n -> r (e o) n"), (wbs_queue,) * 4)
-            elif what == "was":
-                load_scales(was, wat_scales.rearrange("e o r n -> r (e o) n"))
-            elif what == "wbp":
-                load_packed(wbs, wbt_scales, wbs_queue)
-            elif what == "wap":
-                load_packed(was, wat_scales, nc.sync)
-            elif what == "wbl":
-                load_scales(wbs[:, 1, :], wbt_scales[PACK, 0])
-            elif what == "wal":
-                load_scales(was[:, 1, :], wat_scales[PACK, 0])
-            elif what == "wt":
-                nc.sync.dma_start(out=wtw[:].bitcast(I32), in_=wt_words[0].bitcast(I32))
-                load_scales(wts, wt_scales[0])
-            elif what == "pos":
-                nc.sync.dma_start(pos2_sb[:], pos2)
+                rows = gate[0].rearrange("(b p) -> b p", p=P)
+                if GATE_POOL == 2:
+                    nc.scalar.dma_start(out=gate_rows[0:BLOCKS, :], in_=rows)
+                elif GATE_POOL == 3:
+                    nc.sync.dma_start(out=gate_rows[0:8, :], in_=rows[0:8, :])
+                    nc.sync.dma_start(out=gate_rows[8:BLOCKS, :], in_=rows[8:BLOCKS, :])
+                else:
+                    (nc.gpsimd if GATE_POOL else nc.sync).dma_start(out=gate_rows[0:BLOCKS, :], in_=rows)
+            elif what.startswith("wbs"):
+                lo, hi = WBS_CUTS[int(what[3:])]
+                load_scales(wbs[int(what[3:])], wbt_scales.rearrange("e o r n -> r (e o) n")[:, lo:hi, :], (queue_of(what),) * 4)
+            elif what.startswith("was"):
+                lo, hi = WAS_CUTS[int(what[3:])]
+                load_scales(was[int(what[3:])], wat_scales.rearrange("e o r n -> r (e o) n")[:, :, lo * P : hi * P], (queue_of(what),) * 4)
+            elif what == "wts":
+                load_scales(wts, wt_scales[0], (queue_of(what),) * 4)
+            elif what.startswith("wt"):
+                lo, hi = WT_CUTS[int(what[2:])]
+                nc.sync.dma_start(out=wtw[int(what[2:])][:].bitcast(I32), in_=wt_words[0][:, 2 * lo * P : 2 * hi * P].bitcast(I32))
+            elif what == "pos1":
                 nc.sync.dma_start(pos1_sb[:], pos1)
-            elif what == "wae":
-                for e in range(E):
-                    nc.sync.dma_start(out=waw[1][:, e, :], in_=wa_src[:, e, WA_CUTS[1][0] * P : K])
+            elif what == "pos2":
+                nc.sync.dma_start(pos2_sb[:], pos2)
+            elif what == "probe":
+                probe = keep.tile([P, PROBE], F32)
+                nc.sync.dma_start(out=probe[:], in_=gate[:, 0:PROBE])
             elif what.startswith("wb"):
                 lo, hi = WB_CUTS[int(what[2:])]
                 nc.sync.dma_start(out=wbw[int(what[2:])][:], in_=wb_src[:, lo:hi, :])
             elif what.startswith("wa"):
                 h = int(what[2:])
-                nc.sync.dma_start(out=waw[h][:], in_=wa_src[:, :, WA_CUTS[h][0] * P : WA_CUTS[h][1] * P])
+                nc.sync.dma_start(out=waw[h][:], in_=wa_src[:, WA_CUTS[h][2] : WA_CUTS[h][3], WA_CUTS[h][0] * P : WA_CUTS[h][1] * P])
             else:
                 load_a(int(what[1:]))
 
         banks = [psum.tile([P, BANK], F32, name="bank%d" % n) for n in range(8)]
 
-
-        gate_turned = banks[7]
-        nc.tensor.transpose(gate_turned[:, 0:P], gate_rows[:], ident[:])
-        nc.scalar.activation(gate2[:], gate_turned[:, 0:BLOCKS], COPY, scale=2.0)
 
         def warm(acc):
             nc.tensor.matmul_mx(
@@ -192,22 +217,39 @@ def tile_moe_adb_relu2_kernel(
                 rhs=dyw[:, 0:BANK].bitcast(FP8X4), rhs_scale=dys[:, 0:BANK], start=True, stop=True,
             )
 
+        def turn_gate():
+            gate_turned = banks[GATE_BANK]
+            nc.tensor.transpose(gate_turned[:, 0:P], gate_rows[:], ident[:])
+            nc.scalar.activation(gate2[:], gate_turned[:, 0:BLOCKS], COPY, scale=2.0)
+
+        if GATE_BANK == 7:
+            turn_gate()
         for n in range(WARM):
             warm(banks[3])
+        if GATE_BANK == 3:
+            turn_gate()
+
+        if CUT == 2:
+            clocks = keep.tile([P, 24], F32)
+            nc.gpsimd.tensor_copy(clocks[:, 0:1], a_sb[0][:, 0, 0:1])
+            nc.vector.tensor_copy(clocks[:, 8:9].bitcast(U32), wbs[0][:, 0, 0:4].bitcast(U32))
+            nc.scalar.copy(clocks[:, 16:17], a_sb[1][:, 0, 0:1])
+            return
 
         for lo, hi in GATHER_CUTS:
             slots = slice(lo * P, hi * P)
             entries = offs_sb[:, lo * P // PER_COL : hi * P // PER_COL]
-            nc.vector.tensor_copy(xw[:, slots], dyw[:].bitcast(U32).indirect(entries))
-            nc.vector.tensor_copy(xs[:, slots], dys[:].indirect(entries))
+            nc.vector.tensor_copy(piece(xw, x_cuts, lo * P, hi * P), dyw[:].bitcast(U32).indirect(entries))
+            nc.vector.tensor_copy(piece(xs, x_cuts, lo * P, hi * P), dys[:].indirect(entries))
 
         def first(b, acc):
             e = b * P // C
             slots = slice(b * P, (b + 1) * P)
             n = [i for i, (lo, hi) in enumerate(WB_CUTS) if lo <= e < hi][0]
+            m = [i for i, (lo, hi) in enumerate(WBS_CUTS) if lo <= e < hi][0]
             nc.tensor.matmul_mx(
-                out=acc[:], lhsT=xw[:, slots].bitcast(FP8X4), lhsT_scale=xs[:, slots],
-                rhs=wbw[n][:, e - WB_CUTS[n][0], :].bitcast(FP8X4), rhs_scale=plane(wbs, e, slice(0, H)), start=True, stop=True,
+                out=acc[:], lhsT=piece(xw, x_cuts, b * P, (b + 1) * P).bitcast(FP8X4), lhsT_scale=piece(xs, x_cuts, b * P, (b + 1) * P),
+                rhs=wbw[n][:, e - WB_CUTS[n][0], :].bitcast(FP8X4), rhs_scale=wbs[m][:, e - WBS_CUTS[m][0], :], start=True, stop=True,
             )
             if b in POOL_BLOCKS:
                 dst = gated[b][:].rearrange("s (u m d) -> s u m d", u=2, d=2)
@@ -271,87 +313,77 @@ def tile_moe_adb_relu2_kernel(
 
         def quantize(lo, hi):
             nc.vector.quantize_mx(
-                out=dhw[:, lo:hi].bitcast(FP8X4), scales=dhs[:, lo:hi], in_=dh[:, lo * PACK : hi * PACK]
+                out=piece(dhw, q_cuts, lo, hi).bitcast(FP8X4), scales=piece(dhs, q_cuts, lo, hi), in_=dh[:, lo * PACK : hi * PACK]
             )
 
         def second(c, lo, hi, acc, copy):
-            for s0 in range(lo, hi, C):
-                s1 = min(s0 + C, hi)
+            edges = sorted(set([lo, hi] + [x for x in range(0, S, C) if lo < x < hi] + [b0 * P for b0, b1 in q_cuts if lo < b0 * P < hi]))
+            for s0, s1 in zip(edges[:-1], edges[1:]):
                 e = s0 // C
-                n = [i for i, (c0, c1) in enumerate(WA_CUTS) if c0 <= c < c1][0]
-                words = waw[n][:, e, (c - WA_CUTS[n][0]) * P : (c - WA_CUTS[n][0] + 1) * P]
+                n = [i for i, (c0, c1, e0, e1) in enumerate(WA_CUTS) if c0 <= c < c1 and e0 <= e < e1][0]
+                m = [i for i, (c0, c1) in enumerate(WAS_CUTS) if c0 <= c < c1][0]
+                words = waw[n][:, e - WA_CUTS[n][2], (c - WA_CUTS[n][0]) * P : (c - WA_CUTS[n][0] + 1) * P]
                 nc.tensor.matmul_mx(
-                    out=acc[:, s0 - lo : s1 - lo], lhsT=words.bitcast(FP8X4), lhsT_scale=plane(was, e, slice(c * P, (c + 1) * P)),
-                    rhs=dhw[:, s0:s1].bitcast(FP8X4), rhs_scale=dhs[:, s0:s1], start=True, stop=True,
+                    out=acc[:, s0 - lo : s1 - lo], lhsT=words.bitcast(FP8X4), lhsT_scale=was[m][:, e, (c - WAS_CUTS[m][0]) * P : (c - WAS_CUTS[m][0] + 1) * P],
+                    rhs=piece(dhw, q_cuts, s0, s1).bitcast(FP8X4), rhs_scale=piece(dhs, q_cuts, s0, s1), start=True, stop=True,
                 )
             copy(dx[c][:, lo:hi], acc[:, 0 : hi - lo])
 
         def base_pass(c, t0, t1, dst):
+            n = [i for i, (c0, c1) in enumerate(WT_CUTS) if c0 <= c < c1][0]
+            c0 = c - WT_CUTS[n][0]
             nc.tensor.matmul_mx(
-                out=dst, lhsT=wtw[:, 2 * c * P : 2 * (c + 1) * P].bitcast(FP4X4), lhsT_scale=wts[:, c * P : (c + 1) * P],
+                out=dst, lhsT=wtw[n][:, 2 * c0 * P : 2 * (c0 + 1) * P].bitcast(FP4X4), lhsT_scale=wts[:, c * P : (c + 1) * P],
                 rhs=dyw[:, t0:t1].bitcast(FP8X4), rhs_scale=dys[:, t0:t1], start=True, stop=True,
             )
 
-        def base_main(c, acc):
+        def base_main(c, acc, copy):
             base_pass(c, 0, BANK, acc[:])
-            nc.scalar.copy(base[:, c, 0:BANK], acc[:])
+            copy(base[:, c, 0:BANK], acc[:])
 
-        def base_tails(lo, hi, acc):
+        def base_tails(lo, hi, acc, copy):
             for c in range(lo, hi):
                 base_pass(c, BANK, T, acc[:, (c - lo) * P : (c - lo + 1) * P])
-            nc.scalar.copy(base[:, lo:hi, BANK:T], acc[:, 0 : (hi - lo) * P].rearrange("p (c t) -> p c t", t=P))
+            copy(base[:, lo:hi, BANK:T], acc[:, 0 : (hi - lo) * P].rearrange("p (c t) -> p c t", t=P))
 
-        mains_done = []
-        for step in ORDER:
-            kind, n, bank = step[0], int(step[1]), banks[int(step[2:] or 0)]
+        for step in ORDER.split():
+            kind, args = step[0], step[1:].split(".")
+            copy = nc.vector.tensor_copy if args[-1] == "v" else nc.scalar.copy
+            nums = [int(x) for x in args if x != "v"]
+            bank = banks[nums[-1]] if kind not in "qmu" else None
             if kind == "r":
-                relu_turned(n, bank)
+                relu_turned(nums[0], bank)
             elif kind == "f":
-                first(n, bank)
+                first(nums[0], bank)
             elif kind == "u":
-                weave(n)
+                weave(nums[0])
             elif kind == "h":
-                for i in range(n):
+                for i in range(nums[0]):
                     warm(bank)
-            elif kind == "v":
-                pool_weave(n)
             elif kind == "m":
-                pool_product(n)
+                pool_product(nums[0])
             elif kind == "t":
-                make_dh(n, bank)
+                make_dh(nums[0], bank)
             elif kind == "w":
-                words_back(n, bank)
+                words_back(nums[0], bank)
             elif kind == "q":
-                quantize(n * BANK, (n + 1) * BANK)
+                quantize(nums[0] * P, nums[1] * P)
             elif kind == "s":
-                second(0, n * BANK, (n + 1) * BANK, bank, nc.scalar.copy)
+                second(nums[0], nums[1] * P, nums[2] * P, bank, copy)
             elif kind == "b":
-                base_main(n, bank)
-                mains_done.append(n)
+                base_main(nums[0], bank, copy)
             else:
-                base_tails(0, n, bank)
-                tails_done = n
-        tail_banks = [banks[n] for n in TAIL_BANKS]
-        quantize(S - C, S - P)
-        second(0, S - C, S - P, tail_banks[0], nc.scalar.copy)
-        quantize(S - P, S)
-        second(0, S - P, S, tail_banks[1], nc.scalar.copy if LAST_ACT else nc.vector.tensor_copy)
+                base_tails(nums[0], nums[1], bank, copy)
 
-        for c in range(1, 2 if PAIR else CHUNKS):
-            later_banks = [banks[n] for n in LATER[c - 1]]
-            for acc, lo in zip(later_banks, range(0, S, BANK)):
-                second(c, lo, min(lo + BANK, S), acc, nc.scalar.copy)
-            if c not in mains_done:
-                base_main(c, later_banks[3])
-            if c == 1 and tails_done < CHUNKS:
-                base_tails(tails_done, CHUNKS, later_banks[4])
+        if CLOCK:
+            clock = keep.tile([P, 8], F32)
+            what, col = CLOCK
+            src = {"dh": dh[:, col // 2 * 2 : col // 2 * 2 + 2].bitcast(F32), "dhw": piece(dhw, q_cuts, col % S, col % S + 1).bitcast(F32), "dx0": dx[0][:, col % S : col % S + 1], "dx1": dx[1][:, col % S : col % S + 1],
+                   "xw": piece(xw, x_cuts, col % S, col % S + 1), "gated": gated[col % BLOCKS][:, 0:1], "a": a_sb[col % len(a_sb)][:, 0, 0:1], "wb": wbw[col % len(wbw)][:, 0, 0:1]}[what]
+            nc.gpsimd.tensor_copy(clock[:, 0:1].bitcast(U32), src.bitcast(U32))
 
-        if PAIR:
-            for c in (2, 3):
-                base_main(c, banks[LATER[c - 1][3]])
-            for n, lo in enumerate(range(0, S, BANK)):
-                for c in (2, 3):
-                    second(c, lo, min(lo + BANK, S), banks[LATER[c - 1][n]], nc.scalar.copy)
+        if CUT:
+            return
 
         def gather_add(dst, c, pos_sb, other, t0, t1):
             entries = pos_sb[:, t0 // PER_COL : t1 // PER_COL]

@@ -10,50 +10,9 @@ PACK = 4
 BANK = 512
 PER_COL = 16
 CHUNKS = K // P
-BLOCKS = S // P
+GROUPS = S // P
 WINDOW = 768
 FLOPS = 2 * K * N * T + 2 * S * N * H + 2 * S * H * K
-
-GATHER_CUTS = ((0, 3), (3, 6), (6, 10))
-A_CUTS = ((0, 2), (2, 5), (5, 7), (7, 10))
-WB_FIRST = 3
-QUANT_BLOCKS = 4
-LEAD = 2
-POOL_BLOCKS = (0,)
-LOADS = ("dy", "wb0", "gate", "wbs0", "a0", "wb1", "wb2", "a1", "wb3", "a2", "wts", "a3", "wt0", "was0", "wa0", "wa1", "pos1", "wa2", "pos2", "wa3",)
-WB_CUTS = ((0, 2), (2, 3), (3, 4), (4, 5))
-ORDER = "f0.0 f1.1 f2.2 f3.0 t1.3 r0.7 m0 f4.1 t2.4 f5.2 t3.5 f6.0 t4.6 w0.7 f7.1 t5.3 q0.4 f8.2 t6.4 f9.0 t7.5 u9 t8.6 h2.2 q4.8 b0.1 c0.1.2 t9.7 s0.0.4.0 q8.9 q9.10 s0.4.8.3.v s0.8.9.4 s0.9.10.5 s1.0.4.1 s1.4.8.2 s1.8.10.6 b1.0 c1.4.3 b2.1 b3.2 s2.0.4.7 s3.0.4.4 s2.4.8.5 s3.4.8.0 s2.8.10.6 s3.8.10.3"
-GATE_POOL = 0
-WHOLE = 0
-WEAVE_BLOCKS = ()
-WEAVE_OVER = ()
-LAST_PIECES = ((0, 448), (448, T))
-LAST_ACT = 1
-PAIR = 1
-RELU_BLOCKS = (9,)
-WARM = 4
-SPLIT_X = 0
-SPLIT_Q = 0
-Q_CUTS = ((0, 4), (4, 8), (8, 9), (9, 10))
-CUT = 0
-GATE_BANK = 7
-CLOCK = ()
-PROBE = 1280
-DYS_VEC = 1
-POOL_MEMSETS = ()
-WA_CUTS = ((0, 1, 0, 2), (0, 1, 2, 5), (1, 2, 0, 5), (2, 4, 0, 5))
-RFORM = 1
-PACKED = 0
-WBS_ACT = 0
-MEMSETS = ("gate", "wbs0", "was0", "wts")
-WBS_CUTS = ((0, 5),)
-ACT_LOADS = ()
-POOL_LOADS = ()
-WAS_CUTS = ((0, 4),)
-WT_CUTS = ((0, 4),)
-LATER = ((1, 2, 6, 0, 3), (7, 5, 6, 1), (4, 0, 3, 2))
-TAIL_BANKS = (4, 5)
-TOKEN_PIECES = ((0, 384), (384, T))
 
 F32 = mybir.dt.float32
 BF16 = mybir.dt.bfloat16
@@ -67,6 +26,18 @@ COPY = mybir.ActivationFunctionType.Copy
 RELU = mybir.ActivationFunctionType.Relu
 ALU = mybir.AluOpType
 
+GATHER_CUTS = ((0, 3), (3, 6), (6, 10))
+A_CUTS = ((0, 2), (2, 5), (5, 7), (7, 10))
+WB_CUTS = ((0, 2), (2, 3), (3, 4), (4, 5))
+WA_CUTS = ((0, 1, 0, 2), (0, 1, 2, 5), (1, 2, 0, 5), (2, 4, 0, 5))
+DH_TILES = ((0, 4, 0), (4, 8, 8), (8, 10, 9))
+POOL_GROUPS = (0,)
+WOVEN_GROUPS = (9,)
+WAS_CUTS = ((0, 4),)
+WT_CUTS = ((0, 4),)
+TOKEN_PIECES = ((0, 384), (384, T))
+LAST_PIECES = ((0, 448), (448, T))
+
 
 def tile_moe_adb_relu2_kernel(
     tc, dy_words, dy_scales, wt_words, wt_scales, wbt_words, wbt_scales, wat_words, wat_scales, a, gate, offs, pos1, pos2, out
@@ -76,140 +47,74 @@ def tile_moe_adb_relu2_kernel(
         keep = ctx.enter_context(tc.tile_pool(name="keep", bufs=1))
         psum = ctx.enter_context(tc.psum_pool(name="psum", bufs=1))
 
-        offs_sb = keep.tile([P, S // PER_COL], U16)
-        pos1_sb = keep.tile([P, T // PER_COL], U16)
-        pos2_sb = keep.tile([P, T // PER_COL], U16)
-        dyw = keep.tile([P, WINDOW], I32, align_bytes=64)
-        dys = keep.tile([P, WINDOW], U8, align_bytes=64)
-        wts = keep.tile([P, K], U8, align_bytes=64)
+        offs_sb = keep.tile([P, S // PER_COL], U16, name="offs_sb")
+        pos1_sb = keep.tile([P, T // PER_COL], U16, name="pos1_sb")
+        pos2_sb = keep.tile([P, T // PER_COL], U16, name="pos2_sb")
+        dyw = keep.tile([P, WINDOW], I32, name="dyw", align_bytes=64)
+        dys = keep.tile([P, WINDOW], U8, name="dys", align_bytes=64)
         wtw = [keep.tile([P, 2 * (hi - lo) * P], U8, name="wtw%d" % lo, align_bytes=64) for lo, hi in WT_CUTS]
-        base = keep.tile([P, CHUNKS, T], F32)
+        wts = keep.tile([P, K], U8, name="wts", align_bytes=64)
         wbw = [keep.tile([P, hi - lo, H], I32, name="wbw%d" % lo, align_bytes=64) for lo, hi in WB_CUTS]
-        wbs = [keep.tile([P, hi - lo, H], U8, name="wbs%d" % lo, align_bytes=64) for lo, hi in WBS_CUTS]
-        waw = [keep.tile([P, e1 - e0, (hi - lo) * P], I32, name="waw%d_%d" % (lo, e0), align_bytes=64) for lo, hi, e0, e1 in WA_CUTS]
-        was = [keep.tile([P, E, (hi - lo) * P], U8, name="was%d" % lo, align_bytes=64) for lo, hi in WAS_CUTS]
-        gate_rows = keep.tile([P, P], F32)
-        gate2 = keep.tile([P, BLOCKS], F32)
-        ident = keep.tile([P, P], F32)
-        x_cuts = GATHER_CUTS if SPLIT_X else ((0, BLOCKS),)
-        q_cuts = Q_CUTS if SPLIT_Q else ((0, BLOCKS),)
-        xw = [keep.tile([P, (hi - lo) * P], U32, name="xw%d" % lo, align_bytes=64) for lo, hi in x_cuts]
-        xs = [keep.tile([P, (hi - lo) * P], U8, name="xs%d" % lo, align_bytes=64) for lo, hi in x_cuts]
-        gated = [keep.tile([P, H], F32, name="gated%d" % b) for b in range(BLOCKS)]
-        dh = keep.tile([P, S * PACK], BF16, align_bytes=64)
-        relu_rows = {b: keep.tile([P, H], F32, name="relu%d" % b) for b in POOL_BLOCKS}
-        relu_woven = {b: keep.tile([P, H], F32, name="woven%d" % b)[:] for b in RELU_BLOCKS + WEAVE_BLOCKS if b not in WEAVE_OVER}
-        for b in WEAVE_OVER:
-            relu_woven[b] = dh[:, 0 : 2 * H].bitcast(F32)
-        dh_rows = {b: keep.tile([P, H], BF16, name="rows%d" % b, align_bytes=64) for b in POOL_BLOCKS}
-        dhw = [keep.tile([P, (hi - lo) * P], U32, name="dhw%d" % lo, align_bytes=64) for lo, hi in q_cuts]
-        dhs = [keep.tile([P, (hi - lo) * P], U8, name="dhs%d" % lo, align_bytes=64) for lo, hi in q_cuts]
-
-        def piece(tiles, cuts, lo, hi):
-            n = [i for i, (b0, b1) in enumerate(cuts) if b0 * P <= lo and hi <= b1 * P][0]
-            return tiles[n][:, lo - cuts[n][0] * P : hi - cuts[n][0] * P]
-
-        a_sb = [
-            keep.tile([P, PACK, (hi - lo) * P], F32, name="a%d" % lo, align_bytes=64) for lo, hi in A_CUTS
+        wbs = keep.tile([P, E, H], U8, name="wbs", align_bytes=64)
+        waw = [
+            keep.tile([P, e1 - e0, (c1 - c0) * P], I32, name="waw%d_%d" % (c0, e0), tag="waw%d_%d" % (c0, e0), align_bytes=64)
+            for c0, c1, e0, e1 in WA_CUTS
         ]
+        was = [keep.tile([P, E, (hi - lo) * P], U8, name="was%d" % lo, align_bytes=64) for lo, hi in WAS_CUTS]
+        a_sb = [keep.tile([P, PACK, (hi - lo) * P], F32, name="a%d" % lo, align_bytes=64) for lo, hi in A_CUTS]
+        gate_rows = keep.tile([P, P], F32, name="gate_rows")
+        gate2 = keep.tile([P, GROUPS], F32, name="gate2")
+        ident = keep.tile([P, P], F32, name="ident")
+        xw = keep.tile([P, S], U32, name="xw", align_bytes=64)
+        xs = keep.tile([P, S], U8, name="xs", align_bytes=64)
+        gated = [keep.tile([P, H], F32, name="gated%d" % b, tag="gated%d" % b, align_bytes=64) for b in range(GROUPS)]
+        relu_rows = {b: keep.tile([P, H], F32, name="relu%d" % b) for b in POOL_GROUPS}
+        relu_woven = {b: keep.tile([P, H], F32, name="woven%d" % b) for b in WOVEN_GROUPS}
+        dh_rows = {b: keep.tile([P, H], BF16, name="rows%d" % b, align_bytes=64) for b in POOL_GROUPS}
+        dh = keep.tile([P, S * PACK], BF16, name="dh", align_bytes=64)
+        dhw = {}
+        dhs = keep.tile([P, S], U8, name="dhs", align_bytes=64)
+        base = keep.tile([P, CHUNKS, T], F32, name="base")
         dx = [keep.tile([P, S], F32, name="dx%d" % c) for c in range(CHUNKS)]
         part = [keep.tile([P, T], F32, name="part%d" % c) for c in range(CHUNKS)]
-        res = {c: keep.tile([P, T], F32, name="res%d" % c) for c in range(CHUNKS)}
-
-        (nc.vector if DYS_VEC else nc.gpsimd).memset(dys[:].bitcast(I32), 0)
-        nc.vector.memset(dyw[:, T:WINDOW], 0)
-        zeroed = {
-            "gate": gate_rows[:].bitcast(I32),
-            "wts": wts[:].bitcast(I32),
-        }
-        for n in range(len(WBS_CUTS)):
-            zeroed["wbs%d" % n] = wbs[n][:].rearrange("p e n -> p (e n)").bitcast(I32)
-        for n in range(len(WAS_CUTS)):
-            zeroed["was%d" % n] = was[n][:].rearrange("p e n -> p (e n)").bitcast(I32)
-        for what in MEMSETS:
-            (nc.gpsimd if what in POOL_MEMSETS else nc.vector).memset(zeroed[what], 0)
-        make_identity(nc, ident[:])
+        res = {c: keep.tile([P, T], F32, name="res%d" % c) for c in (0, 3)}
+        banks = [psum.tile([P, BANK], F32, name="bank%d" % n) for n in range(8)]
 
         wb_src = wbt_words.rearrange("e o p n d -> p (e o) (n d)").bitcast(I32)
         wa_src = wat_words.rearrange("e o p n d -> p (e o) (n d)").bitcast(I32)
         a_src = a.rearrange("(p t) s -> p t s", t=PACK)
+        wbs_src = wbt_scales.rearrange("e o r n -> r (e o) n")
+        was_src = wat_scales.rearrange("e o r n -> r (e o) n")
 
-        def load_scales(tile, rows, queues=(nc.sync,) * 4):
+        def load_scale_rows(tile, rows, r, queue=nc.sync):
             rest = (slice(None),) * (len(rows.shape) - 1)
-            for q in range(4):
-                if RFORM:
-                    queues[q].dma_start(
-                        out=tile[(slice(q, P, 32),) + rest].bitcast(I32),
-                        in_=rows[(slice(q, 16, 4),) + rest].bitcast(I32),
-                    )
-                else:
-                    queues[q].dma_start(
-                        out=tile[(slice(32 * q, 32 * q + 4),) + rest].bitcast(I32),
-                        in_=rows[(slice(4 * q, 4 * q + 4),) + rest].bitcast(I32),
-                    )
+            queue.dma_start(
+                out=tile[(slice(r, P, 32),) + rest].bitcast(I32), in_=rows[(slice(r, 16, 4),) + rest].bitcast(I32)
+            )
 
-        def load_packed(tile, scales, queue):
-            for q in range(4):
-                queue.dma_start(
-                    out=tile[32 * q : 32 * q + 16, 0, :].bitcast(I32),
-                    in_=scales[0:PACK, 0, 4 * q : 4 * q + 4, :].bitcast(I32),
-                )
-
-        def plane(tile, e, cols):
-            if PACKED:
-                return tile[4 * (e % PACK) : P, e // PACK, cols]
-            return tile[:, e, cols]
+        def load_scales(tile, rows, queues):
+            for r in range(4):
+                load_scale_rows(tile, rows, r, queues[r])
 
         def load_a(n):
             lo, hi = A_CUTS[n]
             nc.sync.dma_start(out=a_sb[n][:], in_=a_src[:, :, lo * P : hi * P])
 
-        def queue_of(what):
-            return nc.gpsimd if what in POOL_LOADS else nc.scalar if what in ACT_LOADS else nc.sync
+        def load_wb(n):
+            lo, hi = WB_CUTS[n]
+            nc.sync.dma_start(out=wbw[n][:], in_=wb_src[:, lo:hi, :])
 
-        for what in LOADS:
-            if what == "dy":
-                nc.sync.dma_start(out=dyw[:, 0:T], in_=dy_words[0].rearrange("p t d -> p (t d)").bitcast(I32))
-                load_scales(dys[:, 0:T], dy_scales[0], (nc.scalar, nc.scalar, nc.sync, nc.sync))
-                nc.sync.dma_start(offs_sb[:], offs)
-            elif what == "gate":
-                rows = gate[0].rearrange("(b p) -> b p", p=P)
-                if GATE_POOL == 2:
-                    nc.scalar.dma_start(out=gate_rows[0:BLOCKS, :], in_=rows)
-                elif GATE_POOL == 3:
-                    nc.sync.dma_start(out=gate_rows[0:8, :], in_=rows[0:8, :])
-                    nc.sync.dma_start(out=gate_rows[8:BLOCKS, :], in_=rows[8:BLOCKS, :])
-                else:
-                    (nc.gpsimd if GATE_POOL else nc.sync).dma_start(out=gate_rows[0:BLOCKS, :], in_=rows)
-            elif what.startswith("wbs"):
-                lo, hi = WBS_CUTS[int(what[3:])]
-                load_scales(wbs[int(what[3:])], wbt_scales.rearrange("e o r n -> r (e o) n")[:, lo:hi, :], (queue_of(what),) * 4)
-            elif what.startswith("was"):
-                lo, hi = WAS_CUTS[int(what[3:])]
-                load_scales(was[int(what[3:])], wat_scales.rearrange("e o r n -> r (e o) n")[:, :, lo * P : hi * P], (queue_of(what),) * 4)
-            elif what == "wts":
-                load_scales(wts, wt_scales[0], (queue_of(what),) * 4)
-            elif what.startswith("wt"):
-                lo, hi = WT_CUTS[int(what[2:])]
-                nc.sync.dma_start(out=wtw[int(what[2:])][:].bitcast(I32), in_=wt_words[0][:, 2 * lo * P : 2 * hi * P].bitcast(I32))
-            elif what == "pos1":
-                nc.sync.dma_start(pos1_sb[:], pos1)
-            elif what == "pos2":
-                nc.sync.dma_start(pos2_sb[:], pos2)
-            elif what == "probe":
-                probe = keep.tile([P, PROBE], F32)
-                nc.sync.dma_start(out=probe[:], in_=gate[:, 0:PROBE])
-            elif what.startswith("wb"):
-                lo, hi = WB_CUTS[int(what[2:])]
-                nc.sync.dma_start(out=wbw[int(what[2:])][:], in_=wb_src[:, lo:hi, :])
-            elif what.startswith("wa"):
-                h = int(what[2:])
-                nc.sync.dma_start(out=waw[h][:], in_=wa_src[:, WA_CUTS[h][2] : WA_CUTS[h][3], WA_CUTS[h][0] * P : WA_CUTS[h][1] * P])
-            else:
-                load_a(int(what[1:]))
+        def load_wa(n):
+            c0, c1, e0, e1 = WA_CUTS[n]
+            nc.sync.dma_start(out=waw[n][:], in_=wa_src[:, e0:e1, c0 * P : c1 * P])
 
-        banks = [psum.tile([P, BANK], F32, name="bank%d" % n) for n in range(8)]
+        def load_was(n):
+            lo, hi = WAS_CUTS[n]
+            load_scales(was[n], was_src[:, :, lo * P : hi * P], (nc.sync,) * 4)
 
+        def load_wt(n):
+            lo, hi = WT_CUTS[n]
+            nc.sync.dma_start(out=wtw[n][:].bitcast(I32), in_=wt_words[0][:, 2 * lo * P : 2 * hi * P].bitcast(I32))
 
         def warm(acc):
             nc.tensor.matmul_mx(
@@ -217,41 +122,22 @@ def tile_moe_adb_relu2_kernel(
                 rhs=dyw[:, 0:BANK].bitcast(FP8X4), rhs_scale=dys[:, 0:BANK], start=True, stop=True,
             )
 
-        def turn_gate():
-            gate_turned = banks[GATE_BANK]
-            nc.tensor.transpose(gate_turned[:, 0:P], gate_rows[:], ident[:])
-            nc.scalar.activation(gate2[:], gate_turned[:, 0:BLOCKS], COPY, scale=2.0)
-
-        if GATE_BANK == 7:
-            turn_gate()
-        for n in range(WARM):
-            warm(banks[3])
-        if GATE_BANK == 3:
-            turn_gate()
-
-        if CUT == 2:
-            clocks = keep.tile([P, 24], F32)
-            nc.gpsimd.tensor_copy(clocks[:, 0:1], a_sb[0][:, 0, 0:1])
-            nc.vector.tensor_copy(clocks[:, 8:9].bitcast(U32), wbs[0][:, 0, 0:4].bitcast(U32))
-            nc.scalar.copy(clocks[:, 16:17], a_sb[1][:, 0, 0:1])
-            return
-
-        for lo, hi in GATHER_CUTS:
-            slots = slice(lo * P, hi * P)
+        def gather_in(n):
+            lo, hi = GATHER_CUTS[n]
             entries = offs_sb[:, lo * P // PER_COL : hi * P // PER_COL]
-            nc.vector.tensor_copy(piece(xw, x_cuts, lo * P, hi * P), dyw[:].bitcast(U32).indirect(entries))
-            nc.vector.tensor_copy(piece(xs, x_cuts, lo * P, hi * P), dys[:].indirect(entries))
+            nc.vector.tensor_copy(xw[:, lo * P : hi * P], dyw[:].bitcast(U32).indirect(entries))
+            nc.vector.tensor_copy(xs[:, lo * P : hi * P], dys[:].indirect(entries))
 
         def first(b, acc):
             e = b * P // C
-            slots = slice(b * P, (b + 1) * P)
             n = [i for i, (lo, hi) in enumerate(WB_CUTS) if lo <= e < hi][0]
-            m = [i for i, (lo, hi) in enumerate(WBS_CUTS) if lo <= e < hi][0]
             nc.tensor.matmul_mx(
-                out=acc[:], lhsT=piece(xw, x_cuts, b * P, (b + 1) * P).bitcast(FP8X4), lhsT_scale=piece(xs, x_cuts, b * P, (b + 1) * P),
-                rhs=wbw[n][:, e - WB_CUTS[n][0], :].bitcast(FP8X4), rhs_scale=wbs[m][:, e - WBS_CUTS[m][0], :], start=True, stop=True,
+                out=acc[:], lhsT=xw[:, b * P : (b + 1) * P].bitcast(FP8X4), lhsT_scale=xs[:, b * P : (b + 1) * P],
+                rhs=wbw[n][:, e - WB_CUTS[n][0], :].bitcast(FP8X4), rhs_scale=wbs[:, e, :], start=True, stop=True,
             )
-            if b in POOL_BLOCKS:
+
+        def apply_gate(b, acc):
+            if b in POOL_GROUPS:
                 dst = gated[b][:].rearrange("s (u m d) -> s u m d", u=2, d=2)
                 src = acc[:].rearrange("s (m u d) -> s u m d", u=2, d=2)
             else:
@@ -259,26 +145,24 @@ def tile_moe_adb_relu2_kernel(
                 src = acc[:].rearrange("s (m t) -> s t m", t=PACK)
             nc.scalar.activation(dst, src, COPY, scale=gate2[:, b : b + 1])
 
-        def a_block(b):
+        def a_group(b):
             n = [i for i, (lo, hi) in enumerate(A_CUTS) if lo <= b < hi][0]
             s0 = (b - A_CUTS[n][0]) * P
             return a_sb[n][:, :, s0 : s0 + P]
 
-        def relu_turned(b, turned):
+        def turn_a(b, turned):
             for t in range(PACK):
-                nc.tensor.transpose(turned[:, t * P : (t + 1) * P], a_block(b)[:, t, :], ident[:])
+                nc.tensor.transpose(turned[:, t * P : (t + 1) * P], a_group(b)[:, t, :], ident[:])
+
+        def relu_out(b, turned):
             nc.scalar.activation(
                 relu_rows[b][:].rearrange("s (u m d) -> s u m d", u=2, d=2),
                 turned[:].rearrange("s (u d m) -> s u m d", u=2, d=2), RELU,
             )
 
         def weave(b):
-            woven = relu_woven[b].rearrange("p (s t) -> p s t", t=PACK)
-            nc.scalar.activation(woven, a_block(b).rearrange("p t s -> p s t"), RELU)
-
-        def pool_weave(b):
-            woven = relu_woven[b].rearrange("p (s t) -> p s t", t=PACK)
-            nc.gpsimd.tensor_scalar(woven, a_block(b).rearrange("p t s -> p s t"), 1.0, 0.0, ALU.mult, ALU.add)
+            woven = relu_woven[b][:].rearrange("p (s t) -> p s t", t=PACK)
+            nc.scalar.activation(woven, a_group(b).rearrange("p t s -> p s t"), RELU)
 
         def pool_product(b):
             nc.gpsimd.tensor_tensor(dh_rows[b][:], gated[b][:], relu_rows[b][:], ALU.mult)
@@ -292,98 +176,71 @@ def tile_moe_adb_relu2_kernel(
                 turned[:, 0 : 2 * P].rearrange("p (u s) -> p s u", u=2),
             )
 
-        def make_dh(b, turned):
+        def turn(b, turned):
             for t in range(PACK):
                 nc.tensor.transpose(turned[:, t * P : (t + 1) * P], gated[b][:, t * P : (t + 1) * P], ident[:])
-            if b in RELU_BLOCKS:
-                woven = relu_woven[b].rearrange("p (s t) -> p s t", t=PACK)
+
+        def product(b, turned):
+            if b in WOVEN_GROUPS:
                 nc.vector.tensor_tensor(
-                    dh[:, b * H : (b + 1) * H].rearrange("p (s t) -> p s t", t=PACK), woven,
+                    dh[:, b * H : (b + 1) * H].rearrange("p (s t) -> p s t", t=PACK),
+                    relu_woven[b][:].rearrange("p (s t) -> p s t", t=PACK),
                     turned[:].rearrange("p (t s) -> p s t", t=PACK), ALU.mult,
                 )
                 return
             nc.vector.scalar_tensor_tensor(
                 out=dh[:, b * H : (b + 1) * H].rearrange("p (s t) -> p s t", t=PACK),
-                in0=relu_woven[b].rearrange("p (s t) -> p s t", t=PACK) if b in WEAVE_BLOCKS else a_block(b).rearrange("p t s -> p s t"),
+                in0=a_group(b).rearrange("p t s -> p s t"),
                 scalar=0.0,
                 in1=turned[:].rearrange("p (t s) -> p s t", t=PACK),
                 op0=ALU.max,
                 op1=ALU.mult,
             )
 
+        def dh_words(s0, s1):
+            lo = [g0 for g0, g1, holder in DH_TILES if g0 * P <= s0 and s1 <= g1 * P][0]
+            return dhw[lo][:, s0 - lo * P : s1 - lo * P]
+
         def quantize(lo, hi):
+            for g0, g1, holder in DH_TILES:
+                if g0 <= lo < g1 and g0 not in dhw:
+                    dhw[g0] = keep.tile([P, (g1 - g0) * P], U32, name="dhw%d" % g0, tag="gated%d" % holder, align_bytes=64)
             nc.vector.quantize_mx(
-                out=piece(dhw, q_cuts, lo, hi).bitcast(FP8X4), scales=piece(dhs, q_cuts, lo, hi), in_=dh[:, lo * PACK : hi * PACK]
+                out=dh_words(lo * P, hi * P).bitcast(FP8X4), scales=dhs[:, lo * P : hi * P], in_=dh[:, lo * H : hi * H]
             )
 
-        def second(c, lo, hi, acc, copy):
-            edges = sorted(set([lo, hi] + [x for x in range(0, S, C) if lo < x < hi] + [b0 * P for b0, b1 in q_cuts if lo < b0 * P < hi]))
+        def second(c, lo, hi, acc, copy=nc.scalar.copy):
+            edges = [lo * P] + [x for x in range(0, S, C) if lo * P < x < hi * P] + [hi * P]
             for s0, s1 in zip(edges[:-1], edges[1:]):
                 e = s0 // C
                 n = [i for i, (c0, c1, e0, e1) in enumerate(WA_CUTS) if c0 <= c < c1 and e0 <= e < e1][0]
-                m = [i for i, (c0, c1) in enumerate(WAS_CUTS) if c0 <= c < c1][0]
-                words = waw[n][:, e - WA_CUTS[n][2], (c - WA_CUTS[n][0]) * P : (c - WA_CUTS[n][0] + 1) * P]
+                c0, e0 = WA_CUTS[n][0], WA_CUTS[n][2]
+                m = [i for i, (s_lo, s_hi) in enumerate(WAS_CUTS) if s_lo <= c < s_hi][0]
+                sc = c - WAS_CUTS[m][0]
                 nc.tensor.matmul_mx(
-                    out=acc[:, s0 - lo : s1 - lo], lhsT=words.bitcast(FP8X4), lhsT_scale=was[m][:, e, (c - WAS_CUTS[m][0]) * P : (c - WAS_CUTS[m][0] + 1) * P],
-                    rhs=piece(dhw, q_cuts, s0, s1).bitcast(FP8X4), rhs_scale=piece(dhs, q_cuts, s0, s1), start=True, stop=True,
+                    out=acc[:, s0 - lo * P : s1 - lo * P],
+                    lhsT=waw[n][:, e - e0, (c - c0) * P : (c - c0 + 1) * P].bitcast(FP8X4),
+                    lhsT_scale=was[m][:, e, sc * P : (sc + 1) * P],
+                    rhs=dh_words(s0, s1).bitcast(FP8X4), rhs_scale=dhs[:, s0:s1], start=True, stop=True,
                 )
-            copy(dx[c][:, lo:hi], acc[:, 0 : hi - lo])
+            copy(dx[c][:, lo * P : hi * P], acc[:, 0 : (hi - lo) * P])
 
         def base_pass(c, t0, t1, dst):
-            n = [i for i, (c0, c1) in enumerate(WT_CUTS) if c0 <= c < c1][0]
+            n = [i for i, (lo, hi) in enumerate(WT_CUTS) if lo <= c < hi][0]
             c0 = c - WT_CUTS[n][0]
             nc.tensor.matmul_mx(
                 out=dst, lhsT=wtw[n][:, 2 * c0 * P : 2 * (c0 + 1) * P].bitcast(FP4X4), lhsT_scale=wts[:, c * P : (c + 1) * P],
                 rhs=dyw[:, t0:t1].bitcast(FP8X4), rhs_scale=dys[:, t0:t1], start=True, stop=True,
             )
 
-        def base_main(c, acc, copy):
+        def base_main(c, acc, copy=nc.scalar.copy):
             base_pass(c, 0, BANK, acc[:])
             copy(base[:, c, 0:BANK], acc[:])
 
-        def base_tails(lo, hi, acc, copy):
+        def base_tails(lo, hi, acc, copy=nc.scalar.copy):
             for c in range(lo, hi):
                 base_pass(c, BANK, T, acc[:, (c - lo) * P : (c - lo + 1) * P])
             copy(base[:, lo:hi, BANK:T], acc[:, 0 : (hi - lo) * P].rearrange("p (c t) -> p c t", t=P))
-
-        for step in ORDER.split():
-            kind, args = step[0], step[1:].split(".")
-            copy = nc.vector.tensor_copy if args[-1] == "v" else nc.scalar.copy
-            nums = [int(x) for x in args if x != "v"]
-            bank = banks[nums[-1]] if kind not in "qmu" else None
-            if kind == "r":
-                relu_turned(nums[0], bank)
-            elif kind == "f":
-                first(nums[0], bank)
-            elif kind == "u":
-                weave(nums[0])
-            elif kind == "h":
-                for i in range(nums[0]):
-                    warm(bank)
-            elif kind == "m":
-                pool_product(nums[0])
-            elif kind == "t":
-                make_dh(nums[0], bank)
-            elif kind == "w":
-                words_back(nums[0], bank)
-            elif kind == "q":
-                quantize(nums[0] * P, nums[1] * P)
-            elif kind == "s":
-                second(nums[0], nums[1] * P, nums[2] * P, bank, copy)
-            elif kind == "b":
-                base_main(nums[0], bank, copy)
-            else:
-                base_tails(nums[0], nums[1], bank, copy)
-
-        if CLOCK:
-            clock = keep.tile([P, 8], F32)
-            what, col = CLOCK
-            src = {"dh": dh[:, col // 2 * 2 : col // 2 * 2 + 2].bitcast(F32), "dhw": piece(dhw, q_cuts, col % S, col % S + 1).bitcast(F32), "dx0": dx[0][:, col % S : col % S + 1], "dx1": dx[1][:, col % S : col % S + 1],
-                   "xw": piece(xw, x_cuts, col % S, col % S + 1), "gated": gated[col % BLOCKS][:, 0:1], "a": a_sb[col % len(a_sb)][:, 0, 0:1], "wb": wbw[col % len(wbw)][:, 0, 0:1]}[what]
-            nc.gpsimd.tensor_copy(clock[:, 0:1].bitcast(U32), src.bitcast(U32))
-
-        if CUT:
-            return
 
         def gather_add(dst, c, pos_sb, other, t0, t1):
             entries = pos_sb[:, t0 // PER_COL : t1 // PER_COL]
@@ -392,44 +249,124 @@ def tile_moe_adb_relu2_kernel(
         def store(c, t0, t1):
             nc.sync.dma_start(out=out[c * P : (c + 1) * P, t0:t1], in_=res[c][:, t0:t1])
 
-        last = CHUNKS - 1
-        if PAIR:
-            for c in (0, 1):
-                for t0, t1 in TOKEN_PIECES:
-                    gather_add(part[c], c, pos1_sb, base[:, c, :], t0, t1)
-                for t0, t1 in TOKEN_PIECES:
-                    gather_add(res[c], c, pos2_sb, part[c], t0, t1)
-                store(c, 0, T)
-            for c in (2, 3):
-                gather_add(part[c], c, pos1_sb, base[:, c, :], 0, T)
-            gather_add(res[2], 2, pos2_sb, part[2], 0, T)
-            store(2, 0, T)
-            for t0, t1 in LAST_PIECES:
-                gather_add(res[3], 3, pos2_sb, part[3], t0, t1)
-                store(3, t0, t1)
-        elif WHOLE:
-            for t0, t1 in TOKEN_PIECES:
-                gather_add(part[0], 0, pos1_sb, base[:, 0, :], t0, t1)
-            for t0, t1 in TOKEN_PIECES:
-                gather_add(res[0], 0, pos2_sb, part[0], t0, t1)
-            store(0, 0, T)
-            gather_add(part[1], 1, pos1_sb, base[:, 1, :], 0, T)
-            gather_add(part[2], 2, pos1_sb, base[:, 2, :], 0, T)
-            for c in range(1, last):
-                gather_add(res[c], c, pos2_sb, part[c], 0, T)
-                store(c, 0, T)
-            for t0, t1 in TOKEN_PIECES:
-                gather_add(part[last], last, pos1_sb, base[:, last, :], t0, t1)
-            for t0, t1 in TOKEN_PIECES:
-                gather_add(res[last], last, pos2_sb, part[last], t0, t1)
-                store(last, t0, t1)
-        else:
-            for c in range(CHUNKS):
-                for t0, t1 in TOKEN_PIECES:
-                    gather_add(part[c], c, pos1_sb, base[:, c, :], t0, t1)
-                for t0, t1 in TOKEN_PIECES:
-                    gather_add(res[c], c, pos2_sb, part[c], t0, t1)
-                    if c == last:
-                        store(c, t0, t1)
-                if c != last:
-                    store(c, 0, T)
+        nc.vector.memset(dys[:].bitcast(I32), 0)
+        nc.vector.memset(dyw[:, T:WINDOW], 0)
+        nc.vector.memset(gate_rows[:].bitcast(I32), 0)
+        nc.vector.memset(wbs[:].rearrange("p e n -> p (e n)").bitcast(I32), 0)
+        nc.vector.memset(was[0][:].rearrange("p e n -> p (e n)").bitcast(I32), 0)
+        nc.vector.memset(wts[:].bitcast(I32), 0)
+        make_identity(nc, ident[:])
+
+        nc.sync.dma_start(out=dyw[:, 0:T], in_=dy_words[0].rearrange("p t d -> p (t d)").bitcast(I32))
+        load_scales(dys[:, 0:T], dy_scales[0], (nc.scalar, nc.scalar, nc.sync, nc.sync))
+        nc.sync.dma_start(offs_sb[:], offs)
+        load_wb(0)
+        nc.sync.dma_start(out=gate_rows[0:GROUPS, :], in_=gate[0].rearrange("(b p) -> b p", p=P))
+        load_scales(wbs, wbs_src, (nc.sync,) * 4)
+        load_a(0)
+        load_wb(1)
+        load_wb(2)
+        load_a(1)
+        load_wb(3)
+        load_a(2)
+        load_scales(wts, wt_scales[0], (nc.sync,) * 4)
+        load_a(3)
+        load_wt(0)
+        load_was(0)
+        load_wa(0)
+        load_wa(1)
+        nc.sync.dma_start(pos1_sb[:], pos1)
+        load_wa(2)
+        nc.sync.dma_start(pos2_sb[:], pos2)
+        load_wa(3)
+
+        nc.tensor.transpose(banks[7][:, 0:P], gate_rows[:], ident[:])
+        nc.scalar.activation(gate2[:], banks[7][:, 0:GROUPS], COPY, scale=2.0)
+        for n in range(4):
+            warm(banks[3])
+        for n in range(len(GATHER_CUTS)):
+            gather_in(n)
+
+        first(0, banks[0])
+        apply_gate(0, banks[0])
+        first(1, banks[1])
+        apply_gate(1, banks[1])
+        first(2, banks[2])
+        apply_gate(2, banks[2])
+        first(3, banks[0])
+        apply_gate(3, banks[0])
+        turn(1, banks[3])
+        product(1, banks[3])
+        turn_a(0, banks[7])
+        relu_out(0, banks[7])
+        pool_product(0)
+        first(4, banks[1])
+        apply_gate(4, banks[1])
+        turn(2, banks[4])
+        product(2, banks[4])
+        first(5, banks[2])
+        apply_gate(5, banks[2])
+        turn(3, banks[5])
+        product(3, banks[5])
+        first(6, banks[0])
+        apply_gate(6, banks[0])
+        turn(4, banks[6])
+        product(4, banks[6])
+        words_back(0, banks[7])
+        first(7, banks[1])
+        apply_gate(7, banks[1])
+        turn(5, banks[3])
+        product(5, banks[3])
+        quantize(0, 4)
+        first(8, banks[2])
+        apply_gate(8, banks[2])
+        turn(6, banks[4])
+        product(6, banks[4])
+        first(9, banks[0])
+        apply_gate(9, banks[0])
+        turn(7, banks[5])
+        product(7, banks[5])
+        weave(9)
+        turn(8, banks[6])
+        product(8, banks[6])
+        warm(banks[2])
+        quantize(4, 8)
+        base_main(0, banks[1])
+        base_tails(0, 4, banks[2])
+        turn(9, banks[7])
+        product(9, banks[7])
+        base_main(1, banks[0])
+        second(0, 0, 4, banks[1])
+        quantize(8, 9)
+        quantize(9, 10)
+        second(0, 4, 8, banks[3], nc.vector.tensor_copy)
+        second(0, 8, 9, banks[4])
+        second(0, 9, 10, banks[5])
+        second(1, 0, 4, banks[2])
+        second(1, 4, 8, banks[0])
+        second(1, 8, 10, banks[6])
+        base_main(2, banks[2])
+        base_main(3, banks[0])
+        second(2, 0, 4, banks[3])
+        second(2, 4, 8, banks[7])
+        second(2, 8, 10, banks[1])
+        second(3, 0, 4, banks[4])
+        second(3, 4, 8, banks[5])
+        second(3, 8, 10, banks[5])
+
+        for t0, t1 in TOKEN_PIECES:
+            gather_add(part[0], 0, pos1_sb, base[:, 0, :], t0, t1)
+        for t0, t1 in TOKEN_PIECES:
+            gather_add(res[0], 0, pos2_sb, part[0], t0, t1)
+        store(0, 0, T)
+        gather_add(part[1], 1, pos1_sb, base[:, 1, :], 0, T)
+        for c in (1, 2):
+            gather_add(part[c + 1], c + 1, pos1_sb, base[:, c + 1, :], 0, T)
+            if c == 1:
+                middle = keep.tile([P, 2, T], F32, name="res_middle", tag="waw2_0", align_bytes=64)
+                res[1], res[2] = middle[:, 0, :], middle[:, 1, :]
+            gather_add(res[c], c, pos2_sb, part[c], 0, T)
+            store(c, 0, T)
+        for t0, t1 in LAST_PIECES:
+            gather_add(res[3], 3, pos2_sb, part[3], t0, t1)
+            store(3, t0, t1)

@@ -57,7 +57,7 @@ def tile_moe_adb_relu2_kernel(
         wbw = [keep.tile([P, hi - lo, H], I32, name="wbw%d" % lo, align_bytes=64) for lo, hi in WB_CUTS]
         wbs = keep.tile([P, E, H], U8, name="wbs", align_bytes=64)
         waw = [
-            keep.tile([P, e1 - e0, (c1 - c0) * P], I32, name="waw%d_%d" % (c0, e0), tag="waw%d_%d" % (c0, e0), align_bytes=64)
+            keep.tile([P, e1 - e0, (c1 - c0) * P], I32, name="waw%d_%d" % (c0, e0), align_bytes=64)
             for c0, c1, e0, e1 in WA_CUTS
         ]
         was = [keep.tile([P, E, (hi - lo) * P], U8, name="was%d" % lo, align_bytes=64) for lo, hi in WAS_CUTS]
@@ -77,7 +77,7 @@ def tile_moe_adb_relu2_kernel(
         base = keep.tile([P, CHUNKS, T], F32, name="base")
         dx = [keep.tile([P, S], F32, name="dx%d" % c) for c in range(CHUNKS)]
         part = [keep.tile([P, T], F32, name="part%d" % c) for c in range(CHUNKS)]
-        res = {c: keep.tile([P, T], F32, name="res%d" % c) for c in (0, 3)}
+        res = [keep.tile([P, T], F32, name="res%d" % c) for c in range(CHUNKS)]
         banks = [psum.tile([P, BANK], F32, name="bank%d" % n) for n in range(8)]
 
         wb_src = wbt_words.rearrange("e o p n d -> p (e o) (n d)").bitcast(I32)
@@ -330,43 +330,42 @@ def tile_moe_adb_relu2_kernel(
         turn(8, banks[6])
         product(8, banks[6])
         warm(banks[2])
-        quantize(4, 8)
-        base_main(0, banks[1])
-        base_tails(0, 4, banks[2])
         turn(9, banks[7])
+        quantize(4, 8)
         product(9, banks[7])
-        base_main(1, banks[0])
+        base_main(0, banks[0])
+        base_tails(0, 1, banks[2])
+        warm(banks[5])
         second(0, 0, 4, banks[1])
         quantize(8, 9)
         quantize(9, 10)
         second(0, 4, 8, banks[3], nc.vector.tensor_copy)
         second(0, 8, 9, banks[4])
         second(0, 9, 10, banks[5])
-        second(1, 0, 4, banks[2])
-        second(1, 4, 8, banks[0])
+        second(1, 0, 4, banks[0])
+        second(1, 4, 8, banks[2])
         second(1, 8, 10, banks[6])
-        base_main(2, banks[2])
-        base_main(3, banks[0])
-        second(2, 0, 4, banks[3])
-        second(2, 4, 8, banks[7])
-        second(2, 8, 10, banks[1])
+        base_main(1, banks[1])
+        base_tails(1, 4, banks[3])
+        base_main(2, banks[0])
+        base_main(3, banks[2])
+        second(2, 0, 4, banks[7])
         second(3, 0, 4, banks[4])
-        second(3, 4, 8, banks[5])
-        second(3, 8, 10, banks[5])
+        second(2, 4, 8, banks[5])
+        second(3, 4, 8, banks[1])
+        second(2, 8, 10, banks[6])
+        second(3, 8, 10, banks[3])
 
-        for t0, t1 in TOKEN_PIECES:
-            gather_add(part[0], 0, pos1_sb, base[:, 0, :], t0, t1)
-        for t0, t1 in TOKEN_PIECES:
-            gather_add(res[0], 0, pos2_sb, part[0], t0, t1)
-        store(0, 0, T)
-        gather_add(part[1], 1, pos1_sb, base[:, 1, :], 0, T)
-        for c in (1, 2):
-            gather_add(part[c + 1], c + 1, pos1_sb, base[:, c + 1, :], 0, T)
-            if c == 1:
-                middle = keep.tile([P, 2, T], F32, name="res_middle", tag="waw2_0", align_bytes=64)
-                res[1], res[2] = middle[:, 0, :], middle[:, 1, :]
-            gather_add(res[c], c, pos2_sb, part[c], 0, T)
+        for c in (0, 1):
+            for t0, t1 in TOKEN_PIECES:
+                gather_add(part[c], c, pos1_sb, base[:, c, :], t0, t1)
+            for t0, t1 in TOKEN_PIECES:
+                gather_add(res[c], c, pos2_sb, part[c], t0, t1)
             store(c, 0, T)
+        for c in (2, 3):
+            gather_add(part[c], c, pos1_sb, base[:, c, :], 0, T)
+        gather_add(res[2], 2, pos2_sb, part[2], 0, T)
+        store(2, 0, T)
         for t0, t1 in LAST_PIECES:
             gather_add(res[3], 3, pos2_sb, part[3], t0, t1)
             store(3, t0, t1)

@@ -29,14 +29,15 @@ ALU = mybir.AluOpType
 GATHER_CUTS = ((0, 3), (3, 6), (6, 10))
 A_CUTS = ((0, 2), (2, 5), (5, 7), (7, 10))
 WB_CUTS = ((0, 2), (2, 3), (3, 4), (4, 5))
-WA_CUTS = ((0, 1, 0, 2), (0, 1, 2, 5), (1, 2, 0, 5), (2, 4, 0, 5))
+WA_CUTS = ((0, 1, 0, 2), (0, 1, 2, 5), (1, 2, 0, 5), (2, 3, 0, 5), (3, 4, 0, 5))
 DH_TILES = ((0, 4, 0), (4, 8, 8), (8, 10, 9))
 POOL_GROUPS = (0,)
 WOVEN_GROUPS = (9,)
 WAS_CUTS = ((0, 4),)
 WT_CUTS = ((0, 4),)
 TOKEN_PIECES = ((0, 384), (384, T))
-LAST_PIECES = ((0, 448), (448, T))
+BANK_PIECES = ((0, BANK), (BANK, T))
+LAST_PIECES = ((0, 320), (320, BANK), (BANK, T))
 
 
 def tile_moe_adb_relu2_kernel(
@@ -74,9 +75,10 @@ def tile_moe_adb_relu2_kernel(
         dh = keep.tile([P, S * PACK], BF16, name="dh", align_bytes=64)
         dhw = {}
         dhs = keep.tile([P, S], U8, name="dhs", align_bytes=64)
-        base = keep.tile([P, CHUNKS, T], F32, name="base")
+        base0 = keep.tile([P, T], F32, name="base0")
         dx = [keep.tile([P, S], F32, name="dx%d" % c) for c in range(CHUNKS)]
-        part = [keep.tile([P, T], F32, name="part%d" % c) for c in range(CHUNKS)]
+        part = [keep.tile([P, T], F32, name="part%d" % c) for c in range(2)] * 2
+        picked = [keep.tile([P, T], F32, name="picked%d" % c) for c in range(CHUNKS)]
         res = [keep.tile([P, T], F32, name="res%d" % c) for c in range(CHUNKS)]
         banks = [psum.tile([P, BANK], F32, name="bank%d" % n) for n in range(8)]
 
@@ -233,14 +235,16 @@ def tile_moe_adb_relu2_kernel(
                 rhs=dyw[:, t0:t1].bitcast(FP8X4), rhs_scale=dys[:, t0:t1], start=True, stop=True,
             )
 
-        def base_main(c, acc, copy=nc.scalar.copy):
-            base_pass(c, 0, BANK, acc[:])
-            copy(base[:, c, 0:BANK], acc[:])
+        def base_out(main, tail):
+            base_pass(0, 0, BANK, main[:])
+            nc.scalar.copy(base0[:, 0:BANK], main[:])
+            for c in range(CHUNKS):
+                base_pass(c, BANK, T, tail[:, c * P : (c + 1) * P])
+            nc.scalar.copy(base0[:, BANK:T], tail[:, 0:P])
 
-        def base_tails(lo, hi, acc, copy=nc.scalar.copy):
-            for c in range(lo, hi):
-                base_pass(c, BANK, T, acc[:, (c - lo) * P : (c - lo + 1) * P])
-            copy(base[:, lo:hi, BANK:T], acc[:, 0 : (hi - lo) * P].rearrange("p (c t) -> p c t", t=P))
+        def pick(c, t0, t1):
+            entries = pos1_sb[:, t0 // PER_COL : t1 // PER_COL]
+            nc.scalar.activation(picked[c][:, t0:t1], dx[c][:].indirect(entries), COPY)
 
         def gather_add(dst, c, pos_sb, other, t0, t1):
             entries = pos_sb[:, t0 // PER_COL : t1 // PER_COL]
@@ -279,6 +283,7 @@ def tile_moe_adb_relu2_kernel(
         load_wa(2)
         nc.sync.dma_start(pos2_sb[:], pos2)
         load_wa(3)
+        load_wa(4)
 
         nc.tensor.transpose(banks[7][:, 0:P], gate_rows[:], ident[:])
         nc.scalar.activation(gate2[:], banks[7][:, 0:GROUPS], COPY, scale=2.0)
@@ -333,39 +338,55 @@ def tile_moe_adb_relu2_kernel(
         turn(9, banks[7])
         quantize(4, 8)
         product(9, banks[7])
-        base_main(0, banks[0])
-        base_tails(0, 1, banks[2])
-        warm(banks[5])
-        second(0, 0, 4, banks[1])
+        tails = banks[5]
+        base_out(banks[0], tails)
+        second(0, 0, 4, banks[6])
         quantize(8, 9)
         quantize(9, 10)
-        second(0, 4, 8, banks[3], nc.vector.tensor_copy)
+        second(0, 4, 8, banks[7], nc.vector.tensor_copy)
         second(0, 8, 9, banks[4])
-        second(0, 9, 10, banks[5])
-        second(1, 0, 4, banks[0])
-        second(1, 4, 8, banks[2])
-        second(1, 8, 10, banks[6])
-        base_main(1, banks[1])
-        base_tails(1, 4, banks[3])
-        base_main(2, banks[0])
-        base_main(3, banks[2])
-        second(2, 0, 4, banks[7])
-        second(3, 0, 4, banks[4])
-        second(2, 4, 8, banks[5])
-        second(3, 4, 8, banks[1])
-        second(2, 8, 10, banks[6])
-        second(3, 8, 10, banks[3])
+        second(0, 9, 10, banks[3])
+        second(1, 8, 10, banks[2])
+        second(1, 0, 4, banks[4])
+        second(1, 4, 8, banks[3])
+        base_bank = banks[2]
+        base_pass(1, 0, BANK, base_bank[:])
 
-        for c in (0, 1):
-            for t0, t1 in TOKEN_PIECES:
-                gather_add(part[c], c, pos1_sb, base[:, c, :], t0, t1)
-            for t0, t1 in TOKEN_PIECES:
-                gather_add(res[c], c, pos2_sb, part[c], t0, t1)
+        for t0, t1 in TOKEN_PIECES:
+            gather_add(part[0], 0, pos1_sb, base0, t0, t1)
+        for t0, t1 in TOKEN_PIECES:
+            gather_add(res[0], 0, pos2_sb, part[0], t0, t1)
+        store(0, 0, T)
+
+        def add_base(c, t0, t1):
+            src = base_bank[:, t0:t1] if t1 <= BANK else tails[:, c * P : (c + 1) * P]
+            nc.vector.tensor_tensor(res[c][:, t0:t1], part[c][:, t0:t1], src, ALU.add)
+
+        def finish(c):
+            for t0, t1 in BANK_PIECES:
+                gather_add(part[c], c, pos2_sb, picked[c], t0, t1)
+            for t0, t1 in BANK_PIECES:
+                add_base(c, t0, t1)
             store(c, 0, T)
-        for c in (2, 3):
-            gather_add(part[c], c, pos1_sb, base[:, c, :], 0, T)
-        gather_add(res[2], 2, pos2_sb, part[2], 0, T)
-        store(2, 0, T)
+
+        pick(1, 0, T)
+        second(2, 8, 10, banks[4])
+        second(2, 0, 4, banks[3])
+        second(2, 4, 8, banks[4])
+        finish(1)
+        base_pass(2, 0, BANK, base_bank[:])
+        pick(2, 0, T)
+        second(3, 8, 10, banks[3])
+        second(3, 0, 4, banks[4])
+        second(3, 4, 8, banks[3])
+        finish(2)
+        base_pass(3, 0, BANK, base_bank[:])
         for t0, t1 in LAST_PIECES:
-            gather_add(res[3], 3, pos2_sb, part[3], t0, t1)
-            store(3, t0, t1)
+            pick(3, t0, t1)
+        for n, (t0, t1) in enumerate(LAST_PIECES):
+            gather_add(part[3], 3, pos2_sb, picked[3], t0, t1)
+            if n > 0:
+                add_base(3, *LAST_PIECES[n - 1])
+        store(3, 0, BANK)
+        add_base(3, BANK, T)
+        store(3, BANK, T)

@@ -29,7 +29,7 @@ ALU = mybir.AluOpType
 GATHER_CUTS = ((0, 3), (3, 6), (6, 10))
 A_CUTS = ((0, 2), (2, 5), (5, 7), (7, 10))
 WB_CUTS = ((0, 2), (2, 3), (3, 4), (4, 5))
-WA_CUTS = ((0, 1, 0, 2), (0, 1, 2, 5), (1, 2, 0, 5), (2, 3, 0, 5), (3, 4, 0, 5))
+WA_CUTS = ((0, 2, 0, 2), (0, 2, 2, 4), (0, 2, 4, 5), (2, 3, 0, 5), (3, 4, 0, 5))
 DH_TILES = ((0, 4, 0), (4, 8, 8), (8, 10, 9))
 POOL_GROUPS = (0,)
 WOVEN_GROUPS = (9,)
@@ -72,10 +72,9 @@ def tile_moe_adb_relu2_kernel(
         relu_rows = {b: keep.tile([P, H], F32, name="relu%d" % b) for b in POOL_GROUPS}
         relu_woven = {b: keep.tile([P, H], F32, name="woven%d" % b) for b in WOVEN_GROUPS}
         dh_rows = {b: keep.tile([P, H], BF16, name="rows%d" % b, align_bytes=64) for b in POOL_GROUPS}
-        dh = keep.tile([P, S * PACK], BF16, name="dh", align_bytes=64)
+        dh = keep.tile([P, S * PACK], BF16, name="dh", tag="dh", align_bytes=64)
         dhw = {}
         dhs = keep.tile([P, S], U8, name="dhs", align_bytes=64)
-        base0 = keep.tile([P, T], F32, name="base0")
         dx = [keep.tile([P, S], F32, name="dx%d" % c) for c in range(CHUNKS)]
         part = [keep.tile([P, T], F32, name="part%d" % c) for c in range(2)] * 2
         picked = [keep.tile([P, T], F32, name="picked%d" % c) for c in range(CHUNKS)]
@@ -235,13 +234,6 @@ def tile_moe_adb_relu2_kernel(
                 rhs=dyw[:, t0:t1].bitcast(FP8X4), rhs_scale=dys[:, t0:t1], start=True, stop=True,
             )
 
-        def base_out(main, tail):
-            base_pass(0, 0, BANK, main[:])
-            nc.scalar.copy(base0[:, 0:BANK], main[:])
-            for c in range(CHUNKS):
-                base_pass(c, BANK, T, tail[:, c * P : (c + 1) * P])
-            nc.scalar.copy(base0[:, BANK:T], tail[:, 0:P])
-
         def pick(c, t0, t1):
             entries = pos1_sb[:, t0 // PER_COL : t1 // PER_COL]
             nc.scalar.activation(picked[c][:, t0:t1], dx[c][:].indirect(entries), COPY)
@@ -279,8 +271,8 @@ def tile_moe_adb_relu2_kernel(
         load_was(0)
         load_wa(0)
         load_wa(1)
-        nc.sync.dma_start(pos1_sb[:], pos1)
         load_wa(2)
+        nc.sync.dma_start(pos1_sb[:], pos1)
         nc.sync.dma_start(pos2_sb[:], pos2)
         load_wa(3)
         load_wa(4)
@@ -339,18 +331,23 @@ def tile_moe_adb_relu2_kernel(
         quantize(4, 8)
         product(9, banks[7])
         tails = banks[5]
-        base_out(banks[0], tails)
-        second(0, 0, 4, banks[6])
+        second(0, 0, 4, banks[0])
+        second(1, 0, 4, banks[1])
+        base_pass(0, 0, BANK, banks[6][:])
+        for c in range(CHUNKS):
+            base_pass(c, BANK, T, tails[:, c * P : (c + 1) * P])
+        second(1, 4, 8, banks[2])
         quantize(8, 9)
         quantize(9, 10)
+        base0 = keep.tile([P, T], F32, name="base0", tag="dh", align_bytes=64)
+        nc.vector.tensor_copy(base0[:, 0:BANK], banks[6][:])
+        nc.vector.tensor_copy(base0[:, BANK:T], tails[:, 0:P])
         second(0, 4, 8, banks[7], nc.vector.tensor_copy)
         second(0, 8, 9, banks[4])
         second(0, 9, 10, banks[3])
-        second(1, 8, 10, banks[2])
-        second(1, 0, 4, banks[4])
-        second(1, 4, 8, banks[3])
-        base_bank = banks[2]
-        base_pass(1, 0, BANK, base_bank[:])
+        second(1, 8, 10, banks[0])
+        base_bank = {1: banks[0], 2: banks[4], 3: banks[3]}
+        base_pass(1, 0, BANK, base_bank[1][:])
 
         for t0, t1 in TOKEN_PIECES:
             gather_add(part[0], 0, pos1_sb, base0, t0, t1)
@@ -359,7 +356,7 @@ def tile_moe_adb_relu2_kernel(
         store(0, 0, T)
 
         def add_base(c, t0, t1):
-            src = base_bank[:, t0:t1] if t1 <= BANK else tails[:, c * P : (c + 1) * P]
+            src = base_bank[c][:, t0:t1] if t1 <= BANK else tails[:, c * P : (c + 1) * P]
             nc.vector.tensor_tensor(res[c][:, t0:t1], part[c][:, t0:t1], src, ALU.add)
 
         def finish(c):
@@ -372,15 +369,15 @@ def tile_moe_adb_relu2_kernel(
         pick(1, 0, T)
         second(2, 8, 10, banks[4])
         second(2, 0, 4, banks[3])
-        second(2, 4, 8, banks[4])
+        second(2, 4, 8, banks[1])
+        for c in (2, 3):
+            base_pass(c, 0, BANK, base_bank[c][:])
         finish(1)
-        base_pass(2, 0, BANK, base_bank[:])
         pick(2, 0, T)
-        second(3, 8, 10, banks[3])
-        second(3, 0, 4, banks[4])
-        second(3, 4, 8, banks[3])
+        second(3, 8, 10, banks[2])
+        second(3, 0, 4, banks[6])
+        second(3, 4, 8, banks[7])
         finish(2)
-        base_pass(3, 0, BANK, base_bank[:])
         for t0, t1 in LAST_PIECES:
             pick(3, t0, t1)
         for n, (t0, t1) in enumerate(LAST_PIECES):

@@ -33,7 +33,7 @@ WA_CUTS = ((0, 2, 0, 2), (0, 2, 2, 4), (0, 2, 4, 5), (2, 3, 0, 5), (3, 4, 0, 5))
 DH_TILES = ((0, 4, 0), (4, 8, 8), (8, 10, 9))
 POOL_GROUPS = (0,)
 WOVEN_GROUPS = (9,)
-WAS_CUTS = ((0, 4),)
+WAS_CUTS = ((0, 2), (2, 4))
 WT_CUTS = ((0, 4),)
 TOKEN_PIECES = ((0, 384), (384, T))
 BANK_PIECES = ((0, BANK), (BANK, T))
@@ -72,7 +72,8 @@ def tile_moe_adb_relu2_kernel(
         relu_rows = {b: keep.tile([P, H], F32, name="relu%d" % b) for b in POOL_GROUPS}
         relu_woven = {b: keep.tile([P, H], F32, name="woven%d" % b) for b in WOVEN_GROUPS}
         dh_rows = {b: keep.tile([P, H], BF16, name="rows%d" % b, align_bytes=64) for b in POOL_GROUPS}
-        dh = keep.tile([P, S * PACK], BF16, name="dh", tag="dh", align_bytes=64)
+        dh = keep.tile([P, S * PACK], BF16, name="dh", align_bytes=64)
+        base0 = keep.tile([P, T], F32, name="base0")
         dhw = {}
         dhs = keep.tile([P, S], U8, name="dhs", align_bytes=64)
         dx = [keep.tile([P, S], F32, name="dx%d" % c) for c in range(CHUNKS)]
@@ -249,7 +250,8 @@ def tile_moe_adb_relu2_kernel(
         nc.vector.memset(dyw[:, T:WINDOW], 0)
         nc.vector.memset(gate_rows[:].bitcast(I32), 0)
         nc.vector.memset(wbs[:].rearrange("p e n -> p (e n)").bitcast(I32), 0)
-        nc.vector.memset(was[0][:].rearrange("p e n -> p (e n)").bitcast(I32), 0)
+        for tile in was:
+            nc.vector.memset(tile[:].rearrange("p e n -> p (e n)").bitcast(I32), 0)
         nc.vector.memset(wts[:].bitcast(I32), 0)
         make_identity(nc, ident[:])
 
@@ -275,11 +277,12 @@ def tile_moe_adb_relu2_kernel(
         nc.sync.dma_start(pos1_sb[:], pos1)
         nc.sync.dma_start(pos2_sb[:], pos2)
         load_wa(3)
+        load_was(1)
         load_wa(4)
 
         nc.tensor.transpose(banks[7][:, 0:P], gate_rows[:], ident[:])
         nc.scalar.activation(gate2[:], banks[7][:, 0:GROUPS], COPY, scale=2.0)
-        for n in range(4):
+        for n in range(2):
             warm(banks[3])
         for n in range(len(GATHER_CUTS)):
             gather_in(n)
@@ -326,25 +329,23 @@ def tile_moe_adb_relu2_kernel(
         weave(9)
         turn(8, banks[6])
         product(8, banks[6])
-        warm(banks[2])
+        base_pass(0, 0, BANK, banks[2][:])
+        nc.scalar.copy(base0[:, 0:BANK], banks[2][:])
         turn(9, banks[7])
         quantize(4, 8)
         product(9, banks[7])
         tails = banks[5]
-        second(0, 0, 4, banks[0])
-        second(1, 0, 4, banks[1])
-        base_pass(0, 0, BANK, banks[6][:])
         for c in range(CHUNKS):
             base_pass(c, BANK, T, tails[:, c * P : (c + 1) * P])
+        nc.scalar.copy(base0[:, BANK:T], tails[:, 0:P])
+        second(0, 0, 4, banks[0])
+        second(1, 0, 4, banks[1])
         second(1, 4, 8, banks[2])
         quantize(8, 9)
         quantize(9, 10)
-        base0 = keep.tile([P, T], F32, name="base0", tag="dh", align_bytes=64)
-        nc.vector.tensor_copy(base0[:, 0:BANK], banks[6][:])
-        nc.vector.tensor_copy(base0[:, BANK:T], tails[:, 0:P])
         second(0, 4, 8, banks[7], nc.vector.tensor_copy)
         second(0, 8, 9, banks[4])
-        second(0, 9, 10, banks[3])
+        second(0, 9, 10, banks[3], nc.vector.tensor_copy)
         second(1, 8, 10, banks[0])
         base_bank = {1: banks[0], 2: banks[4], 3: banks[3]}
         base_pass(1, 0, BANK, base_bank[1][:])

@@ -9,6 +9,7 @@ P = 128
 PACK = 4
 BANK = 512
 PER_COL = 16
+SCALE_ROWS = 4
 CHUNKS = K // P
 GROUPS = S // P
 WINDOW = 768
@@ -30,14 +31,19 @@ GATHER_CUTS = ((0, 3), (3, 6), (6, 10))
 A_CUTS = ((0, 2), (2, 5), (5, 7), (7, 10))
 WB_CUTS = ((0, 2), (2, 3), (3, 4), (4, 5))
 WA_CUTS = ((0, 2, 0, 2), (0, 2, 2, 4), (0, 2, 4, 5), (2, 3, 0, 5), (3, 4, 0, 5))
-DH_TILES = ((0, 4, 0), (4, 8, 8), (8, 10, 9))
-POOL_GROUPS = (0,)
-WOVEN_GROUPS = (9,)
 WAS_CUTS = ((0, 2), (2, 4))
-WT_CUTS = ((0, 4),)
+DH_TILES = ((0, 4, 0), (4, 8, 8), (8, 10, 9))
+POOL_GROUP = 0
+WOVEN_GROUP = GROUPS - 1
+AHEAD = 2
+WARM_UPS = 2
 TOKEN_PIECES = ((0, 384), (384, T))
 BANK_PIECES = ((0, BANK), (BANK, T))
 LAST_PIECES = ((0, 320), (320, BANK), (BANK, T))
+
+
+def cut_of(cuts, x):
+    return [n for n, cut in enumerate(cuts) if cut[0] <= x < cut[1]][0]
 
 
 def tile_moe_adb_relu2_kernel(
@@ -53,7 +59,7 @@ def tile_moe_adb_relu2_kernel(
         pos2_sb = keep.tile([P, T // PER_COL], U16, name="pos2_sb")
         dyw = keep.tile([P, WINDOW], I32, name="dyw", align_bytes=64)
         dys = keep.tile([P, WINDOW], U8, name="dys", align_bytes=64)
-        wtw = [keep.tile([P, 2 * (hi - lo) * P], U8, name="wtw%d" % lo, align_bytes=64) for lo, hi in WT_CUTS]
+        wtw = keep.tile([P, 2 * K], U8, name="wtw", align_bytes=64)
         wts = keep.tile([P, K], U8, name="wts", align_bytes=64)
         wbw = [keep.tile([P, hi - lo, H], I32, name="wbw%d" % lo, align_bytes=64) for lo, hi in WB_CUTS]
         wbs = keep.tile([P, E, H], U8, name="wbs", align_bytes=64)
@@ -69,16 +75,16 @@ def tile_moe_adb_relu2_kernel(
         xw = keep.tile([P, S], U32, name="xw", align_bytes=64)
         xs = keep.tile([P, S], U8, name="xs", align_bytes=64)
         gated = [keep.tile([P, H], F32, name="gated%d" % b, tag="gated%d" % b, align_bytes=64) for b in range(GROUPS)]
-        relu_rows = {b: keep.tile([P, H], F32, name="relu%d" % b) for b in POOL_GROUPS}
-        relu_woven = {b: keep.tile([P, H], F32, name="woven%d" % b) for b in WOVEN_GROUPS}
-        dh_rows = {b: keep.tile([P, H], BF16, name="rows%d" % b, align_bytes=64) for b in POOL_GROUPS}
+        relu_rows = keep.tile([P, H], F32, name="relu_rows")
+        relu_woven = keep.tile([P, H], F32, name="relu_woven")
+        dh_rows = keep.tile([P, H], BF16, name="dh_rows", align_bytes=64)
         dh = keep.tile([P, S * PACK], BF16, name="dh", align_bytes=64)
         base0 = keep.tile([P, T], F32, name="base0")
         dhw = {}
         dhs = keep.tile([P, S], U8, name="dhs", align_bytes=64)
         dx = [keep.tile([P, S], F32, name="dx%d" % c) for c in range(CHUNKS)]
         part = [keep.tile([P, T], F32, name="part%d" % c) for c in range(2)] * 2
-        picked = [keep.tile([P, T], F32, name="picked%d" % c) for c in range(CHUNKS)]
+        picked = {c: keep.tile([P, T], F32, name="picked%d" % c) for c in range(1, CHUNKS)}
         res = [keep.tile([P, T], F32, name="res%d" % c) for c in range(CHUNKS)]
         banks = [psum.tile([P, BANK], F32, name="bank%d" % n) for n in range(8)]
 
@@ -88,15 +94,13 @@ def tile_moe_adb_relu2_kernel(
         wbs_src = wbt_scales.rearrange("e o r n -> r (e o) n")
         was_src = wat_scales.rearrange("e o r n -> r (e o) n")
 
-        def load_scale_rows(tile, rows, r, queue=nc.sync):
+        def load_scales(tile, rows, queues=(nc.sync,) * SCALE_ROWS):
             rest = (slice(None),) * (len(rows.shape) - 1)
-            queue.dma_start(
-                out=tile[(slice(r, P, 32),) + rest].bitcast(I32), in_=rows[(slice(r, 16, 4),) + rest].bitcast(I32)
-            )
-
-        def load_scales(tile, rows, queues):
-            for r in range(4):
-                load_scale_rows(tile, rows, r, queues[r])
+            for r, queue in enumerate(queues):
+                queue.dma_start(
+                    out=tile[(slice(r, P, 32),) + rest].bitcast(I32),
+                    in_=rows[(slice(r, 16, SCALE_ROWS),) + rest].bitcast(I32),
+                )
 
         def load_a(n):
             lo, hi = A_CUTS[n]
@@ -112,34 +116,17 @@ def tile_moe_adb_relu2_kernel(
 
         def load_was(n):
             lo, hi = WAS_CUTS[n]
-            load_scales(was[n], was_src[:, :, lo * P : hi * P], (nc.sync,) * 4)
+            load_scales(was[n], was_src[:, :, lo * P : hi * P])
 
-        def load_wt(n):
-            lo, hi = WT_CUTS[n]
-            nc.sync.dma_start(out=wtw[n][:].bitcast(I32), in_=wt_words[0][:, 2 * lo * P : 2 * hi * P].bitcast(I32))
-
-        def warm(acc):
-            nc.tensor.matmul_mx(
-                out=acc[:], lhsT=dyw[:, 0:P].bitcast(FP8X4), lhsT_scale=dys[:, 0:P],
-                rhs=dyw[:, 0:BANK].bitcast(FP8X4), rhs_scale=dys[:, 0:BANK], start=True, stop=True,
-            )
-
-        def gather_in(n):
-            lo, hi = GATHER_CUTS[n]
-            entries = offs_sb[:, lo * P // PER_COL : hi * P // PER_COL]
-            nc.vector.tensor_copy(xw[:, lo * P : hi * P], dyw[:].bitcast(U32).indirect(entries))
-            nc.vector.tensor_copy(xs[:, lo * P : hi * P], dys[:].indirect(entries))
-
-        def first(b, acc):
+        def first(b):
             e = b * P // C
-            n = [i for i, (lo, hi) in enumerate(WB_CUTS) if lo <= e < hi][0]
+            n = cut_of(WB_CUTS, e)
+            acc = banks[b % 3]
             nc.tensor.matmul_mx(
                 out=acc[:], lhsT=xw[:, b * P : (b + 1) * P].bitcast(FP8X4), lhsT_scale=xs[:, b * P : (b + 1) * P],
                 rhs=wbw[n][:, e - WB_CUTS[n][0], :].bitcast(FP8X4), rhs_scale=wbs[:, e, :], start=True, stop=True,
             )
-
-        def apply_gate(b, acc):
-            if b in POOL_GROUPS:
+            if b == POOL_GROUP:
                 dst = gated[b][:].rearrange("s (u m d) -> s u m d", u=2, d=2)
                 src = acc[:].rearrange("s (m u d) -> s u m d", u=2, d=2)
             else:
@@ -148,33 +135,28 @@ def tile_moe_adb_relu2_kernel(
             nc.scalar.activation(dst, src, COPY, scale=gate2[:, b : b + 1])
 
         def a_group(b):
-            n = [i for i, (lo, hi) in enumerate(A_CUTS) if lo <= b < hi][0]
+            n = cut_of(A_CUTS, b)
             s0 = (b - A_CUTS[n][0]) * P
             return a_sb[n][:, :, s0 : s0 + P]
 
-        def turn_a(b, turned):
-            for t in range(PACK):
-                nc.tensor.transpose(turned[:, t * P : (t + 1) * P], a_group(b)[:, t, :], ident[:])
+        def dh_group(b):
+            return dh[:, b * H : (b + 1) * H]
 
-        def relu_out(b, turned):
+        def pool_product(turned):
+            for t in range(PACK):
+                nc.tensor.transpose(turned[:, t * P : (t + 1) * P], a_group(POOL_GROUP)[:, t, :], ident[:])
             nc.scalar.activation(
-                relu_rows[b][:].rearrange("s (u m d) -> s u m d", u=2, d=2),
+                relu_rows[:].rearrange("s (u m d) -> s u m d", u=2, d=2),
                 turned[:].rearrange("s (u d m) -> s u m d", u=2, d=2), RELU,
             )
+            nc.gpsimd.tensor_tensor(dh_rows[:], gated[POOL_GROUP][:], relu_rows[:], ALU.mult)
 
-        def weave(b):
-            woven = relu_woven[b][:].rearrange("p (s t) -> p s t", t=PACK)
-            nc.scalar.activation(woven, a_group(b).rearrange("p t s -> p s t"), RELU)
-
-        def pool_product(b):
-            nc.gpsimd.tensor_tensor(dh_rows[b][:], gated[b][:], relu_rows[b][:], ALU.mult)
-
-        def words_back(b, turned):
-            words = dh_rows[b][:].bitcast(F32)
+        def pool_words_back(turned):
+            pairs = dh_rows[:].bitcast(F32)
             for u in range(2):
-                nc.tensor.transpose(turned[:, u * P : (u + 1) * P], words[:, u * P : (u + 1) * P], ident[:])
+                nc.tensor.transpose(turned[:, u * P : (u + 1) * P], pairs[:, u * P : (u + 1) * P], ident[:])
             nc.scalar.copy(
-                dh[:, b * H : (b + 1) * H].bitcast(F32).rearrange("p (s u) -> p s u", u=2),
+                dh_group(POOL_GROUP).bitcast(F32).rearrange("p (s u) -> p s u", u=2),
                 turned[:, 0 : 2 * P].rearrange("p (u s) -> p s u", u=2),
             )
 
@@ -183,55 +165,46 @@ def tile_moe_adb_relu2_kernel(
                 nc.tensor.transpose(turned[:, t * P : (t + 1) * P], gated[b][:, t * P : (t + 1) * P], ident[:])
 
         def product(b, turned):
-            if b in WOVEN_GROUPS:
-                nc.vector.tensor_tensor(
-                    dh[:, b * H : (b + 1) * H].rearrange("p (s t) -> p s t", t=PACK),
-                    relu_woven[b][:].rearrange("p (s t) -> p s t", t=PACK),
-                    turned[:].rearrange("p (t s) -> p s t", t=PACK), ALU.mult,
+            dst = dh_group(b).rearrange("p (s t) -> p s t", t=PACK)
+            sums = turned[:].rearrange("p (t s) -> p s t", t=PACK)
+            if b == WOVEN_GROUP:
+                nc.vector.tensor_tensor(dst, relu_woven[:].rearrange("p (s t) -> p s t", t=PACK), sums, ALU.mult)
+            else:
+                nc.vector.scalar_tensor_tensor(
+                    out=dst, in0=a_group(b).rearrange("p t s -> p s t"), scalar=0.0, in1=sums, op0=ALU.max, op1=ALU.mult
                 )
-                return
-            nc.vector.scalar_tensor_tensor(
-                out=dh[:, b * H : (b + 1) * H].rearrange("p (s t) -> p s t", t=PACK),
-                in0=a_group(b).rearrange("p t s -> p s t"),
-                scalar=0.0,
-                in1=turned[:].rearrange("p (t s) -> p s t", t=PACK),
-                op0=ALU.max,
-                op1=ALU.mult,
-            )
 
         def dh_words(s0, s1):
-            lo = [g0 for g0, g1, holder in DH_TILES if g0 * P <= s0 and s1 <= g1 * P][0]
+            lo = DH_TILES[cut_of(DH_TILES, s0 // P)][0]
             return dhw[lo][:, s0 - lo * P : s1 - lo * P]
 
         def quantize(lo, hi):
-            for g0, g1, holder in DH_TILES:
-                if g0 <= lo < g1 and g0 not in dhw:
-                    dhw[g0] = keep.tile([P, (g1 - g0) * P], U32, name="dhw%d" % g0, tag="gated%d" % holder, align_bytes=64)
+            g0, g1, holder = DH_TILES[cut_of(DH_TILES, lo)]
+            if lo == g0:
+                dhw[g0] = keep.tile([P, (g1 - g0) * P], U32, name="dhw%d" % g0, tag="gated%d" % holder, align_bytes=64)
             nc.vector.quantize_mx(
                 out=dh_words(lo * P, hi * P).bitcast(FP8X4), scales=dhs[:, lo * P : hi * P], in_=dh[:, lo * H : hi * H]
             )
 
         def second(c, lo, hi, acc, copy=nc.scalar.copy):
             edges = [lo * P] + [x for x in range(0, S, C) if lo * P < x < hi * P] + [hi * P]
+            m = cut_of(WAS_CUTS, c)
+            sc = c - WAS_CUTS[m][0]
             for s0, s1 in zip(edges[:-1], edges[1:]):
                 e = s0 // C
                 n = [i for i, (c0, c1, e0, e1) in enumerate(WA_CUTS) if c0 <= c < c1 and e0 <= e < e1][0]
-                c0, e0 = WA_CUTS[n][0], WA_CUTS[n][2]
-                m = [i for i, (s_lo, s_hi) in enumerate(WAS_CUTS) if s_lo <= c < s_hi][0]
-                sc = c - WAS_CUTS[m][0]
+                wc, we = c - WA_CUTS[n][0], e - WA_CUTS[n][2]
                 nc.tensor.matmul_mx(
                     out=acc[:, s0 - lo * P : s1 - lo * P],
-                    lhsT=waw[n][:, e - e0, (c - c0) * P : (c - c0 + 1) * P].bitcast(FP8X4),
+                    lhsT=waw[n][:, we, wc * P : (wc + 1) * P].bitcast(FP8X4),
                     lhsT_scale=was[m][:, e, sc * P : (sc + 1) * P],
                     rhs=dh_words(s0, s1).bitcast(FP8X4), rhs_scale=dhs[:, s0:s1], start=True, stop=True,
                 )
             copy(dx[c][:, lo * P : hi * P], acc[:, 0 : (hi - lo) * P])
 
         def base_pass(c, t0, t1, dst):
-            n = [i for i, (lo, hi) in enumerate(WT_CUTS) if lo <= c < hi][0]
-            c0 = c - WT_CUTS[n][0]
             nc.tensor.matmul_mx(
-                out=dst, lhsT=wtw[n][:, 2 * c0 * P : 2 * (c0 + 1) * P].bitcast(FP4X4), lhsT_scale=wts[:, c * P : (c + 1) * P],
+                out=dst, lhsT=wtw[:, 2 * c * P : 2 * (c + 1) * P].bitcast(FP4X4), lhsT_scale=wts[:, c * P : (c + 1) * P],
                 rhs=dyw[:, t0:t1].bitcast(FP8X4), rhs_scale=dys[:, t0:t1], start=True, stop=True,
             )
 
@@ -246,7 +219,7 @@ def tile_moe_adb_relu2_kernel(
         def store(c, t0, t1):
             nc.sync.dma_start(out=out[c * P : (c + 1) * P, t0:t1], in_=res[c][:, t0:t1])
 
-        nc.vector.memset(dys[:].bitcast(I32), 0)
+        nc.gpsimd.memset(dys[:].bitcast(I32), 0)
         nc.vector.memset(dyw[:, T:WINDOW], 0)
         nc.vector.memset(gate_rows[:].bitcast(I32), 0)
         nc.vector.memset(wbs[:].rearrange("p e n -> p (e n)").bitcast(I32), 0)
@@ -260,20 +233,19 @@ def tile_moe_adb_relu2_kernel(
         nc.sync.dma_start(offs_sb[:], offs)
         load_wb(0)
         nc.sync.dma_start(out=gate_rows[0:GROUPS, :], in_=gate[0].rearrange("(b p) -> b p", p=P))
-        load_scales(wbs, wbs_src, (nc.sync,) * 4)
+        load_scales(wbs, wbs_src)
         load_a(0)
         load_wb(1)
         load_wb(2)
         load_a(1)
         load_wb(3)
         load_a(2)
-        load_scales(wts, wt_scales[0], (nc.sync,) * 4)
+        load_scales(wts, wt_scales[0])
         load_a(3)
-        load_wt(0)
+        nc.sync.dma_start(out=wtw[:].bitcast(I32), in_=wt_words[0].bitcast(I32))
         load_was(0)
-        load_wa(0)
-        load_wa(1)
-        load_wa(2)
+        for n in range(3):
+            load_wa(n)
         nc.sync.dma_start(pos1_sb[:], pos1)
         nc.sync.dma_start(pos2_sb[:], pos2)
         load_wa(3)
@@ -282,64 +254,47 @@ def tile_moe_adb_relu2_kernel(
 
         nc.tensor.transpose(banks[7][:, 0:P], gate_rows[:], ident[:])
         nc.scalar.activation(gate2[:], banks[7][:, 0:GROUPS], COPY, scale=2.0)
-        for n in range(2):
-            warm(banks[3])
-        for n in range(len(GATHER_CUTS)):
-            gather_in(n)
+        for n in range(WARM_UPS):
+            nc.tensor.matmul_mx(
+                out=banks[3][:], lhsT=dyw[:, 0:P].bitcast(FP8X4), lhsT_scale=dys[:, 0:P],
+                rhs=dyw[:, 0:BANK].bitcast(FP8X4), rhs_scale=dys[:, 0:BANK], start=True, stop=True,
+            )
+        for lo, hi in GATHER_CUTS:
+            entries = offs_sb[:, lo * P // PER_COL : hi * P // PER_COL]
+            nc.vector.tensor_copy(xw[:, lo * P : hi * P], dyw[:].bitcast(U32).indirect(entries))
+            nc.vector.tensor_copy(xs[:, lo * P : hi * P], dys[:].indirect(entries))
 
-        first(0, banks[0])
-        apply_gate(0, banks[0])
-        first(1, banks[1])
-        apply_gate(1, banks[1])
-        first(2, banks[2])
-        apply_gate(2, banks[2])
-        first(3, banks[0])
-        apply_gate(3, banks[0])
-        turn(1, banks[3])
-        product(1, banks[3])
-        turn_a(0, banks[7])
-        relu_out(0, banks[7])
-        pool_product(0)
-        first(4, banks[1])
-        apply_gate(4, banks[1])
-        turn(2, banks[4])
-        product(2, banks[4])
-        first(5, banks[2])
-        apply_gate(5, banks[2])
-        turn(3, banks[5])
-        product(3, banks[5])
-        first(6, banks[0])
-        apply_gate(6, banks[0])
-        turn(4, banks[6])
-        product(4, banks[6])
-        words_back(0, banks[7])
-        first(7, banks[1])
-        apply_gate(7, banks[1])
-        turn(5, banks[3])
-        product(5, banks[3])
-        quantize(0, 4)
-        first(8, banks[2])
-        apply_gate(8, banks[2])
-        turn(6, banks[4])
-        product(6, banks[4])
-        first(9, banks[0])
-        apply_gate(9, banks[0])
-        turn(7, banks[5])
-        product(7, banks[5])
-        weave(9)
-        turn(8, banks[6])
-        product(8, banks[6])
+        for b in range(AHEAD + 1):
+            first(b)
+        for b in range(1, GROUPS - 1):
+            if b + AHEAD < GROUPS:
+                first(b + AHEAD)
+            else:
+                woven = relu_woven[:].rearrange("p (s t) -> p s t", t=PACK)
+                nc.scalar.activation(woven, a_group(WOVEN_GROUP).rearrange("p t s -> p s t"), RELU)
+            turn(b, banks[3 + (b - 1) % 4])
+            product(b, banks[3 + (b - 1) % 4])
+            if b + 1 == A_CUTS[0][1]:
+                pool_product(banks[7])
+            if b + 1 == A_CUTS[1][1]:
+                pool_words_back(banks[7])
+            if b == A_CUTS[1][1]:
+                quantize(0, 4)
+
+        last = GROUPS - 1
         base_pass(0, 0, BANK, banks[2][:])
         nc.scalar.copy(base0[:, 0:BANK], banks[2][:])
-        turn(9, banks[7])
+        turn(last, banks[7])
         quantize(4, 8)
-        product(9, banks[7])
+        product(last, banks[7])
         tails = banks[5]
         for c in range(CHUNKS):
             base_pass(c, BANK, T, tails[:, c * P : (c + 1) * P])
         nc.scalar.copy(base0[:, BANK:T], tails[:, 0:P])
+        base_bank = {1: banks[1], 2: banks[4], 3: banks[3]}
+        base_pass(1, 0, BANK, base_bank[1][:])
         second(0, 0, 4, banks[0])
-        second(1, 0, 4, banks[1])
+        second(1, 0, 4, banks[6])
         second(1, 4, 8, banks[2])
         quantize(8, 9)
         quantize(9, 10)
@@ -347,8 +302,6 @@ def tile_moe_adb_relu2_kernel(
         second(0, 8, 9, banks[4])
         second(0, 9, 10, banks[3], nc.vector.tensor_copy)
         second(1, 8, 10, banks[0])
-        base_bank = {1: banks[0], 2: banks[4], 3: banks[3]}
-        base_pass(1, 0, BANK, base_bank[1][:])
 
         for t0, t1 in TOKEN_PIECES:
             gather_add(part[0], 0, pos1_sb, base0, t0, t1)
@@ -370,7 +323,7 @@ def tile_moe_adb_relu2_kernel(
         pick(1, 0, T)
         second(2, 8, 10, banks[4])
         second(2, 0, 4, banks[3])
-        second(2, 4, 8, banks[1])
+        second(2, 4, 8, banks[0])
         for c in (2, 3):
             base_pass(c, 0, BANK, base_bank[c][:])
         finish(1)
@@ -385,6 +338,6 @@ def tile_moe_adb_relu2_kernel(
             gather_add(part[3], 3, pos2_sb, picked[3], t0, t1)
             if n > 0:
                 add_base(3, *LAST_PIECES[n - 1])
-        store(3, 0, BANK)
-        add_base(3, BANK, T)
-        store(3, BANK, T)
+                store(3, *LAST_PIECES[n - 1])
+        add_base(3, *LAST_PIECES[-1])
+        store(3, *LAST_PIECES[-1])

@@ -85,6 +85,7 @@ def tile_moe_adb_relu2_kernel(
         dx = [keep.tile([P, S], F32, name="dx%d" % c) for c in range(CHUNKS)]
         part = [keep.tile([P, T], F32, name="part%d" % c) for c in range(2)] * 2
         picked = {c: keep.tile([P, T], F32, name="picked%d" % c) for c in range(1, CHUNKS)}
+        picked2 = keep.tile([P, T], F32, name="picked_by_pos2")
         res = [keep.tile([P, T], F32, name="res%d" % c) for c in range(CHUNKS)]
         banks = [psum.tile([P, BANK], F32, name="bank%d" % n) for n in range(8)]
 
@@ -208,9 +209,9 @@ def tile_moe_adb_relu2_kernel(
                 rhs=dyw[:, t0:t1].bitcast(FP8X4), rhs_scale=dys[:, t0:t1], start=True, stop=True,
             )
 
-        def pick(c, t0, t1):
-            entries = pos1_sb[:, t0 // PER_COL : t1 // PER_COL]
-            nc.scalar.activation(picked[c][:, t0:t1], dx[c][:].indirect(entries), COPY)
+        def pick(c, t0, t1, pos_sb=pos1_sb, dst=None):
+            dst = picked[c] if dst is None else dst
+            nc.scalar.activation(dst[:, t0:t1], dx[c][:].indirect(pos_sb[:, t0 // PER_COL : t1 // PER_COL]), COPY)
 
         def gather_add(dst, c, pos_sb, other, t0, t1):
             entries = pos_sb[:, t0 // PER_COL : t1 // PER_COL]
@@ -332,12 +333,17 @@ def tile_moe_adb_relu2_kernel(
         second(3, 0, 4, banks[6])
         second(3, 4, 8, banks[7])
         finish(2)
-        for t0, t1 in LAST_PIECES:
-            pick(3, t0, t1)
-        for n, (t0, t1) in enumerate(LAST_PIECES):
-            gather_add(part[3], 3, pos2_sb, picked[3], t0, t1)
-            if n > 0:
-                add_base(3, *LAST_PIECES[n - 1])
-                store(3, *LAST_PIECES[n - 1])
-        add_base(3, *LAST_PIECES[-1])
-        store(3, *LAST_PIECES[-1])
+        head, middle, tail = LAST_PIECES
+        pick(3, *head)
+        pick(3, *middle)
+        pick(3, *middle, pos2_sb, picked2)
+        pick(3, *tail)
+        gather_add(part[3], 3, pos2_sb, picked[3], *head)
+        m0, m1 = middle
+        nc.vector.tensor_tensor(part[3][:, m0:m1], picked[3][:, m0:m1], picked2[:, m0:m1], ALU.add)
+        add_base(3, *head)
+        store(3, *head)
+        gather_add(part[3], 3, pos2_sb, picked[3], *tail)
+        for piece in (middle, tail):
+            add_base(3, *piece)
+            store(3, *piece)

from contextlib import ExitStack

import concourse.mybir as mybir
from concourse.masks import make_identity

K, T, E, C, H, N = 512, 640, 5, 256, 512, 512
S = E * C
P = 128
PACK = 4
BANK = 512
PER_COL = 16
SCALE_ROWS = 4
CHUNKS = K // P
GROUPS = S // P
WINDOW = 768
FLOPS = 2 * K * N * T + 2 * S * N * H + 2 * S * H * K

F32 = mybir.dt.float32
BF16 = mybir.dt.bfloat16
I32 = mybir.dt.int32
U32 = mybir.dt.uint32
U16 = mybir.dt.uint16
U8 = mybir.dt.uint8
FP8X4 = mybir.dt.float8_e4m3fn_x4
FP4X4 = mybir.dt.float4_e2m1fn_x4
COPY = mybir.ActivationFunctionType.Copy
RELU = mybir.ActivationFunctionType.Relu
ALU = mybir.AluOpType

GATHER_CUTS = ((0, 3), (3, 6), (6, 10))
A_CUTS = ((0, 2), (2, 5), (5, 7), (7, 10))
WB_CUTS = ((0, 2), (2, 3), (3, 4), (4, 5))
WA_CUTS = ((0, 2, 0, 2), (0, 2, 2, 4), (0, 2, 4, 5), (2, 3, 0, 5), (3, 4, 0, 5))
WAS_CUTS = ((0, 2), (2, 4))
DH_TILES = ((0, 4, 0), (4, 8, 8), (8, 10, 9))
POOL_GROUP = 0
WOVEN_GROUP = GROUPS - 1
AHEAD = 2
WARM_UPS = 2
TOKEN_PIECES = ((0, 384), (384, T))
BANK_PIECES = ((0, BANK), (BANK, T))
LAST_PIECES = ((0, 320), (320, BANK), (BANK, T))


def cut_of(cuts, x):
    return [n for n, cut in enumerate(cuts) if cut[0] <= x < cut[1]][0]


def tile_moe_adb_relu2_kernel(
    tc, dy_words, dy_scales, wt_words, wt_scales, wbt_words, wbt_scales, wat_words, wat_scales, a, gate, offs, pos1, pos2, out
):
    nc = tc.nc
    with ExitStack() as ctx:
        keep = ctx.enter_context(tc.tile_pool(name="keep", bufs=1))
        psum = ctx.enter_context(tc.psum_pool(name="psum", bufs=1))

        offs_sb = keep.tile([P, S // PER_COL], U16, name="offs_sb")
        pos1_sb = keep.tile([P, T // PER_COL], U16, name="pos1_sb")
        pos2_sb = keep.tile([P, T // PER_COL], U16, name="pos2_sb")
        dyw = keep.tile([P, WINDOW], I32, name="dyw", align_bytes=64)
        dys = keep.tile([P, WINDOW], U8, name="dys", align_bytes=64)
        wtw = keep.tile([P, 2 * K], U8, name="wtw", align_bytes=64)
        wts = keep.tile([P, K], U8, name="wts", align_bytes=64)
        wbw = [keep.tile([P, hi - lo, H], I32, name="wbw%d" % lo, align_bytes=64) for lo, hi in WB_CUTS]
        wbs = keep.tile([P, E, H], U8, name="wbs", align_bytes=64)
        waw = [
            keep.tile([P, e1 - e0, (c1 - c0) * P], I32, name="waw%d_%d" % (c0, e0), align_bytes=64)
            for c0, c1, e0, e1 in WA_CUTS
        ]
        was = [keep.tile([P, E, (hi - lo) * P], U8, name="was%d" % lo, align_bytes=64) for lo, hi in WAS_CUTS]
        a_sb = [keep.tile([P, PACK, (hi - lo) * P], F32, name="a%d" % lo, align_bytes=64) for lo, hi in A_CUTS]
        gate_rows = keep.tile([P, P], F32, name="gate_rows")
        gate2 = keep.tile([P, GROUPS], F32, name="gate2")
        ident = keep.tile([P, P], F32, name="ident")
        xw = keep.tile([P, S], U32, name="xw", align_bytes=64)
        xs = keep.tile([P, S], U8, name="xs", align_bytes=64)
        gated = [keep.tile([P, H], F32, name="gated%d" % b, tag="gated%d" % b, align_bytes=64) for b in range(GROUPS)]
        relu_rows = keep.tile([P, H], F32, name="relu_rows")
        relu_woven = keep.tile([P, H], F32, name="relu_woven")
        dh_rows = keep.tile([P, H], BF16, name="dh_rows", align_bytes=64)
        dh = keep.tile([P, S * PACK], BF16, name="dh", align_bytes=64)
        base0 = keep.tile([P, T], F32, name="base0")
        dhw = {}
        dhs = keep.tile([P, S], U8, name="dhs", align_bytes=64)
        dx = [keep.tile([P, S], F32, name="dx%d" % c) for c in range(CHUNKS)]
        part = [keep.tile([P, T], F32, name="part%d" % c) for c in range(2)] * 2
        picked = {c: keep.tile([P, T], F32, name="picked%d" % c) for c in range(1, CHUNKS)}
        picked2 = keep.tile([P, T], F32, name="picked_by_pos2")
        res = [keep.tile([P, T], F32, name="res%d" % c) for c in range(CHUNKS)]
        banks = [psum.tile([P, BANK], F32, name="bank%d" % n) for n in range(8)]

        wb_src = wbt_words.rearrange("e o p n d -> p (e o) (n d)").bitcast(I32)
        wa_src = wat_words.rearrange("e o p n d -> p (e o) (n d)").bitcast(I32)
        a_src = a.rearrange("(p t) s -> p t s", t=PACK)
        wbs_src = wbt_scales.rearrange("e o r n -> r (e o) n")
        was_src = wat_scales.rearrange("e o r n -> r (e o) n")

        def load_scales(tile, rows, queues=(nc.sync,) * SCALE_ROWS):
            rest = (slice(None),) * (len(rows.shape) - 1)
            for r, queue in enumerate(queues):
                queue.dma_start(
                    out=tile[(slice(r, P, 32),) + rest].bitcast(I32),
                    in_=rows[(slice(r, 16, SCALE_ROWS),) + rest].bitcast(I32),
                )

        def load_a(n):
            lo, hi = A_CUTS[n]
            nc.sync.dma_start(out=a_sb[n][:], in_=a_src[:, :, lo * P : hi * P])

        def load_wb(n):
            lo, hi = WB_CUTS[n]
            nc.sync.dma_start(out=wbw[n][:], in_=wb_src[:, lo:hi, :])

        def load_wa(n):
            c0, c1, e0, e1 = WA_CUTS[n]
            nc.sync.dma_start(out=waw[n][:], in_=wa_src[:, e0:e1, c0 * P : c1 * P])

        def load_was(n):
            lo, hi = WAS_CUTS[n]
            load_scales(was[n], was_src[:, :, lo * P : hi * P])

        def first(b):
            e = b * P // C
            n = cut_of(WB_CUTS, e)
            acc = banks[b % 3]
            nc.tensor.matmul_mx(
                out=acc[:], lhsT=xw[:, b * P : (b + 1) * P].bitcast(FP8X4), lhsT_scale=xs[:, b * P : (b + 1) * P],
                rhs=wbw[n][:, e - WB_CUTS[n][0], :].bitcast(FP8X4), rhs_scale=wbs[:, e, :], start=True, stop=True,
            )
            if b == POOL_GROUP:
                dst = gated[b][:].rearrange("s (u m d) -> s u m d", u=2, d=2)
                src = acc[:].rearrange("s (m u d) -> s u m d", u=2, d=2)
            else:
                dst = gated[b][:].rearrange("s (t m) -> s t m", t=PACK)
                src = acc[:].rearrange("s (m t) -> s t m", t=PACK)
            nc.scalar.activation(dst, src, COPY, scale=gate2[:, b : b + 1])

        def a_group(b):
            n = cut_of(A_CUTS, b)
            s0 = (b - A_CUTS[n][0]) * P
            return a_sb[n][:, :, s0 : s0 + P]

        def dh_group(b):
            return dh[:, b * H : (b + 1) * H]

        def pool_product(turned):
            for t in range(PACK):
                nc.tensor.transpose(turned[:, t * P : (t + 1) * P], a_group(POOL_GROUP)[:, t, :], ident[:])
            nc.scalar.activation(
                relu_rows[:].rearrange("s (u m d) -> s u m d", u=2, d=2),
                turned[:].rearrange("s (u d m) -> s u m d", u=2, d=2), RELU,
            )
            nc.gpsimd.tensor_tensor(dh_rows[:], gated[POOL_GROUP][:], relu_rows[:], ALU.mult)

        def pool_words_back(turned):
            pairs = dh_rows[:].bitcast(F32)
            for u in range(2):
                nc.tensor.transpose(turned[:, u * P : (u + 1) * P], pairs[:, u * P : (u + 1) * P], ident[:])
            nc.scalar.copy(
                dh_group(POOL_GROUP).bitcast(F32).rearrange("p (s u) -> p s u", u=2),
                turned[:, 0 : 2 * P].rearrange("p (u s) -> p s u", u=2),
            )

        def turn(b, turned):
            for t in range(PACK):
                nc.tensor.transpose(turned[:, t * P : (t + 1) * P], gated[b][:, t * P : (t + 1) * P], ident[:])

        def product(b, turned):
            dst = dh_group(b).rearrange("p (s t) -> p s t", t=PACK)
            sums = turned[:].rearrange("p (t s) -> p s t", t=PACK)
            if b == WOVEN_GROUP:
                nc.vector.tensor_tensor(dst, relu_woven[:].rearrange("p (s t) -> p s t", t=PACK), sums, ALU.mult)
            else:
                nc.vector.scalar_tensor_tensor(
                    out=dst, in0=a_group(b).rearrange("p t s -> p s t"), scalar=0.0, in1=sums, op0=ALU.max, op1=ALU.mult
                )

        def dh_words(s0, s1):
            lo = DH_TILES[cut_of(DH_TILES, s0 // P)][0]
            return dhw[lo][:, s0 - lo * P : s1 - lo * P]

        def quantize(lo, hi):
            g0, g1, holder = DH_TILES[cut_of(DH_TILES, lo)]
            if lo == g0:
                dhw[g0] = keep.tile([P, (g1 - g0) * P], U32, name="dhw%d" % g0, tag="gated%d" % holder, align_bytes=64)
            nc.vector.quantize_mx(
                out=dh_words(lo * P, hi * P).bitcast(FP8X4), scales=dhs[:, lo * P : hi * P], in_=dh[:, lo * H : hi * H]
            )

        def second(c, lo, hi, acc, copy=nc.scalar.copy):
            edges = [lo * P] + [x for x in range(0, S, C) if lo * P < x < hi * P] + [hi * P]
            m = cut_of(WAS_CUTS, c)
            sc = c - WAS_CUTS[m][0]
            for s0, s1 in zip(edges[:-1], edges[1:]):
                e = s0 // C
                n = [i for i, (c0, c1, e0, e1) in enumerate(WA_CUTS) if c0 <= c < c1 and e0 <= e < e1][0]
                wc, we = c - WA_CUTS[n][0], e - WA_CUTS[n][2]
                nc.tensor.matmul_mx(
                    out=acc[:, s0 - lo * P : s1 - lo * P],
                    lhsT=waw[n][:, we, wc * P : (wc + 1) * P].bitcast(FP8X4),
                    lhsT_scale=was[m][:, e, sc * P : (sc + 1) * P],
                    rhs=dh_words(s0, s1).bitcast(FP8X4), rhs_scale=dhs[:, s0:s1], start=True, stop=True,
                )
            copy(dx[c][:, lo * P : hi * P], acc[:, 0 : (hi - lo) * P])

        def base_pass(c, t0, t1, dst):
            nc.tensor.matmul_mx(
                out=dst, lhsT=wtw[:, 2 * c * P : 2 * (c + 1) * P].bitcast(FP4X4), lhsT_scale=wts[:, c * P : (c + 1) * P],
                rhs=dyw[:, t0:t1].bitcast(FP8X4), rhs_scale=dys[:, t0:t1], start=True, stop=True,
            )

        def pick(c, t0, t1, pos_sb=pos1_sb, dst=None):
            dst = picked[c] if dst is None else dst
            nc.scalar.activation(dst[:, t0:t1], dx[c][:].indirect(pos_sb[:, t0 // PER_COL : t1 // PER_COL]), COPY)

        def gather_add(dst, c, pos_sb, other, t0, t1):
            entries = pos_sb[:, t0 // PER_COL : t1 // PER_COL]
            nc.vector.tensor_tensor(dst[:, t0:t1], dx[c][:].indirect(entries), other[:, t0:t1], ALU.add)

        def store(c, t0, t1):
            nc.sync.dma_start(out=out[c * P : (c + 1) * P, t0:t1], in_=res[c][:, t0:t1])

        nc.gpsimd.memset(dys[:].bitcast(I32), 0)
        nc.vector.memset(dyw[:, T:WINDOW], 0)
        nc.vector.memset(gate_rows[:].bitcast(I32), 0)
        nc.vector.memset(wbs[:].rearrange("p e n -> p (e n)").bitcast(I32), 0)
        for tile in was:
            nc.vector.memset(tile[:].rearrange("p e n -> p (e n)").bitcast(I32), 0)
        nc.vector.memset(wts[:].bitcast(I32), 0)
        make_identity(nc, ident[:])

        nc.sync.dma_start(out=dyw[:, 0:T], in_=dy_words[0].rearrange("p t d -> p (t d)").bitcast(I32))
        load_scales(dys[:, 0:T], dy_scales[0], (nc.scalar, nc.scalar, nc.sync, nc.sync))
        nc.sync.dma_start(offs_sb[:], offs)
        load_wb(0)
        nc.sync.dma_start(out=gate_rows[0:GROUPS, :], in_=gate[0].rearrange("(b p) -> b p", p=P))
        load_scales(wbs, wbs_src)
        load_a(0)
        load_wb(1)
        load_wb(2)
        load_a(1)
        load_wb(3)
        load_a(2)
        load_scales(wts, wt_scales[0])
        load_a(3)
        nc.sync.dma_start(out=wtw[:].bitcast(I32), in_=wt_words[0].bitcast(I32))
        load_was(0)
        for n in range(3):
            load_wa(n)
        nc.sync.dma_start(pos1_sb[:], pos1)
        nc.sync.dma_start(pos2_sb[:], pos2)
        load_wa(3)
        load_was(1)
        load_wa(4)

        nc.tensor.transpose(banks[7][:, 0:P], gate_rows[:], ident[:])
        nc.scalar.activation(gate2[:], banks[7][:, 0:GROUPS], COPY, scale=2.0)
        for n in range(WARM_UPS):
            nc.tensor.matmul_mx(
                out=banks[3][:], lhsT=dyw[:, 0:P].bitcast(FP8X4), lhsT_scale=dys[:, 0:P],
                rhs=dyw[:, 0:BANK].bitcast(FP8X4), rhs_scale=dys[:, 0:BANK], start=True, stop=True,
            )
        for lo, hi in GATHER_CUTS:
            entries = offs_sb[:, lo * P // PER_COL : hi * P // PER_COL]
            nc.vector.tensor_copy(xw[:, lo * P : hi * P], dyw[:].bitcast(U32).indirect(entries))
            nc.vector.tensor_copy(xs[:, lo * P : hi * P], dys[:].indirect(entries))

        for b in range(AHEAD + 1):
            first(b)
        for b in range(1, GROUPS - 1):
            if b + AHEAD < GROUPS:
                first(b + AHEAD)
            else:
                woven = relu_woven[:].rearrange("p (s t) -> p s t", t=PACK)
                nc.scalar.activation(woven, a_group(WOVEN_GROUP).rearrange("p t s -> p s t"), RELU)
            turn(b, banks[3 + (b - 1) % 4])
            product(b, banks[3 + (b - 1) % 4])
            if b + 1 == A_CUTS[0][1]:
                pool_product(banks[7])
            if b + 1 == A_CUTS[1][1]:
                pool_words_back(banks[7])
            if b == A_CUTS[1][1]:
                quantize(0, 4)

        last = GROUPS - 1
        base_pass(0, 0, BANK, banks[2][:])
        nc.scalar.copy(base0[:, 0:BANK], banks[2][:])
        turn(last, banks[7])
        quantize(4, 8)
        product(last, banks[7])
        tails = banks[5]
        for c in range(CHUNKS):
            base_pass(c, BANK, T, tails[:, c * P : (c + 1) * P])
        nc.scalar.copy(base0[:, BANK:T], tails[:, 0:P])
        base_bank = {1: banks[1], 2: banks[4], 3: banks[3]}
        base_pass(1, 0, BANK, base_bank[1][:])
        second(0, 0, 4, banks[0])
        second(1, 0, 4, banks[6])
        second(1, 4, 8, banks[2])
        quantize(8, 9)
        quantize(9, 10)
        second(0, 4, 8, banks[7], nc.vector.tensor_copy)
        second(0, 8, 9, banks[4])
        second(0, 9, 10, banks[3], nc.vector.tensor_copy)
        second(1, 8, 10, banks[0])

        for t0, t1 in TOKEN_PIECES:
            gather_add(part[0], 0, pos1_sb, base0, t0, t1)
        for t0, t1 in TOKEN_PIECES:
            gather_add(res[0], 0, pos2_sb, part[0], t0, t1)
        store(0, 0, T)

        def add_base(c, t0, t1):
            src = base_bank[c][:, t0:t1] if t1 <= BANK else tails[:, c * P : (c + 1) * P]
            nc.vector.tensor_tensor(res[c][:, t0:t1], part[c][:, t0:t1], src, ALU.add)

        def finish(c):
            for t0, t1 in BANK_PIECES:
                gather_add(part[c], c, pos2_sb, picked[c], t0, t1)
            for t0, t1 in BANK_PIECES:
                add_base(c, t0, t1)
            store(c, 0, T)

        pick(1, 0, T)
        second(2, 8, 10, banks[4])
        second(2, 0, 4, banks[3])
        second(2, 4, 8, banks[0])
        for c in (2, 3):
            base_pass(c, 0, BANK, base_bank[c][:])
        finish(1)
        pick(2, 0, T)
        second(3, 8, 10, banks[2])
        second(3, 0, 4, banks[6])
        second(3, 4, 8, banks[7])
        finish(2)
        head, middle, tail = LAST_PIECES
        pick(3, *head)
        pick(3, *middle)
        pick(3, *middle, pos2_sb, picked2)
        pick(3, *tail)
        gather_add(part[3], 3, pos2_sb, picked[3], *head)
        m0, m1 = middle
        nc.vector.tensor_tensor(part[3][:, m0:m1], picked[3][:, m0:m1], picked2[:, m0:m1], ALU.add)
        add_base(3, *head)
        store(3, *head)
        gather_add(part[3], 3, pos2_sb, picked[3], *tail)
        for piece in (middle, tail):
            add_base(3, *piece)
            store(3, *piece)
